import numpy as np, ml_dtypes
CORES = [6,15,38,47]
N = 4
BF = ml_dtypes.bfloat16
M, P, T, H, C, HM = 2048, 256, 5, 2, 64, 2048
E = M + T * P
def crowd(rng, cen, s, n):
    pick = (rng.random((N, 8, 1, n)) * s).astype(np.int64)
    return np.clip(np.take_along_axis(cen, pick, 3) + rng.integers(-1, 2, (N, 8, 16, n)), 0, 15)
def rows(rng):
    v = np.arange(M); i = np.arange(16)[:, None]
    a = np.where(i < rng.integers(2, 17, (N, 8, 1, M)), rng.integers(0, M, (N, 8, 16, M)), E)
    a[:, :, 1] = np.where(v < M - P, v + P, E)
    own = v - P * (1 + (rng.random((N, 8, M)) * (v // P)).astype(np.int64)); low = (rng.random((N, 8, M)) * v).astype(np.int64)
    k = np.where(rng.random((N, 8, M)) < 0.6, own, low)
    a[:, :, 0] = np.where((v < P) | (rng.random((N, 8, M)) < 0.04), E, k)
    return a
def base(rng):
    s = rng.choice(np.array([4, 8, 12, 16, 32]), (N, 8, 1, 1)); cen = np.repeat(rng.integers(0, 16, (1, 8, 16, 32)), N, 0)
    return crowd(rng, cen, s, M), rows(rng), crowd(rng, cen, s, T * P), rng.integers(0, 256, (N, 8, 16, 1)), rng.integers(10, 30, (N, 8, 16, 1))
def pack(f, a, x, w, t):
    return {"fr": np.ascontiguousarray(f.reshape(N, 128, M)).astype(np.float32).astype(BF), "ptr": np.ascontiguousarray(a.reshape(N, 128, M)).astype(np.int32),
            "nw": np.ascontiguousarray(x.reshape(N, 128, T * P)).astype(np.float32).astype(BF),
            "hw": np.ascontiguousarray(w.reshape(N, 128, 1)).astype(np.int32), "th": np.ascontiguousarray(t.reshape(N, 128, 1)).astype(np.int32)}
def setup_inputs(rng):
    return pack(*base(rng))
def setup_inputs_room(rng):
    f, a, x, w, t = base(rng); f = np.minimum(f, 10)
    for q in range(N):
        for g in range(8):
            n = int(rng.choice(np.array([0, 1, C - 1, C, C + 1, P])))
            if q == 0: n = (C, C + 1, P, C - 1, 1, 0, C, C + 1)[g]
            o = rng.permutation(P); esc, rest = o[:n], o[n:]
            k = rng.integers(0, M - P, P - n); a[q, g, 0, M - P + rest] = k; x[q, g][:, rest] = f[q, g][:, k + P]
            a[q, g, 0, M - P + esc] = E
            far = esc[:n // 2]; k = P * rng.integers(1, M // P - 1, len(far)) + far
            a[q, g, 0, M - P + far] = k; a[q, g, 0, k] = k - P; a[q, g, 0, k - P] = E
            x[q, g][:, far] = 15 - rng.integers(0, 2, (16, len(far)))
    return pack(f, a, x, w, t)
def jog(rng, n):
    return (np.arange(16)[:, None] == rng.integers(0, 16, (N, 8, 1, n))) * rng.choice(np.array([-4, 4]), (N, 8, 1, n))
def setup_inputs_ties(rng):
    f, a, x, w, t = base(rng); cen = np.repeat(rng.integers(4, 12, (1, 8, 16, 1)), N, 0)
    f = cen + jog(rng, M); x = cen + jog(rng, T * P) * ((np.arange(T * P) // P) & 1)
    t = rng.integers(3, 6, (N, 8, 16, 1)); t[:, 1::2] = 3
    return pack(f, a, x, w, t)
def setup_inputs_loops(rng):
    f, a, x, w, t = base(rng); v = np.arange(M)
    a[:, :, 2:] = np.where(rng.random((N, 8, 14, M)) < 0.5, rng.integers(0, M, (N, 8, 14, M)), E)
    mate = np.where((((v // P) & 1) == 0) & (v + P < M), v + P, v - P)
    a[:, ::2, 0] = np.where(rng.random((N, 4, M)) < 0.4, v, np.where(rng.random((N, 4, M)) < 0.6, mate, a[:, ::2, 0]))
    a[:, 1, 0] = rng.choice(np.array([0, M - 1, M // 2, E]), (N, M))
    a[:, 3, 2:] = rng.integers(0, M, (N, 14, M)); a[:, 5, 2:] = E; a[:, 7, 2:] = rng.integers(0, M, (N, 1, M))
    return pack(f, a, x, w, t)
def setup_inputs_calm(rng):
    f, a, x, w, t = base(rng); q = [int(c) for c in rng.permutation(8)]
    t[:, q[0]] = 240; a[:, q[0], 0] = np.where(a[:, q[0], 0] == E, rng.integers(0, M, (N, M)), a[:, q[0], 0])
    a[:, q[1], 0] = E
    t[:, q[2]] = 0; f[:, q[2]] = 15 * rng.integers(0, 2, (N, 1, M)); x[:, q[2]] = 15 * rng.integers(0, 2, (N, 1, T * P))
    t[1::2, q[2], 2::2] = 239; t[1::2, q[2], 3::2] = 240
    w[:, q[3]] = 0; w[:, q[4]] = 255
    t[:, q[5]] = 240; t[:, q[5], 1] = 0
    f[:, q[6]] = rng.integers(0, 2, (N, 16, M)); x[:, q[6]] = np.where(((np.arange(T * P) // P) & 1) == 1, 0, 14) + rng.integers(0, 2, (N, 16, T * P))
    a[:, q[6], 0] = np.where(a[:, q[6], 0] < M - P, a[:, q[6], 0], rng.integers(0, M - P, (N, M)))
    w[:, q[6]] = rng.integers(225, 256, (N, 16, 1)); t[:, q[6]] = rng.integers(128, 208, (N, 16, 1))
    f[:, q[7]] = np.abs(15 * rng.integers(0, 2, (N, 1, M)) - rng.integers(0, 2, (N, 16, M)))
    x[:, q[7]] = np.abs(15 * rng.integers(0, 2, (N, 1, T * P)) - rng.integers(0, 2, (N, 16, T * P)))
    a[:, q[7], 0] = np.where(a[:, q[7], 0] == E, rng.integers(0, M, (N, M)), a[:, q[7], 0])
    w[:, q[7]] = rng.integers(128, 256, (N, 16, 1)); t[:, q[7]] = rng.integers(0, 241, (N, 16, 1))
    return pack(f, a, x, w, t)
def setup_inputs_spread(rng):
    f, a, x, w, t = base(rng); e = np.array([0.25, 0.5, 1.0, 1.0, 2.0, 4.0])
    f = np.minimum((16 * rng.random((N, 8, 16, M)) ** rng.choice(e, (N, 8, 1, M))).astype(np.int64), 15)
    x = np.minimum((16 * rng.random((N, 8, 16, T * P)) ** rng.choice(e, (N, 8, 1, T * P))).astype(np.int64), 15)
    a = np.where(rng.random((N, 8, 16, M)) < rng.random((N, 8, 1, M)), rng.integers(0, M, (N, 8, 16, M)), E)
    a[:, :, 0] = np.where(rng.random((N, 8, M)) < 0.1, E, rng.integers(0, M, (N, 8, M)))
    a[:, :, 1, :M - P] = rng.integers(0, M, (N, 8, M - P))
    t = rng.choice(np.array([0, 20, 40, 50, 60, 60, 70, 240]), (N, 8, 16, 1)); t = np.where(rng.random((N, 8, 1, 1)) < 0.5, np.minimum(t, 60), t)
    return pack(f, a, x, w, t)
def check_inputs(d):
    bad = []
    for k in ("fr", "nw"):
        z = d[k].astype(np.float32)
        if not np.all((z >= 0) & (z <= 15) & (z == np.floor(z))): bad.append("whole numbers from 0 to 15 in " + k)
    for k, hi in (("hw", 255), ("th", 240)):
        if np.min(d[k]) < 0 or np.max(d[k]) > hi: bad.append("range of " + k)
    a = d["ptr"]; full = (a >= 0) & (a < M)
    if not np.all(full | (a == E)): bad.append("range of ptr")
    if not np.all(full[:, 1::16, :M - P]): bad.append("row 1 of an old state before the last P is empty")
    return bad
def gaps(F, c, x):
    out = np.empty(c.shape, np.int64)
    for a in range(N):
        for g in range(8): out[a, g] = np.add.reduce(np.abs(F[a, g][:, c[a, g]] - x[a, g][:, None, :]), axis=0)
    return out
def reference(fr, ptr, nw, hw, th):
    F = np.full((N, 8, 16, E + 1), 99, np.int32); F[..., :M] = fr.astype(np.float32).astype(np.int32).reshape(N, 8, 16, M)
    A = np.full((N, 8, 16, E + 1), E, np.int64); A[..., :M] = ptr.reshape(N, 8, 16, M)
    X = nw.astype(np.float32).astype(np.int32).reshape(N, 8, 16, T, P)
    w = hw.astype(np.int64).reshape(N, 8, 16, 1); lim = th.astype(np.int64).reshape(N, 8, 16, 1); piece = np.arange(P)
    for t in range(T):
        n0 = M + P * t; n = n0 + piece; x = X[:, :, :, t]
        F[..., n0:n0 + P] = x; A[:, :, 1, n0 - P:n0] = n
        k = np.array(A[:, :, 0, n0 - P:n0]); link = np.full((N, 8, P), E, np.int64); going = np.ones((N, 8, P), bool)
        for h in range(H):
            c = np.take_along_axis(A, k[:, :, None, :], 3)
            ok = (gaps(F, c, x) <= lim) & (c < E); ok[:, :, 0] = False
            hit = np.any(ok, axis=2); to = np.take_along_axis(c, np.argmax(ok, axis=2)[:, :, None, :], 2)[:, :, 0]
            link = np.where(going & hit, to, link); going = going & ~hit
            free = c == E; free[:, :, 0] = False
            wr = going & (k < E) & ((k & (P - 1)) == piece) & np.any(free, axis=2)
            a, g, p = np.nonzero(wr); A[a, g, np.argmax(free, axis=2)[wr], k[wr]] = n[p]
            k = np.where(going, c[:, :, 0], k)
        A[:, :, 0, n0:n0 + P] = np.where(going, k, link)
        if t < T - 1:
            for a in range(N):
                b = (a + 1 + t % (N - 1)) % N
                for g in range(8):
                    ps = np.nonzero(going[a, g])[0][:C]; z = x[a, g][:, ps].astype(np.int64)
                    q = np.add.reduce(w[b, g] * z, axis=0) & (HM - 1)
                    c = A[b, g][1:, q]
                    best = np.argmin(np.add.reduce(np.abs(F[b, g][:, c] - z[:, None, :]), axis=0), axis=0)
                    f = F[b, g][:, c[best, np.arange(len(ps))]]
                    X[a, g][:, t + 1, ps] = (X[a, g][:, t + 1, ps] + f) >> 1
    return {"yp": np.ascontiguousarray(A[..., :E]).reshape(N, 128, E).astype(np.float32), "yx": X.reshape(N, 128, T * P).astype(np.float32).astype(BF)}

@@ -1,0 +1,649 @@
+import numpy as np
+from concourse.mybir import dt, AluOpType, AxisListType, ActivationFunctionType
+
+M, P, NT, C = 2048, 256, 5, 64
+E = M + NT * P
+CEN = 1792
+AD = 3336
+FD = 3344
+B = 4096.0
+BETA = 1920.0
+NS = 4
+G1, GV = 64, 224
+f32, bf, f16, i32, u16 = "float32", "bfloat16", "float16", "int32", "uint16"
+
+SB = {
+    "A": ([AD + 512], f32), "F": ([FD + 832], bf), "pin": ([M], i32), "thw": ([8], i32),
+    "a0": ([4096], bf), "a1": ([4096], bf), "m0": ([4096], bf), "m1": ([4096], bf),
+    "af": ([256], bf), "c32": ([512], f32), "cs32": ([256], f32), "cu": ([512], u16), "c16": ([512], f16),
+    "ee": ([512], bf), "e12": ([256], bf), "hi": ([256], bf), "w": ([256], bf), "pen": ([256], bf), "s": ([512], bf),
+    "n1": ([256], bf), "go": ([256], bf), "sel": ([512], f16), "tw": ([512], f32), "cum": ([256], bf),
+    "jk": ([1024], bf), "acc": ([8], f32), "psu": ([8], u16), "psf": ([8], f32),
+    "pst": ([8], f32), "apu": ([8], u16), "sc": ([256], f32), "kk": ([48], i32), "ku": ([48], u16), "pm": ([32], i32),
+    "pu": ([16], u16), "own": ([32], f32), "so": ([32], f32), "sou": ([32], u16), "dmj": ([8], f32), "ne": ([16], f32),
+    "xs": ([256], bf), "lx": ([256], bf), "fh": ([256], bf), "lf": ([256], bf), "pre": ([64], f32), "vv": ([64], bf),
+    "q32": ([8], i32), "q33": ([8], i32), "qu": ([8], u16), "cq": ([64], u16), "sa": ([1024], bf), "sm": ([1024], bf),
+    "sq": ([64], f32), "pi": ([8], i32), "col": ([32], f32), "U": ([144], bf), "t0": ([144], bf), "t1": ([128], bf),
+    "t2": ([128], bf), "t3": ([128], bf), "t4": ([128], bf), "inb": ([128], bf), "eq": ([128], bf), "gt": ([128], bf),
+    "z0": ([128], bf), "bb": ([144], bf), "b0": ([128], bf), "u1": ([128], bf),
+    "big": ([4, 144], bf), "bigh": ([2, 144], f16), "mb": ([26, 128], bf), "mh": ([4, 128], f16),
+    "iop": ([256], f32), "iob": ([256], bf), "one": ([256], bf), "dg": ([256], f32), "dh": ([64], f32), "rs": ([64], f32),
+    "kc": ([64], f16), "neg": ([64], bf), "ioo": ([32], f32), "dum": ([32], f32), "dj": ([4], f32), "thr": ([8], f32),
+    "c0": ([256], f16), "t256": ([256], f32), "prm": ([8], u16), "prf": ([8], f32),
+}
+SCRATCH = {k: ("sbuf", [128] + v[0], v[1]) for k, v in SB.items()}
+for _b in range(8):
+    SCRATCH["p%d" % _b] = ("psum", [128, 512], f32)
+SEMAPHORES = (["v", "s", "pe", "gc", "ld0", "ld1", "ld2", "ld3", "ld4", "ld5", "ld6", "st0", "st1", "st2", "sent"]
+              + ["req%d" % t for t in range(4)] + ["rep%d" % t for t in range(4)])
+
+
+def priority_weights():
+    y1 = np.zeros((16, 16))
+    y2 = np.zeros((16, 16))
+    for i in range(16):
+        y1[i, i] = 2048.0
+        y2[i, i] = 2048.0
+        for j in range(1, i):
+            y1[j, i] = -BETA
+            y2[j, i] = -BETA
+        if i >= 1:
+            y1[0, i] = BETA * (i - 1)
+            y2[0, i] = BETA * (i + 1)
+    y2[0, 0] = 2 * BETA - 2048.0 + 15 * BETA
+    y2[1:, 0] = -BETA
+    return y1, y2
+
+
+def rank_program(g, core, T, topo):
+    rank = T.rank_of(core)
+    if rank is None:
+        return
+    N = len(T.cores)
+    AL, AF = AluOpType, ActivationFunctionType
+    Q = {"v": g.vector, "s": g.scalar, "pe": g.tensor, "gc": g, "sy": g.sync}
+    cnt = {"v": 0, "s": 0, "pe": 0, "gc": 0}
+    seen = {q: {} for q in Q}
+    lastw, readers = {}, {}
+    sent = [0]
+
+    def need(q, ev):
+        sem, val = ev
+        if seen[q].get(sem, 0) < val:
+            Q[q].wait_ge(T.sem[sem], val)
+            seen[q][sem] = val
+
+    def deps(q, rd, wr):
+        best = {}
+        evs = [lastw[r] for r in list(rd) + list(wr) if r in lastw and not (r[0] == "#" and lastw[r][0] == q)]
+        for r in wr:
+            evs += readers.get(r, [])
+        for sem, val in evs:
+            best[sem] = max(best.get(sem, 0), val)
+        for sem in best:
+            need(q, (sem, best[sem]))
+
+    def mark(ev, rd, wr):
+        for r in rd:
+            readers.setdefault(r, []).append(ev)
+        for r in wr:
+            lastw[r] = ev
+            readers[r] = []
+
+    def op(q, fn, rd, wr):
+        wr = list(wr) + [r for r in rd if r[0] == "#"]
+        rd = [r for r in rd if r[0] != "#"]
+        deps(q, rd, wr)
+        cnt[q] += 1
+        fn().then_inc(T.sem[q], 1)
+        mark((q, cnt[q]), rd, wr)
+
+    def mms(bank, items, rd, start=True, stop=True, each=False):
+        wr = ["#%d" % bank]
+        deps("pe", rd, wr)
+        for k, (o, l, r) in enumerate(items):
+            ins = g.tensor.matmul(o, l, r, each or (start and k == 0), each or (stop and k == len(items) - 1))
+        cnt["pe"] += 1
+        ins.then_inc(T.sem.pe, 1)
+        mark(("pe", cnt["pe"]), rd, wr)
+
+    def dma(q, sem, out, in_, rd, wr):
+        deps(q, rd, wr)
+        Q[q].dma_start(out, in_).then_inc(T.sem[sem], 16)
+        mark((sem, 16), rd, wr)
+
+    def send(dst_rank, out, in_, sem, rd):
+        dst = T.cores[dst_rank]
+        rid, pid = topo.addr(dst)[:2]
+        deps("gc", rd, [])
+        g.remote_dma(out, in_, T.sem[sem], T.sem.sent, pid, rid, topo.mask(core, dst))
+        sent[0] += len(topo.engines(core, dst))
+
+    def arrives(src_rank, sem, name):
+        lastw[name] = (sem, len(topo.engines(T.cores[src_rank], core)))
+
+    V, S = g.vector, g.scalar
+
+    def ts(out, in0, s1, s2, o0, o1, rd, wr):
+        if o1 is None:
+            op("v", lambda: V.tensor_scalar(out, in0, s1, None, o0), rd, wr)
+        else:
+            op("v", lambda: V.tensor_scalar(out, in0, s1, s2, o0, o1), rd, wr)
+
+    def tt(out, a, b, o, rd, wr):
+        op("v", lambda: V.tensor_tensor(out, a, b, o), rd, wr)
+
+    def cp(out, a, rd, wr):
+        op("v", lambda: V.tensor_copy(out, a), rd, wr)
+
+    def ms(out, val, wr):
+        op("v", lambda: V.memset(out, val), [], wr)
+
+    def scan(out, d0, d1, o0, o1, rd, wr):
+        op("v", lambda: V.tensor_tensor_scan(out, d0, d1, 0.0, o0, o1), rd, wr)
+
+    def act(out, a, f, rd, wr, **kw):
+        op("s", lambda: S.activation(out, a, f, **kw), rd, wr)
+
+    def iota(out, pat, cm, wr, flag=True, base=0):
+        if flag:
+            op("gc", lambda: g.iota(out, pat, base, cm, allow_small_or_imprecise_dtypes=True), [], wr)
+        else:
+            op("gc", lambda: g.iota(out, pat, base, cm), [], wr)
+
+    def aff(q, out, a, scale, bias, rd, wr):
+        if q == "v":
+            ts(out, a, scale, bias, AL.mult, AL.add, rd, wr)
+        else:
+            act(out, a, AF.Identity, rd, wr, scale=scale, bias=bias)
+
+    PS = [T["p%d" % b] for b in range(8)]
+    A, F = T.A, T.F
+    Aw, Ar, Fw = A[:, 0:AD + 512], A[:, 0:E + 8], F[:, 0:FD + 64]
+    U = T.U[:, 0:128]
+
+    dma("sy", "ld0", T.pin[:, 1792:M], T.ptr[:, 1792:M], [], ["pinT"])
+    dma("sy", "ld5", T.thw[:, 0:1], T.th[:], [], ["th"])
+    dma("sy", "ld1", T.pin[:, 0:896], T.ptr[:, 0:896], [], ["pin0"])
+    dma("sy", "ld2", T.pin[:, 896:1792], T.ptr[:, 896:1792], [], ["pin1"])
+    dma("sy", "ld3", F[:, 0:M], T.fr[:], [], ["F0"])
+    dma("sy", "ld4", F[:, M:E], T.nw[:], [], ["F1"])
+    dma("sy", "ld6", T.thw[:, 4:5], T.hw[:], [], ["hw"])
+
+    col = T.col
+    cG, cR, cR0, cR1, cN1, cTH, cKD, cMX, cW, cX, cY, cZ, cM = [col[:, j:j + 1] for j in range(13)]
+    cAB = [col[:, 16 + t:17 + t] for t in range(NT)]
+    cC1, cC2, cZ2, cZ3, cB0, cY2, cT2, cN15 = [col[:, j:j + 1] for j in range(24, 32)]
+    iota(T.pi[:, 0:1], [[0, 1]], 1, ["pi0"], False)
+    iota(T.t0[:], [[1, 144]], 0, ["t0"])
+    iota(T.t1[:], [[16, 8], [0, 16]], 0, ["t1"])
+    iota(T.iop[:], [[1, 256]], 0, ["iop"])
+    iota(A[:, M:E + 8], [[0, E + 8 - M]], 0, ["A2"], base=E)
+    iota(T.ioo[:], [[0, 2], [16, 16]], 0, ["ioo"])
+    iota(T.one[:], [[0, 256]], 0, ["Kf"], base=1)
+    iota(T.t256[:], [[0, 16], [1, 16]], 0, ["t256"])
+    iota(T.dj[:], [[16, 4]], 0, ["dj"])
+    iota(T.sq[:], [[1, 64]], 0, ["sq"])
+    iota(T.prf[:, 0:4], [[4, 4]], 0, ["prf"])
+    iota(T.neg[:], [[0, 64]], 0, ["j7"], base=-192)
+    ms(F[:, E:FD + 64], 99.0, ["F2"])
+    ts(T.pi[:, 1:2], T.pi[:, 0:1], 112, None, AL.bitwise_and, None, ["pi0"], ["pi1"])
+    ts(T.pi[:, 2:3], T.pi[:, 0:1], 15, None, AL.bitwise_and, None, ["pi0"], ["pi2"])
+    cp(col[:, 0:2], T.pi[:, 1:3], ["pi1", "pi2"], ["cG"])
+    ts(cR0, cR, 0.0, None, AL.is_equal, None, ["cG"], ["cR0"])
+    ts(T.U[:], T.t0[:], cG, None, AL.subtract, None, ["t0", "cG"], ["U"])
+    ts(cR1, cR, 1.0, None, AL.is_equal, None, ["cG"], ["cR1"])
+    ts(T.inb[:], T.t1[:], cG, None, AL.is_equal, None, ["t1", "cG"], ["inb"])
+    ts(T.bb[:], T.U[:], 15.0, None, AL.is_equal, None, ["U"], ["bb"])
+    ts(T.eq[:], U, cR, None, AL.is_equal, None, ["U", "cG"], ["eq"])
+    ts(T.bigh[:, 0, :], T.bb[:], cR0, None, AL.mult, None, ["bb", "cR0"], ["bigh0"])
+    ts(T.t2[:], U, 1.0, None, AL.add, None, ["U"], ["t2"])
+    ts(T.b0[:], T.inb[:], cR0, None, AL.mult, None, ["inb", "cR0"], ["b0"])
+    tt(T.u1[:], T.t2[:], T.inb[:], AL.mult, ["t2", "inb"], ["u1"])
+    ts(cN1, cR, 1.0, None, AL.not_equal, None, ["cG"], ["cN1"])
+    ts(T.bigh[:, 1, :], T.bb[:], cR1, None, AL.mult, None, ["bb", "cR1"], ["bigh1"])
+    ts(cZ, cR, 1.0, None, AL.add, None, ["cG"], ["cZ"])
+    ts(T.cs32[:], T.iop[:], float(M), cR1, AL.add, AL.mult, ["iop", "cR1"], ["cs32"])
+    ts(T.gt[:], T.u1[:], cZ, None, AL.is_gt, None, ["u1", "cZ"], ["gt"])
+    ts(T.z0[:], T.u1[:], 1.0, None, AL.is_equal, None, ["u1"], ["z0"])
+
+    def SEL(r, m):
+        return T.bigh[:, r, 15 - m:143 - m]
+
+    def RED(k, i):
+        return T.big[:, k, 15 - i:143 - i]
+
+    names = {"I": -1}
+
+    def mat(name):
+        names[name] = len(names)
+        return T.mb[:, names[name], :]
+
+    def MB(name):
+        return T.eq[:] if name == "I" else T.mb[:, names[name], :]
+
+    y1w, y2w = priority_weights()
+    cor1, cor2 = y1w.sum(1), y2w.sum(1)
+    LINKC = float(2048.0 + cor1[0] + cor2[0] + CEN)
+    done = {"K": ["eq", "Kf"], "K2": [], "K3": ["j7"]}
+
+    def key(s, name):
+        done[s].append(s + name)
+        return [s + name]
+
+    def scaled(q, s, todo):
+        for nm, base, bn, wgt, rd in todo:
+            aff(q, mat(nm), base, wgt, 0.0, [bn] + rd, key(s, nm))
+
+    def first_k():
+        ts(T.c0[:], T.pin[:, 1792:M], float(-CEN), None, AL.add, None, ["pinT"], ["c0"])
+        mms(6, [(PS[6][:, 0:16], SEL(0, m), T.c0[:, m::16]) for m in range(16)], ["bigh0", "c0"])
+        ts(T.sc[:], T.pin[:, 1792:M], cN1, None, AL.mult, None, ["pinT", "cN1"], ["sc"])
+        tt(T.t3[:], T.eq[:], T.gt[:], AL.subtract, ["eq", "gt"], ["t3"])
+        tt(A[:, 1792:M], T.sc[:], T.cs32[:], AL.add, ["sc", "cs32"], ["A1"])
+        ts(T.ku[:, 0:16], PS[6][:, 0:16], float(CEN), None, AL.add, None, ["#6"], ["k1u"])
+        ts(T.mh[:, 0, :], T.b0[:], 1.0, None, AL.mult, None, ["b0"], key("K", "h0"))
+        ts(T.ioo[:], T.ioo[:], cR, None, AL.add, None, ["ioo", "cG"], ["ioo"])
+        cp(cT2, T.thw[:, 0:1], ["th"], ["cT2"])
+        aff("v", cTH, cR0, -10000.0, 0.5, ["cR0"], ["cTH"])
+        cp(T.iob[:], T.iop[:], ["iop"], key("K2", "iob"))
+        tt(cTH, cTH, cT2, AL.add, ["cTH", "cT2"], ["cTH"])
+        ts(T.t1[:], T.u1[:], 16.5 - NS, None, AL.is_gt, None, ["u1"], ["t1"])
+        aff("v", cY, cR0, BETA, 0.0, ["cR0"], ["cY"])
+        tt(mat("nblk2"), T.t1[:], T.inb[:], AL.subtract, ["t1", "inb"], key("K2", "nb2"))
+        cp(A[:, 0:896], T.pin[:, 0:896], ["pin0"], ["A0"])
+        cp(A[:, 896:1792], T.pin[:, 896:1792], ["pin1", "A0", "A1", "A2"], ["A"])
+
+    def consts_s():
+        aff("s", cX, cR0, B, -B, ["cR0"], ["cX"])
+        for k in (0, 1):
+            aff("s", T.big[:, k, :], T.bb[:], (2.0, -1.0)[k], 0.0, ["bb"], key("K", "b%d" % k))
+        scaled("s", "K", [("nI", T.eq[:], "eq", -1.0, []), ("nblk", T.inb[:], "inb", -1.0, [])]
+               + [(nm, T.b0[:], "b0", wgt, []) for nm, wgt in (("b0e", -B), ("b0p", B), ("b0h", -256.0), ("b0c", 59392.0))])
+        aff("s", cZ2, cR0, float(y2w[0, 0] + BETA), -BETA, ["cR0"], ["cZ2"])
+        aff("s", cY2, cR0, -15.0, 1.0, ["cR0"], ["cY2"])
+        aff("s", cN15, cR0, -15.0, 0.0, ["cR0"], ["cN15"])
+        scaled("s", "K2", [("I256", T.eq[:], "eq", 256.0, []), ("In1", T.eq[:], "eq", BETA * 2 / B, []), ("I1", T.eq[:], "eq", cR1, ["cR1"]),
+                           ("LG", T.inb[:], "inb", cZ2, ["cZ2"]), ("LH", T.inb[:], "inb", cY2, ["cY2"]),
+                           ("CNb", T.b0[:], "b0", -15.0, []), ("CNa", T.z0[:], "z0", cN15, ["cN15"])])
+
+    def consts_s2():
+        scaled("s", "K", [("LF", T.t3[:], "t3", cX, ["cX"])])
+        aff("s", T.dum[:, 0:16], T.ioo[:, 0:16], 1.0, float(AD), ["ioo"], key("K", "d0"))
+        aff("s", T.dum[:, 16:32], T.ioo[:, 0:16], 1.0, float(AD + 256), ["ioo"] + done["K"], ["K"])
+
+    def consts_b():
+        aff("v", T.t1[:], T.eq[:], 2048.0, 0.0, ["eq"], ["t1"])
+        aff("v", T.t2[:], T.gt[:], -BETA, 0.0, ["gt"], ["t2"])
+        ts(T.t4[:], T.u1[:], -1.0, 0.0, AL.add, AL.max, ["u1"], ["t4"])
+        tt(T.t1[:], T.t1[:], T.t2[:], AL.add, ["t1", "t2"], ["t1"])
+        aff("v", T.t4[:], T.t4[:], cY, 0.0, ["t4", "cY"], ["t4"])
+        aff("v", cM, cR0, float(y2w[0, 0] - 2048.0 - BETA), -BETA, ["cR0"], ["cM"])
+        aff("v", T.t2[:], T.b0[:], 2 * BETA, 0.0, ["b0"], ["t2"])
+        tt(mat("LY1"), T.t1[:], T.t4[:], AL.add, ["t1", "t4"], key("K2", "ly1"))
+        aff("v", T.t1[:], T.z0[:], cM, 0.0, ["z0", "cM"], ["t1"])
+        aff("v", cZ3, cR0, -1.0, 1.0, ["cR0"], ["cZ3"])
+        tt(T.t1[:], T.t1[:], T.t2[:], AL.add, ["t1", "t2"], ["t1"])
+        aff("v", cC1, cR, -BETA, float(BETA - cor1[1]), ["cG"], ["cC1"])
+        aff("v", cC2, cR, -BETA, float(BETA - cor2[1]), ["cG"], ["cC2"])
+        tt(mat("LY2"), T.t1[:], MB("LY1"), AL.add, ["t1", "K2ly1"], key("K2", "ly2"))
+        ts(col[:, 24:26], col[:, 24:26], cZ3, None, AL.mult, None, ["cC1", "cC2", "cZ3"], ["cC"])
+        aff("v", cB0, cR0, LINKC - E, float(E), ["cR0"], ["cB0"])
+        scaled("v", "K2", [("C1b", T.inb[:], "inb", cC1, ["cC"]), ("C1a", T.z0[:], "z0", cC1, ["cC"]),
+                           ("C2b", T.inb[:], "inb", cC2, ["cC"]), ("C2a", T.z0[:], "z0", cC2, ["cC"])])
+        cp(T.mh[:, 1, :], T.inb[:], ["inb"], key("K2", "h1"))
+        cp(T.mh[:, 2, :], T.z0[:], ["z0"], key("K2", "h2"))
+        aff("v", cKD, cR, -8192.0, LINKC + 15 * 8192.0, ["cG"], key("K2", "kd"))
+        for t in range(NT):
+            aff("v", cAB[t], cR1, float(M + P * (t + 1) - E) if t < NT - 1 else 0.0, cB0, ["cR1", "cB0"], key("K2", "ab%d" % t))
+        ts(T.t256[:], T.t256[:], cR, None, AL.is_equal, None, ["t256", "cG"], ["t256"])
+        ts(T.dj[:], T.dj[:], cR, None, AL.add, None, ["dj", "cG"], ["dj"])
+        aff("v", T.dg[:], T.t256[:], float(2 ** 20 + 8192), -8192.0, ["t256"], key("K2", "dg"))
+        aff("v", T.thr[:, 4:8], T.dj[:], -B, -B / 2, ["dj", "cTH"] + done["K2"], ["K2"])
+
+    def consts_c():
+        aff("v", T.dh[:], T.t256[:, 0:64], float(2 ** 21 + 65536), -65536.0, ["t256"], key("K3", "dh"))
+        ms(T.rs[:], 0.0, ["rs"])
+        aff("v", cM, cR, 64.0, 0.0, ["cG"], ["cM"])
+        cp(cW, T.thw[:, 4:5], ["hw"], ["cW"])
+        ms(T.rs[:, 0::16], float(2 ** 22), ["rs"])
+        ts(T.kc[:], T.sq[:], cM, None, AL.add, None, ["sq", "cM"], key("K3", "kc"))
+        aff("v", cMX, cR0, float(E), 0.0, ["cR0"], key("K3", "mx"))
+        cp(T.mh[:, 3, :], T.eq[:], ["eq"], key("K3", "h3"))
+        scaled("v", "K3", [("W", T.inb[:], "inb", cW, ["cW"])])
+        for k in (2, 3):
+            aff("v", T.big[:, k, :], T.bb[:], (2048.0, -1024.0)[k - 2], 0.0, ["bb"], key("K3", "b%d" % k))
+        ts(T.pi[:, 3:4], T.pi[:, 2:3], 3, None, AL.bitwise_and, None, ["pi2"], ["pi3"])
+        ts(T.pi[:, 4:5], T.pi[:, 2:3], 2, None, AL.logical_shift_right, None, ["pi2"], ["pi4"])
+        aff("v", T.dmj[:, 0:4], T.dj[:], 1.0, float(FD - M - P), ["dj"], key("K3", "dm"))
+        cp(col[:, 13:15], T.pi[:, 3:5], ["pi3", "pi4"], ["c13"])
+        ts(col[:, 15:16], col[:, 13:14], 16.0, col[:, 14:15], AL.mult, AL.add, ["c13"], ["c15"])
+        ts(T.prm[:, 0:4], T.prf[:, 0:4], col[:, 15:16], None, AL.add, None, ["prf", "c15", "rs"] + done["K3"], ["K3"])
+
+    FALL = ["F", "F0", "F1", "F2"]
+    AB, MX = (T.a0, T.a1), (T.m0, T.m1)
+
+    def blocks(h, lo, hi):
+        return ["a%d_%d" % (h, k) for k in range(lo // 32, hi // 32)]
+
+    def arow(h, i, lo, hi):
+        return AB[h][:, 16 * lo + i:16 * hi:16]
+
+    def gather_a(q, h, lo, hi):
+        out, src = AB[h][:, 16 * lo:16 * hi], Fw.indirect(T.cu[:, 256 * h + lo:256 * h + hi])
+        if q == "s":
+            act(out, src, AF.Copy, FALL + ["cu%d" % h], blocks(h, lo, hi))
+        else:
+            cp(out, src, FALL + ["cu%d" % h], blocks(h, lo, hi))
+
+    def col1(t):
+        cp(T.cu[:, 0:256], Ar.indirect(T.ku[:, 0:16]), ["A", "k1u"], ["cu0"])
+        ts(T.c16[:, 0:256], T.cu[:, 0:256], float(-CEN), None, AL.add, None, ["cu0"], ["h1"])
+        mms(6, [(PS[6][:, 0:16], SEL(0, m), T.c16[:, m:256:16]) for m in range(16)], ["bigh0", "h1"])
+        if t > 0:
+            mms(1, [(PS[1][:, 0:16], SEL(1, m), T.c16[:, m:256:16]) for m in range(16)], ["bigh1", "h1"])
+
+    def col1_s(t):
+        act(T.c32[:, 0:256], Ar.indirect(T.ku[:, 0:16]), AF.Copy, ["A", "k1u"], ["c1"])
+        act(T.hi[:], T.c32[:, 0:256], AF.Identity, ["c1"], ["hi"], scale=1.0 / 256, bias=0.5 / 256 - 0.5 + 192 - t)
+        act(T.ee[:, 0:256], T.c32[:, 0:256], AF.Relu, ["c1"], ["e1"], bias=float(1 - E))
+
+    def next_k(t):
+        ts(T.ku[:, 16:32], PS[6][:, 0:16], float(CEN), None, AL.add, None, ["#6"], ["k2u"])
+        cp(T.kk[:, 0:32], T.ku[:, 0:32], ["k1u", "k2u"], ["kk"])
+        ts(T.pm[:], T.kk[:, 0:32], 255, None, AL.bitwise_and, None, ["kk"], ["pm"])
+        cp(T.pu[:], T.pm[:, 16:32], ["pm"], ["pu"])
+
+    def row1_k(t):
+        ts(T.ku[:, 32:48], PS[1][:, 0:16], float(CEN), None, AL.add, None, ["#1"], ["r1u"])
+
+    def col2_s(t):
+        act(T.c32[:, 256:512], Ar.indirect(T.ku[:, 16:32]), AF.Copy, ["A", "k2u"], ["c2"])
+        act(T.ee[:, 256:512], T.c32[:, 256:512], AF.Relu, ["c2"], ["e2"], bias=float(1 - E))
+        act(T.cs32[:], T.c32[:, 256:512], AF.Identity, ["c2"], ["cs32"], bias=float(-CEN))
+
+    def col2_v(t):
+        n0 = M + P * t
+        tt(T.e12[:], A[:, n0 - P:n0].indirect(T.pu[:]), T.c32[:, 0:256], AL.is_equal, ["A", "pu", "c1"], ["e12"])
+
+    def col2(t):
+        o = PS[5][:, 0:256]
+        mms(5, [(o, MB("b0c"), T.one[:]), (o, T.mh[:, 0, :], T.c16[:, 0:256]), (o, MB("b0h"), T.hi[:]), (o, MB("b0p"), T.ee[:, 0:256]),
+                (o, MB("LF"), T.ee[:, 256:512]), (o, MB("b0e"), T.e12[:])], ["K", "h1", "hi", "e1", "e2", "e12"])
+        tt(T.c16[:, 256:512], o, T.cs32[:], AL.min, ["#5", "cs32"], ["h2"])
+        ts(T.cu[:, 256:512], T.c16[:, 256:512], float(CEN), None, AL.add, None, ["h2"], ["cu1"])
+
+    def mark_w(t):
+        act(T.w[:], PS[5][:, 0:256], AF.Relu, ["#5"], ["w"], scale=-1.0, bias=float(E - CEN))
+
+    def write_offsets(t):
+        tt(T.own[:], T.pm[:], T.ioo[:], AL.not_equal, ["pm", "ioo"], ["own"])
+        tt(T.ne[:], T.kk[:, 0:16], T.kk[:, 16:32], AL.is_equal, ["kk"], ["ne"])
+        tt(T.own[:, 16:32], T.own[:, 16:32], T.ne[:], AL.max, ["own", "ne"], ["own"])
+        tt(T.own[:], T.own[:], T.dum[:], AL.mult, ["own", "K"], ["own"])
+        tt(T.so[:], T.own[:], T.kk[:, 0:32], AL.max, ["own", "kk"], ["so"])
+        cp(T.sou[:], T.so[:], ["so"], ["sou"])
+
+    def sum_a(h, rows, lo, hi, start):
+        mms(h, [(PS[h][:, lo:hi], RED(1, i), arow(h, i, lo, hi)) for i in rows], ["K"] + blocks(h, lo, hi), start=start, stop=False)
+
+    def xblk(t):
+        return F[:, M + P * t:M + P * t + P]
+
+    def x_psum(t):
+        mms(2, [(PS[2][:, 0:256], MB("I"), xblk(t))], ["K"] + FALL)
+
+    def maxes(h, rows, lo, hi, stop=False):
+        for i in rows:
+            nm = "m%d_%d_%d" % (h, i, lo)
+            o = MX[h][:, 256 * i + lo:256 * i + hi]
+            tt(o, arow(h, i, lo, hi), PS[2][:, lo:hi], AL.max, blocks(h, lo, hi) + ["#2"], [nm])
+            mms(h, [(PS[h][:, lo:hi], RED(0, i), o)], ["K", nm], start=False, stop=stop)
+
+    DB = (3, 5)
+
+    def diff_x(t):
+        for k in range(NS // 2):
+            mms(DB[k], [(PS[DB[k]][:, 256 * r:256 * r + 256], MB("nI"), xblk(t)) for r in range(2)], ["K"] + FALL, stop=False)
+
+    def diff_a(t, lo, hi, stop):
+        for k in range(NS // 2):
+            mms(DB[k], [(PS[DB[k]][:, 256 * r + lo:256 * r + hi], MB("I"), arow(1, 16 - NS + 2 * k + r, lo, hi)) for r in range(2)],
+                ["K"] + blocks(1, lo, hi), start=False, stop=stop)
+
+    def diff_abs(t, k):
+        i = 16 - NS + 2 * k
+        act(T.m1[:, 256 * i:256 * i + 512], PS[DB[k]][:], AF.Abs, ["#%d" % DB[k]], ["md%d" % k], scale=0.5)
+
+    def diff_sum(t, k):
+        i = 16 - NS + 2 * k
+        mms(1, [(PS[1][:, 0:256], RED(0, i + r), T.m1[:, 256 * (i + r):256 * (i + r) + 256]) for r in range(2)], ["K", "md%d" % k],
+            start=False, stop=False)
+
+    def row1_gather(t):
+        act(T.af[:], Fw.indirect(T.ku[:, 32:48]), AF.Copy, FALL + ["r1u"], ["af"])
+
+    def row1_max(t):
+        mms(0, [(PS[0][:, 0:256], RED(1, 1), T.af[:])], ["K", "af"], start=False, stop=False)
+        tt(T.m0[:, 256:512], T.af[:], PS[2][:, 0:256], AL.max, ["af", "#2"], ["m0_1_0"])
+        mms(0, [(PS[0][:, 0:256], RED(0, 1), T.m0[:, 256:512])], ["K", "m0_1_0"], start=False, stop=False)
+
+    def decide1(t):
+        mms(0, [(PS[0][:, 0:256], MB("nblk"), xblk(t))], ["K"] + FALL, start=False)
+        act(T.s[:, 0:256], PS[0][:, 0:256], AF.Sign, ["#0", "K2"], ["s1"], scale=-1.0, bias=cTH)
+        mms(7, [(PS[7][:, 0:256], MB("LH"), T.s[:, 0:256])], ["K2", "s1"])
+        mms(4, [(PS[4][:, 0:256], MB("LY1"), T.s[:, 0:256])], ["K2", "s1"])
+        act(T.n1[:], PS[7][:, 0:256], AF.Relu, ["#7"], ["n1"], scale=-B)
+
+    def write1(t):
+        o = PS[6][:, 0:256]
+        mms(6, [(o, MB("LF"), T.ee[:, 0:256]), (o, MB("I"), T.iob[:]), (o, MB("nI"), T.n1[:])], ["K", "K2", "e1", "n1"])
+        act(T.tw[:, 0:256], o, AF.Relu, ["#6"], ["tw1"], scale=-1.0, bias=float(E - M - P * t - 2 * B))
+
+    def decide1_v(t):
+        tt(T.sel[:, 0:256], PS[4][:, 0:256], T.c16[:, 0:256], AL.min, ["#4", "h1"], ["sel1"])
+        tt(T.pen[:], T.n1[:].indirect(T.pu[:]), T.w[:], AL.is_lt, ["n1", "pu", "w"], ["pen"])
+
+    def scatter(h):
+        tt(Aw.indirect(T.sou[:, 16 * h:16 * h + 16]), T.c32[:, 256 * h:256 * h + 256], T.tw[:, 256 * h:256 * h + 256],
+           AL.subtract, ["sou", "c%d" % (h + 1), "tw%d" % (h + 1)], ["A"])
+
+    def link_a(bank, sfx, hsel, extra):
+        o = PS[bank][:, 0:256]
+        mms(bank, extra + [(o, MB("C1" + sfx), T.s[:, 0:256]), (o, MB("CN" + sfx), T.n1[:]), (o, T.mh[:, hsel, :], T.sel[:, 0:256])],
+            ["K2", "s1", "n1", "sel1"], stop=False)
+
+    def link_b(bank, sfx, hsel):
+        o = PS[bank][:, 0:256]
+        mms(bank, [(o, MB("C2" + sfx), T.s[:, 256:512]), (o, T.mh[:, hsel, :], T.sel[:, 256:512])], ["K2", "s2", "sel2"], start=False)
+
+    def new_rows(t):
+        n0 = M + P * t
+        act(A[:, n0:n0 + P], PS[2][:, 0:256], AF.Identity, ["#2", "K2"], ["A"], bias=cAB[t])
+
+    def counts(t):
+        for c in range(4):
+            act(T.jk[:, 256 * c:256 * c + 256], T.cum[:], AF.Sign, ["cum", "K2"], ["acc%d" % c], bias=T.thr[:, 4 + c:5 + c],
+                accum_out=T.acc[:, c:c + 1])
+
+    ACC = ["acc0", "acc1", "acc2", "acc3"]
+
+    def link_k(t):
+        scan(T.sc[:], T.dg[:], PS[0][:, 0:256], AL.add, AL.min, ["K2", "#0"], ["sc"])
+        ts(T.ku[:, 0:16], T.sc[:, 15::16], cKD, None, AL.add, None, ["sc", "K2"], ["k1u"])
+
+    def ask(t):
+        n0 = M + P * t
+        ts(T.psu[:, 0:4], T.acc[:, 0:4], -0.5, 128.0, AL.mult, AL.add, ACC, ["psu"])
+        cp(T.xs[:, 64 * t:64 * t + 64], F[:, n0:n0 + P + 16].indirect(T.psu[:, 0:4]), FALL + ["psu"], ["xs%d" % t])
+        send((rank + 1 + t % (N - 1)) % N, T.lx[:, 64 * t:64 * t + 64], T.xs[:, 64 * t:64 * t + 64], "req%d" % t, ["xs%d" % t])
+        arrives((rank - 1 - t % (N - 1)) % N, "req%d" % t, "lx%d" % t)
+
+    def ask_b(t):
+        n1 = M + P * (t + 1)
+        ts(T.psf[:, 4:8], T.acc[:, 0:4], -0.5, -127.0, AL.mult, AL.add, ACC, ["psg"])
+        ts(T.psf[:, 0:4], T.acc[:, 0:4], -0.5, 128.0, AL.mult, AL.add, ACC, ["psf"])
+        tt(T.pst[:, 0:4], T.psf[:, 4:8], T.dmj[:, 0:4], AL.mult, ["psg", "K3"], ["pst"])
+        ts(T.pre[:], F[:, n1:n1 + P + 16].indirect(T.psu[:, 0:4]), 0.5, 191.75, AL.mult, AL.add, FALL + ["psu"], ["pre"])
+        tt(T.pst[:, 0:4], T.pst[:, 0:4], T.psf[:, 0:4], AL.max, ["pst", "psf"], ["pst"])
+        cp(T.apu[:, 0:4], T.pst[:, 0:4], ["pst"], ["apu"])
+
+    SBK = (4, 3)
+
+    def serve_a(t):
+        lx, nm = T.lx[:, 64 * t:64 * t + 64], "lx%d" % t
+        mms(7, [(PS[7][:, 0:64], MB("W"), lx)], ["K3", nm])
+        for hf in range(2):
+            mms(SBK[hf], [(PS[SBK[hf]][:, i::16], MB("I"), T.lx[:, 64 * t + 32 * hf:64 * t + 32 * hf + 32]) for i in range(16)],
+                ["K", nm], each=True)
+        scan(T.sq[:], T.dh[:], PS[7][:, 0:64], AL.add, AL.min, ["K3", "#7"], ["sq"])
+        cp(T.q32[:, 0:4], T.sq[:, 15::16], ["sq"], ["q32"])
+        ts(T.q33[:, 0:4], T.q32[:, 0:4], 2047, None, AL.bitwise_and, None, ["q32"], ["q33"])
+        cp(T.qu[:, 0:4], T.q33[:, 0:4], ["q33"], ["qu"])
+        ts(T.cq[:], A[:, 0:M].indirect(T.qu[:, 0:4]), cMX, None, AL.max, None, ["A", "qu", "K3"], ["cq"])
+
+    def serve_s(t):
+        act(T.sa[:, 512:1024], Fw.indirect(T.cq[:, 32:64]), AF.Copy, FALL + ["cq"], ["sa1"])
+
+    def serve_b(t):
+        cp(T.sa[:, 0:512], Fw.indirect(T.cq[:, 0:32]), FALL + ["cq"], ["sa0"])
+        o = PS[7][:, 0:64]
+        for hf in range(2):
+            mms(7, ([(o, T.mh[:, 3, :], T.kc[:])] if hf == 0 else [])
+                + [(o, RED(3, m), T.sa[:, 64 * m:64 * m + 64]) for m in range(8 * hf, 8 * hf + 8)],
+                ["K3", "sa%d" % hf], start=hf == 0, stop=False)
+        for hf in range(2):
+            tt(T.sm[:, 512 * hf:512 * hf + 512], T.sa[:, 512 * hf:512 * hf + 512], PS[SBK[hf]][:], AL.max,
+               ["sa%d" % hf, "#%d" % SBK[hf]], ["sm%d" % hf])
+            mms(7, [(o, RED(2, m), T.sm[:, 64 * m:64 * m + 64]) for m in range(8 * hf, 8 * hf + 8)],
+                ["K3", "sm%d" % hf], start=False, stop=hf == 1)
+
+    def serve_c(t):
+        scan(T.sq[:], T.rs[:], PS[7][:, 0:64], AL.add, AL.min, ["K3", "#7"], ["sq"])
+        cp(T.q32[:, 0:4], T.sq[:, 15::16], ["sq"], ["q32"])
+        ts(T.q33[:, 0:4], T.q32[:, 0:4], 1023, None, AL.bitwise_and, None, ["q32"], ["q33"])
+        cp(T.qu[:, 0:4], T.q33[:, 0:4], ["q33"], ["qu"])
+        ts(T.fh[:, 64 * t:64 * t + 64], T.sa[:, 0:1024].indirect(T.qu[:, 0:4]), 0.5, None, AL.mult, None, ["sa0", "sa1", "qu"], ["fh%d" % t])
+        send((rank - 1 - t % (N - 1)) % N, T.lf[:, 64 * t:64 * t + 64], T.fh[:, 64 * t:64 * t + 64], "rep%d" % t, ["fh%d" % t])
+        arrives((rank + 1 + t % (N - 1)) % N, "rep%d" % t, "lf%d" % t)
+
+    def apply(t):
+        n1 = M + P * (t + 1)
+        tt(T.vv[:], T.lf[:, 64 * t:64 * t + 64].indirect(T.prm[:, 0:4]), T.pre[:], AL.add, ["lf%d" % t, "K3", "pre"], ["vv"])
+        tt(F[:, n1:n1 + FD + 64 - M - P].indirect(T.apu[:, 0:4]), T.vv[:], T.neg[:], AL.add, ["vv", "apu", "K3"], FALL)
+
+    consts_s()
+    first_k()
+    consts_s2()
+    col1(0)
+    col1_s(0)
+    x_psum(0)
+    gather_a("s", 0, 0, 64)
+    next_k(0)
+    col2_s(0)
+    col2_v(0)
+    gather_a("s", 0, 64, 256)
+    col2(0)
+    consts_b()
+    mark_w(0)
+    write_offsets(0)
+    sum_a(0, range(1, 16), 0, 256, True)
+    VR = range(1, 16 - NS)
+    for t in range(NT):
+        last = t == NT - 1
+        n0 = M + P * t
+        if t > 0:
+            row1_gather(t)
+        gather_a("s", 1, 0, 128)
+        maxes(0, range(1 if t == 0 else 2, 8), 0, 256)
+        diff_x(t)
+        mms(1, [(PS[1][:, 0:256], MB("nblk2"), xblk(t))], ["K2"] + FALL, stop=False)
+        if t > 0:
+            row1_max(t)
+        maxes(0, range(8, 13), 0, 256)
+        sum_a(1, VR, 0, 128, False)
+        diff_a(t, 0, 128, False)
+        maxes(0, range(13, 16), 0, 256)
+        gather_a("s", 1, 128, 192)
+        decide1(t)
+        maxes(1, VR[:4], 0, 128)
+        gather_a("s", 1, 192, 256)
+        diff_a(t, 128, 192, False)
+        sum_a(1, VR, 128, 192, False)
+        maxes(1, VR[4:], 0, 128)
+        decide1_v(t)
+        diff_a(t, 192, 256, True)
+        for k in range(NS // 2):
+            diff_abs(t, k)
+        sum_a(1, VR, 192, 256, False)
+        maxes(1, VR[:3], 128, 256)
+        write1(t)
+        mms(1, [(PS[1][:, 0:256], MB("I256"), T.pen[:])], ["K2", "pen"], start=False, stop=False)
+        maxes(1, VR[3:6], 128, 256)
+        diff_sum(t, 0)
+        maxes(1, VR[6:-2], 128, 256)
+        diff_sum(t, 1)
+        maxes(1, VR[-2:-1], 128, 256)
+        maxes(1, VR[-1:], 128, 256, stop=True)
+        act(T.s[:, 256:512], PS[1][:, 0:256], AF.Sign, ["#1", "K2"], ["s2"], scale=-1.0, bias=cTH)
+        for bank in (7, 4):
+            mms(bank, [(PS[bank][:, 0:256], MB("In1"), T.n1[:])], ["K2", "n1"], stop=False)
+        o3 = PS[3][:, 0:256]
+        scatter(0)
+        mms(7, [(PS[7][:, 0:256], MB("LG"), T.s[:, 256:512])], ["K2", "s2"], start=False)
+        act(T.go[:], PS[7][:, 0:256], AF.Relu, ["#7"], ["go"], scale=2.0)
+        mms(4, [(PS[4][:, 0:256], MB("LY2"), T.s[:, 256:512])], ["K2", "s2"], start=False)
+        mms(3, [(o3, MB("LF"), T.ee[:, 256:512]), (o3, MB("I"), T.iob[:]), (o3, MB("nI"), T.go[:])], ["K", "K2", "e2", "go"])
+        if not last:
+            link_a(0, "b", 1, [])
+            scan(T.cum[:], T.one[:], T.go[:], AL.mult, AL.add, ["K", "go"], ["cum"])
+        tt(T.sel[:, 256:512], PS[4][:, 0:256], T.c16[:, 256:512], AL.min, ["#4", "h2"], ["sel2"])
+        act(T.tw[:, 256:512], o3, AF.Relu, ["#3"], ["tw2"], scale=-1.0, bias=float(E - n0 - 2 * B))
+        if not last:
+            link_b(0, "b", 1)
+        link_a(2, "a", 2, [] if last else [(PS[2][:, 0:256], MB("I1"), T.iob[:])])
+        link_b(2, "a", 2)
+        if last:
+            dma("sy", "st0", T.yx[:], F[:, M:E], FALL, [])
+            scatter(1)
+            new_rows(t)
+            break
+        counts(t)
+        scatter(1)
+        ms(A[:, E:E + 1], float(E), ["A"])
+        new_rows(t)
+        ask(t)
+        link_k(t)
+        col1(t + 1)
+        if t == 0:
+            consts_c()
+        col1_s(t + 1)
+        gather_a("s", 0, 0, G1)
+        next_k(t + 1)
+        serve_a(t)
+        serve_s(t)
+        serve_b(t)
+        col2_s(t + 1)
+        gather_a("s", 0, G1, 128)
+        col2_v(t + 1)
+        serve_c(t)
+        gather_a("s", 0, 128, GV)
+        col2(t + 1)
+        mark_w(t + 1)
+        ask_b(t)
+        row1_k(t + 1)
+        if GV < 256:
+            gather_a("v", 0, GV, 256)
+        sum_a(0, range(2, 16), 0, 128, True)
+        write_offsets(t + 1)
+        apply(t)
+        x_psum(t + 1)
+        sum_a(0, range(2, 16), 128, 256, False)
+    dma("sy", "st1", T.yp[:, 0:E // 2], A[:, 0:E // 2], ["A"], [])
+    dma("s", "st2", T.yp[:, E // 2:E], A[:, E // 2:E], ["A"], [])
+    need("sy", ("st0", 16))
+    need("sy", ("st1", 16))
+    need("sy", ("st2", 16))
+    g.wait_ge(T.sem.sent, sent[0])
+    for q in cnt:
+        need("sy", (q, cnt[q]))

@@ -1,58 +1,57 @@
-import numpy as np
 from concourse.mybir import dt, AluOpType, AxisListType, ActivationFunctionType
 
 M, P, NT, C = 2048, 256, 5, 64
 E = M + NT * P
 CEN = 1792
 AD = 3336
-FD = 3344
-B = 4096.0
-BETA = 1920.0
-NS = 4
-G1, GV = 64, 224
+LINK = -49920.0
+XB = True
+GAT = [("s", 0, 0, 32), ("s", 0, 32, 96), ("s", 0, 96, 160), ("s", 0, 160, 192), ("v", 0, 192, 224), ("v", 0, 224, 256), ("s", 1, 0, 64),
+       ("s", 1, 64, 128), ("s", 1, 128, 160), ("s", 1, 160, 192), ("s", 1, 192, 224), ("v", 1, 224, 256)]
+GAT0 = [("s", 0, 0, 64), ("s", 0, 64, 128), ("v", 0, 128, 192), ("s", 0, 192, 256), ("s", 1, 0, 64), ("s", 1, 64, 128),
+        ("s", 1, 128, 192), ("v", 1, 192, 256)]
+MC = ((0, 128), (128, 256))
+SCH = ((0, 64), (64, 128), (128, 192), (192, 256))
+SA = "s"
+CYC, GC, SC, HOP, REM = 0.00091, 1.5, 3.0, 0.11, 2.0
+ORDER = {
+    0: "00070i0n0o0k0p0809010q0j022q0z0a0u0w1a1719180m1t2n100t1l233c110v1d2h390x0r381f1n0b1413272r2s03242u29281y2v151v1x1w1m2d2a2y2b2e2z2f162c2t1z312g0d3a3d0y1h332i3e1q3b1i1j1o0c0e040f050h0g0634352x30323j3o3p1c3f3w1g3k1p3l3q3m413y2o4x3g1b3n3z1u1k3x3v3r444f454q5051534j474g464k3s5557595b2j5d1s4043424b5f5h2l4y3t4z4r565c54584l485a365k5m4o5j5o5q1e493h3i5s5p5g5u5w62696b6d5r4v4i5l4s5e5i4m5t525v6c665n4t6f6h2m2p1r6j126l4a6n4c6p2k6r6t6v0l0s6x6z714d3u76785x6i6a60614h6s20214w5y7a4p4e257c7e7g7i5z7k7m6e6m634n737o7q7s7u7w6w836y72817y842685827f70676u7d7n64772w6k7h7l6g6o657v7p7x7j757t796q687r747b7z4u223780",
+    1: "0e0h090208000a030b06040f0g0q0j0k0i0r0n0s0o0v0w0x0y0l0z0m100c0t0p13110d050u0701181a1914151d12161c171s2d1m2e1l1n1p2g2f1z2h2i202j1o1v2n2k212l2m222p2o2q2r242s1t2t1k1b1e2u2v1f1i2w2x2y23281u1q271w341r1j1x292z30311y393d3f3h3j3l3n1h3a262a322c37334c3p3r3t3w3y4042443b461g484e4l4n4p4r4t4v4x4z51535557595b5d5i5k5m5o5q5s5u5w5y6062646668254i3c3i3g3v3o3e3k3u3s3z3x3q41453m47434m494a2b4w586d506f545l4u4q5a5z4f5n4b5c4d5f565g4g4h634o5v65695x615t4y4j5r5h4s4k5j52675e5p386a6g6e6h6b356c36",
+    2: "0005030c010d06020409070i0j0k0h0e0a0b080l0m0f0n0p0o0q161b1p1z22232425260g0u0v0x280w2021290r270s2c2e0t102a1e2b2d2f1f1g2g182o2p2h172i192j1l2k1t1h0y0z1d2l111a2m1m2n1n2v1o2z1q2q2r1v31333537393b3d3f1u2w2x3i3k3m3o3q3s3u4013124749144b4d4f4h4j1c153y2y1w303h38343z363g3c323l3p3r3n3t3a484c3e4e414k4i3j4g4a3v1i1x3w4l4n1j4p4r4t4v1k4x4z5456585a5c5e45611y3x4s511s4q4y1r5g5i5k5m5o5q5s625u2u42554u524w5z43595j5r5t5d4m445l5b5h4o505n465p575v535f5w5x60632t2s5y",
+    5: "02000305010406070809",
+}
 f32, bf, f16, i32, u16 = "float32", "bfloat16", "float16", "int32", "uint16"
 
 SB = {
-    "A": ([AD + 512], f32), "F": ([FD + 832], bf), "pin": ([M], i32), "thw": ([8], i32),
+    "A": ([AD + 512], f32), "F": ([E + 32], bf), "X": ([NT, 320], bf), "lk": ([256], f32), "pin": ([M + 8], i32), "thw": ([8], i32),
     "a0": ([4096], bf), "a1": ([4096], bf), "m0": ([4096], bf), "m1": ([4096], bf),
-    "af": ([256], bf), "c32": ([512], f32), "cs32": ([256], f32), "cu": ([512], u16), "c16": ([512], f16),
-    "ee": ([512], bf), "e12": ([256], bf), "hi": ([256], bf), "w": ([256], bf), "pen": ([256], bf), "s": ([512], bf),
-    "n1": ([256], bf), "go": ([256], bf), "sel": ([512], f16), "tw": ([512], f32), "cum": ([256], bf),
-    "jk": ([1024], bf), "acc": ([8], f32), "psu": ([8], u16), "psf": ([8], f32),
-    "pst": ([8], f32), "apu": ([8], u16), "sc": ([256], f32), "kk": ([48], i32), "ku": ([48], u16), "pm": ([32], i32),
-    "pu": ([16], u16), "own": ([32], f32), "so": ([32], f32), "sou": ([32], u16), "dmj": ([8], f32), "ne": ([16], f32),
+    "xo": ([512], bf), "cs": ([256], f16), "cu": ([512], u16), "c16": ([512], f16),
+    "ge": ([512], f16), "e12": ([256], f16), "em": ([256], f16), "hi": ([256], bf), "s": ([768], bf), "so1": ([256], bf),
+    "go": ([320], bf), "sel": ([512], f16), "nc": ([512], f32), "cum": ([320], bf),
+    "jk": ([4, 320], bf), "acc": ([8], f32), "psu": ([8], u16), "sc": ([256], f32), "kk": ([32], i32), "ku": ([32], u16), "pm": ([32], i32),
+    "pu": ([32], u16), "own": ([32], f32), "so": ([32], f32), "sou": ([32], u16),
     "xs": ([256], bf), "lx": ([256], bf), "fh": ([256], bf), "lf": ([256], bf), "pre": ([64], f32), "vv": ([64], bf),
     "q32": ([8], i32), "q33": ([8], i32), "qu": ([8], u16), "cq": ([64], u16), "sa": ([1024], bf), "sm": ([1024], bf),
-    "sq": ([64], f32), "pi": ([8], i32), "col": ([32], f32), "U": ([144], bf), "t0": ([144], bf), "t1": ([128], bf),
-    "t2": ([128], bf), "t3": ([128], bf), "t4": ([128], bf), "inb": ([128], bf), "eq": ([128], bf), "gt": ([128], bf),
-    "z0": ([128], bf), "bb": ([144], bf), "b0": ([128], bf), "u1": ([128], bf),
-    "big": ([4, 144], bf), "bigh": ([2, 144], f16), "mb": ([26, 128], bf), "mh": ([4, 128], f16),
-    "iop": ([256], f32), "iob": ([256], bf), "one": ([256], bf), "dg": ([256], f32), "dh": ([64], f32), "rs": ([64], f32),
-    "kc": ([64], f16), "neg": ([64], bf), "ioo": ([32], f32), "dum": ([32], f32), "dj": ([4], f32), "thr": ([8], f32),
-    "c0": ([256], f16), "t256": ([256], f32), "prm": ([8], u16), "prf": ([8], f32),
+    "sq": ([64], f32), "pi": ([8], i32), "col": ([48], f32), "U": ([144], bf), "t0": ([144], bf), "t1": ([128], bf),
+    "bb": ([144], bf), "big": ([4, 144], bf), "bigh": ([2, 144], f16), "mb": ([36, 128], bf), "mh": ([16, 128], f16),
+    "iob": ([256], bf), "iox": ([256], bf), "r1n": ([256], f32), "dh": ([64], f32), "rs": ([64], f32), "t64": ([64], f32),
+    "kc": ([64], f16), "neg": ([64], bf), "ioo": ([32], f32), "dum": ([32], f32), "dj": ([4], f32), "thr": ([4], f32),
+    "c0": ([256], f16), "prm": ([8], u16), "prf": ([8], f32), "i64": ([64], f32),
 }
 SCRATCH = {k: ("sbuf", [128] + v[0], v[1]) for k, v in SB.items()}
 for _b in range(8):
-    SCRATCH["p%d" % _b] = ("psum", [128, 512], f32)
-SEMAPHORES = (["v", "s", "pe", "gc", "ld0", "ld1", "ld2", "ld3", "ld4", "ld5", "ld6", "st0", "st1", "st2", "sent"]
-              + ["req%d" % t for t in range(4)] + ["rep%d" % t for t in range(4)])
+    SCRATCH["p%d" % _b] = ("psum", [128, 1024], bf) if XB and _b == 3 else ("psum", [128, 512], f32)
+SEMAPHORES = (["v", "s", "pe", "gc", "sent"] + ["ld%d" % k for k in range(8)] + ["st%d" % k for k in range(3)]
+              + [nm + str(t) for nm in ("fc", "req", "rep") for t in range(4)])
 
 
-def priority_weights():
-    y1 = np.zeros((16, 16))
-    y2 = np.zeros((16, 16))
-    for i in range(16):
-        y1[i, i] = 2048.0
-        y2[i, i] = 2048.0
-        for j in range(1, i):
-            y1[j, i] = -BETA
-            y2[j, i] = -BETA
-        if i >= 1:
-            y1[0, i] = BETA * (i - 1)
-            y2[0, i] = BETA * (i + 1)
-    y2[0, 0] = 2 * BETA - 2048.0 + 15 * BETA
-    y2[1:, 0] = -BETA
-    return y1, y2
+def issue_order(nodes):
+    seq = []
+    for p in range(NT + 1):
+        ids = [j for j, nd in enumerate(nodes) if nd["per"] == p]
+        o = ORDER[p if p in ORDER else 2]
+        seq += [ids[int(o[k:k + 2], 36)] for k in range(0, len(o), 2)]
+    return seq
 
 
 def rank_program(g, core, T, topo):
@@ -62,150 +61,234 @@ def rank_program(g, core, T, topo):
     N = len(T.cores)
     AL, AF = AluOpType, ActivationFunctionType
     Q = {"v": g.vector, "s": g.scalar, "pe": g.tensor, "gc": g, "sy": g.sync}
-    cnt = {"v": 0, "s": 0, "pe": 0, "gc": 0}
-    seen = {q: {} for q in Q}
-    lastw, readers = {}, {}
-    sent = [0]
+    V, S = g.vector, g.scalar
+    nodes, lastw, readers, per = [], {}, {}, [0]
 
-    def need(q, ev):
-        sem, val = ev
-        if seen[q].get(sem, 0) < val:
-            Q[q].wait_ge(T.sem[sem], val)
-            seen[q][sem] = val
-
-    def deps(q, rd, wr):
-        best = {}
-        evs = [lastw[r] for r in list(rd) + list(wr) if r in lastw and not (r[0] == "#" and lastw[r][0] == q)]
-        for r in wr:
-            evs += readers.get(r, [])
-        for sem, val in evs:
-            best[sem] = max(best.get(sem, 0), val)
-        for sem in best:
-            need(q, (sem, best[sem]))
-
-    def mark(ev, rd, wr):
+    def node(q, fn, rd, wr, cost, lat=HOP, dma=0.0, ev=None, kind=0):
+        pre = {}
+        for r in list(rd) + list(wr):
+            for i in ([lastw[r]] if r in lastw else []) + (readers.get(r, []) if r in wr else []):
+                pre[i] = pre.get(i, False) or not (r[0] == "#" and nodes[i]["q"] == q)
+        j = len(nodes)
+        nodes.append({"q": q, "fn": fn, "pre": pre, "cost": cost, "dma": dma, "ev": ev, "kind": kind, "per": per[0], "lab": list(wr) + list(rd)})
         for r in rd:
-            readers.setdefault(r, []).append(ev)
+            readers.setdefault(r, []).append(j)
         for r in wr:
-            lastw[r] = ev
+            lastw[r] = j
             readers[r] = []
 
-    def op(q, fn, rd, wr):
-        wr = list(wr) + [r for r in rd if r[0] == "#"]
-        rd = [r for r in rd if r[0] != "#"]
-        deps(q, rd, wr)
-        cnt[q] += 1
-        fn().then_inc(T.sem[q], 1)
-        mark((q, cnt[q]), rd, wr)
+    def width(x):
+        n = 1
+        for d in x.shape[1:]:
+            n *= d
+        return n
 
-    def mms(bank, items, rd, start=True, stop=True, each=False):
-        wr = ["#%d" % bank]
-        deps("pe", rd, wr)
-        for k, (o, l, r) in enumerate(items):
-            ins = g.tensor.matmul(o, l, r, each or (start and k == 0), each or (stop and k == len(items) - 1))
-        cnt["pe"] += 1
-        ins.then_inc(T.sem.pe, 1)
-        mark(("pe", cnt["pe"]), rd, wr)
+    def op(q, fn, rd, wr, n, ind=0.0):
+        node(q, fn, [r for r in rd if r[0] != "#"], list(wr) + [r for r in rd if r[0] == "#"],
+             0.06 + n * ind * CYC if ind else max(n, 64) * CYC, kind=1 if ind == GC else 2 if ind else 0)
 
-    def dma(q, sem, out, in_, rd, wr):
-        deps(q, rd, wr)
-        Q[q].dma_start(out, in_).then_inc(T.sem[sem], 16)
-        mark((sem, 16), rd, wr)
+    def mms(bank, items, rd, start=True, stop=True, each=False, wr=()):
+        def fn():
+            for k, (o, l, r) in enumerate(items):
+                ins = g.tensor.matmul(o, l, r, each or (start and k == 0), each or (stop and k == len(items) - 1))
+            return ins
+        b = ["#%d" % bank]
+        mid = not (start or stop)
+        node("pe", fn, list(rd) + (b if mid else []), ([] if mid else b) + list(wr), sum(max(64, width(r)) for _, _, r in items) * CYC / 2)
 
-    def send(dst_rank, out, in_, sem, rd):
+    def dma(q, sem, out, in_, rd, wr, nbytes):
+        node(q, lambda: Q[q].dma_start(out, in_), rd, wr + ["#q" + q], 0.05, 0.0, nbytes / 4e5 + 0.1, (sem, 16))
+
+    sent = [0]
+
+    def send(dst_rank, src_rank, out, in_, sem, rd, name):
         dst = T.cores[dst_rank]
         rid, pid = topo.addr(dst)[:2]
-        deps("gc", rd, [])
-        g.remote_dma(out, in_, T.sem[sem], T.sem.sent, pid, rid, topo.mask(core, dst))
         sent[0] += len(topo.engines(core, dst))
+        node("gc", lambda: g.remote_dma(out, in_, T.sem[sem], T.sem.sent, pid, rid, topo.mask(core, dst)), rd, [name], 0.3, REM, 0.0,
+             (sem, len(topo.engines(T.cores[src_rank], core))), 3)
 
-    def arrives(src_rank, sem, name):
-        lastw[name] = (sem, len(topo.engines(T.cores[src_rank], core)))
-
-    V, S = g.vector, g.scalar
-
-    def ts(out, in0, s1, s2, o0, o1, rd, wr):
+    def ts(out, in0, s1, s2, o0, o1, rd, wr, per=1.0, ind=0.0, n=None):
+        n = n or width(out)
         if o1 is None:
-            op("v", lambda: V.tensor_scalar(out, in0, s1, None, o0), rd, wr)
+            op("v", lambda: V.tensor_scalar(out, in0, s1, None, o0), rd, wr, n * per, ind)
         else:
-            op("v", lambda: V.tensor_scalar(out, in0, s1, s2, o0, o1), rd, wr)
+            op("v", lambda: V.tensor_scalar(out, in0, s1, s2, o0, o1), rd, wr, n * per, ind)
 
-    def tt(out, a, b, o, rd, wr):
-        op("v", lambda: V.tensor_tensor(out, a, b, o), rd, wr)
+    def tt(out, a, b, o, rd, wr, per=1.0, ind=0.0):
+        op("v", lambda: V.tensor_tensor(out, a, b, o), rd, wr, width(b) * per, ind)
 
-    def cp(out, a, rd, wr):
-        op("v", lambda: V.tensor_copy(out, a), rd, wr)
+    def cp(out, a, rd, wr, per=1.0, ind=0.0):
+        op("v", lambda: V.tensor_copy(out, a), rd, wr, width(out) * per, ind)
 
-    def ms(out, val, wr):
-        op("v", lambda: V.memset(out, val), [], wr)
+    def ms(out, val, wr, n=64):
+        op("v", lambda: V.memset(out, val), [], wr, n)
 
-    def scan(out, d0, d1, o0, o1, rd, wr):
-        op("v", lambda: V.tensor_tensor_scan(out, d0, d1, 0.0, o0, o1), rd, wr)
+    def scan(out, d0, d1, o0, o1, rd, wr, per=1.0):
+        op("v", lambda: V.tensor_tensor_scan(out, d0, d1, 0.0, o0, o1), rd, wr, width(out) * per)
 
-    def act(out, a, f, rd, wr, **kw):
-        op("s", lambda: S.activation(out, a, f, **kw), rd, wr)
+    def act(out, a, f, rd, wr, ind=0.0, **kw):
+        op("s", lambda: S.activation(out, a, f, **kw), rd, wr, width(out), ind)
 
     def iota(out, pat, cm, wr, flag=True, base=0):
         if flag:
-            op("gc", lambda: g.iota(out, pat, base, cm, allow_small_or_imprecise_dtypes=True), [], wr)
+            op("gc", lambda: g.iota(out, pat, base, cm, allow_small_or_imprecise_dtypes=True), [], wr, 150 + 2 * width(out))
         else:
-            op("gc", lambda: g.iota(out, pat, base, cm), [], wr)
+            op("gc", lambda: g.iota(out, pat, base, cm), [], wr, 150)
 
-    def aff(q, out, a, scale, bias, rd, wr):
+    def aff(q, out, a, scale, bias, rd, wr, per=1.0):
         if q == "v":
-            ts(out, a, scale, bias, AL.mult, AL.add, rd, wr)
+            ts(out, a, scale, bias, AL.mult, AL.add, rd, wr, per)
         else:
             act(out, a, AF.Identity, rd, wr, scale=scale, bias=bias)
 
     PS = [T["p%d" % b] for b in range(8)]
-    A, F = T.A, T.F
-    Aw, Ar, Fw = A[:, 0:AD + 512], A[:, 0:E + 8], F[:, 0:FD + 64]
+    A, F, X = T.A, T.F, T.X
+    Aw, Fw = A[:, 0:AD + 512], F[:, 0:E + 32]
     U = T.U[:, 0:128]
 
-    dma("sy", "ld0", T.pin[:, 1792:M], T.ptr[:, 1792:M], [], ["pinT"])
-    dma("sy", "ld5", T.thw[:, 0:1], T.th[:], [], ["th"])
-    dma("sy", "ld1", T.pin[:, 0:896], T.ptr[:, 0:896], [], ["pin0"])
-    dma("sy", "ld2", T.pin[:, 896:1792], T.ptr[:, 896:1792], [], ["pin1"])
-    dma("sy", "ld3", F[:, 0:M], T.fr[:], [], ["F0"])
-    dma("sy", "ld4", F[:, M:E], T.nw[:], [], ["F1"])
-    dma("sy", "ld6", T.thw[:, 4:5], T.hw[:], [], ["hw"])
+    dma("sy", "ld0", T.pin[:, 1792:M], T.ptr[:, 1792:M], [], ["pinT"], 131072)
+    dma("sy", "ld5", T.thw[:, 0:1], T.th[:], [], ["th"], 30000)
+    dma("sy", "ld1", T.pin[:, 0:1792], T.ptr[:, 0:1792], [], ["pin0"], 917504)
+    dma("sy", "ld3", F[:, 16:16 + M], T.fr[:], [], ["F0"], 524288)
+    dma("sy", "ld4", X[:, 0, 0:P], T.nw[:, 0:P], [], ["X0"], 65536)
+    dma("sy", "ld7", X[:, 1:NT, 0:P], T.nw[:, P:NT * P], [], ["X2"], 262144)
+    dma("sy", "ld6", T.thw[:, 4:5], T.hw[:], [], ["hw"], 30000)
 
-    col = T.col
-    cG, cR, cR0, cR1, cN1, cTH, cKD, cMX, cW, cX, cY, cZ, cM = [col[:, j:j + 1] for j in range(13)]
-    cAB = [col[:, 16 + t:17 + t] for t in range(NT)]
-    cC1, cC2, cZ2, cZ3, cB0, cY2, cT2, cN15 = [col[:, j:j + 1] for j in range(24, 32)]
+    cols, mats = {}, {}
+
+    def col(nm):
+        cols.setdefault(nm, len(cols))
+        return T.col[:, cols[nm]:cols[nm] + 1]
+
+    def mat(nm, h=False):
+        if nm not in mats:
+            mats[nm] = (T.mh if h else T.mb)[:, sum(1 for v in mats.values() if v[1] == h), :], h
+        return mats[nm][0]
+
+    def cmp(nm, src, val, o, mul=None):
+        if mul is None:
+            ts(col(nm), col(src), val, None, o, None, [src], [nm])
+        else:
+            ts(col(nm), col(src), val, mul, o, AL.mult, [src], [nm])
+
+    def lin(nm, src, mul, add, q="v"):
+        aff(q, col(nm), col(src), col(mul) if mul in cols else mul, col(add) if add in cols else add, [src] + [z for z in (mul, add) if z in cols], [nm])
+
+    def sc(nm, base, w, q="s", h=False):
+        aff("v" if h else q, mat(nm, h), mat(base), col(w) if w in cols else w, 0.0, [base] + ([w] if w in cols else []), [nm], 0.5)
+
+    def add(nm, a, b, o=AL.add, h=False):
+        tt(mat(nm, h), mat(a), mat(b), o, [a, b], [nm], 2.0)
+
     iota(T.pi[:, 0:1], [[0, 1]], 1, ["pi0"], False)
     iota(T.t0[:], [[1, 144]], 0, ["t0"])
     iota(T.t1[:], [[16, 8], [0, 16]], 0, ["t1"])
-    iota(T.iop[:], [[1, 256]], 0, ["iop"])
-    iota(A[:, M:E + 8], [[0, E + 8 - M]], 0, ["A2"], base=E)
+    iota(T.iob[:], [[1, 256]], 0, ["iob"])
     iota(T.ioo[:], [[0, 2], [16, 16]], 0, ["ioo"])
-    iota(T.one[:], [[0, 256]], 0, ["Kf"], base=1)
-    iota(T.t256[:], [[0, 16], [1, 16]], 0, ["t256"])
     iota(T.dj[:], [[16, 4]], 0, ["dj"])
-    iota(T.sq[:], [[1, 64]], 0, ["sq"])
+    iota(A[:, M:E + 8], [[0, E + 8 - M]], 0, ["A2"], base=E)
+    iota(T.t64[:], [[0, 4], [1, 16]], 0, ["t64"])
+    iota(T.i64[:], [[1, 64]], 0, ["i64"])
     iota(T.prf[:, 0:4], [[4, 4]], 0, ["prf"])
-    iota(T.neg[:], [[0, 64]], 0, ["j7"], base=-192)
-    ms(F[:, E:FD + 64], 99.0, ["F2"])
+    iota(T.neg[:], [[0, 64]], 0, ["neg"], base=-192)
+    ms(F[:, 16 + M:E + 32], 99.0, ["F2"], 650)
+    ms(T.go[:, P:320], 1.0, ["go1"])
+    ms(F[:, 0:16], 99.0, ["F1"])
+    ms(X[:, :, P:320], 0.0, ["X1"], 160)
+    ms(T.pin[:, M:M + 8], E, ["pinE"])
     ts(T.pi[:, 1:2], T.pi[:, 0:1], 112, None, AL.bitwise_and, None, ["pi0"], ["pi1"])
     ts(T.pi[:, 2:3], T.pi[:, 0:1], 15, None, AL.bitwise_and, None, ["pi0"], ["pi2"])
-    cp(col[:, 0:2], T.pi[:, 1:3], ["pi1", "pi2"], ["cG"])
-    ts(cR0, cR, 0.0, None, AL.is_equal, None, ["cG"], ["cR0"])
-    ts(T.U[:], T.t0[:], cG, None, AL.subtract, None, ["t0", "cG"], ["U"])
-    ts(cR1, cR, 1.0, None, AL.is_equal, None, ["cG"], ["cR1"])
-    ts(T.inb[:], T.t1[:], cG, None, AL.is_equal, None, ["t1", "cG"], ["inb"])
-    ts(T.bb[:], T.U[:], 15.0, None, AL.is_equal, None, ["U"], ["bb"])
-    ts(T.eq[:], U, cR, None, AL.is_equal, None, ["U", "cG"], ["eq"])
-    ts(T.bigh[:, 0, :], T.bb[:], cR0, None, AL.mult, None, ["bb", "cR0"], ["bigh0"])
-    ts(T.t2[:], U, 1.0, None, AL.add, None, ["U"], ["t2"])
-    ts(T.b0[:], T.inb[:], cR0, None, AL.mult, None, ["inb", "cR0"], ["b0"])
-    tt(T.u1[:], T.t2[:], T.inb[:], AL.mult, ["t2", "inb"], ["u1"])
-    ts(cN1, cR, 1.0, None, AL.not_equal, None, ["cG"], ["cN1"])
-    ts(T.bigh[:, 1, :], T.bb[:], cR1, None, AL.mult, None, ["bb", "cR1"], ["bigh1"])
-    ts(cZ, cR, 1.0, None, AL.add, None, ["cG"], ["cZ"])
-    ts(T.cs32[:], T.iop[:], float(M), cR1, AL.add, AL.mult, ["iop", "cR1"], ["cs32"])
-    ts(T.gt[:], T.u1[:], cZ, None, AL.is_gt, None, ["u1", "cZ"], ["gt"])
-    ts(T.z0[:], T.u1[:], 1.0, None, AL.is_equal, None, ["u1"], ["z0"])
+    cp(col("G"), T.pi[:, 1:2], ["pi1"], ["G"])
+    cp(col("R"), T.pi[:, 2:3], ["pi2"], ["R"])
+    cp(col("TH"), T.thw[:, 0:1], ["th"], ["TH"])
+    cp(col("W"), T.thw[:, 4:5], ["hw"], ["W"])
+    cmp("R0", "R", 0.0, AL.is_equal)
+    cmp("R1", "R", 1.0, AL.is_equal)
+    cmp("N1", "R", 1.0, AL.not_equal)
+    cmp("LFc", "R", 1.5, AL.is_gt, -8192.0)
+    lin("CE", "R1", float(-1 - E), float(E))
+    cp(T.pin[:, M:M + 1], col("CE"), ["CE"], ["pinE"])
+    ts(T.U[:], T.t0[:], col("G"), None, AL.subtract, None, ["t0", "G"], ["U"], 0.5)
+    ts(T.bb[:], T.U[:], 15.0, None, AL.is_equal, None, ["U"], ["bb"], 0.5)
+    ts(T.bigh[:, 0, :], T.bb[:], col("R0"), None, AL.mult, None, ["bb", "R0"], ["SEL"], 0.5)
+    ts(T.bigh[:, 1, :], T.bb[:], -1.0, None, AL.mult, None, ["bb"], ["NRED"], 0.5)
+    for k, w in enumerate((2.0, -1.0, 2048.0, -1024.0)):
+        aff("s", T.big[:, k, :], T.bb[:], w, 0.0, ["bb"], ["big%d" % k])
+    ts(mat("inb"), T.t1[:], col("G"), None, AL.is_equal, None, ["t1", "G"], ["inb"], 0.5)
+    ts(mat("I"), U, col("R"), None, AL.is_equal, None, ["U", "R"], ["I"], 0.5)
+    ts(mat("z0"), U, 0.0, None, AL.is_equal, None, ["U"], ["z0"], 0.5)
+    ts(mat("gU"), U, col("R"), None, AL.is_gt, None, ["U", "R"], ["gU"], 0.5)
+    ts(mat("p01"), U, 1.0, col("R0"), AL.is_equal, AL.mult, ["U", "R0"], ["p01"], 0.5)
+    ts(mat("g2"), U, 1.5, 512.0, AL.is_gt, AL.mult, ["U"], ["g2"], 0.5)
+    add("gt", "gU", "inb", AL.mult)
+    add("PEN", "g2", "inb", AL.mult)
+    add("t3", "I", "gt", AL.subtract)
+    sc("LF", "t3", "LFc", h=True)
+    sc("b0", "inb", "R0", h=True)
+    sc("b0p", "b0", 4096.0, h=True)
+    sc("b0e", "b0", -32768.0, h=True)
+    sc("b0n", "b0", -4096.0, h=True)
+    lin("n256", "R0", -256.0, 0.0, "s")
+    sc("b0h", "inb", "n256")
+    lin("cB", "R1", -1.0, 0.0)
+    ts(col("cA"), col("TH"), 1024.0, col("cB"), AL.add, AL.mult, ["TH", "cB"], ["cA"])
+    sc("R1m", "z0", "cA", h=True)
+    sc("In", "I", -1024.0, h=True)
+    sc("Ip", "I", 1024.0, h=True)
+    sc("nI16", "I", -1.0, h=True)
+    sc("nz16", "z0", -1.0, h=True)
+    sc("I16", "I", 1.0, h=True)
+    for nm, base, w in (("nblk", "inb", -1.0), ("inb2", "inb", 2.0), ("H", "inb", 2048.0), ("ZS", "z0", -1024.0), ("Inb", "I", -1024.0),
+                        ("LY", "t3", 2048.0), ("y1x", "p01", 4096.0), ("nI", "I", -1.0)):
+        sc(nm, base, w)
+    lin("y2c", "R0", -2048.0, -2048.0, "s")
+    sc("y2x", "z0", "y2c")
+    add("LY1", "LY", "y1x")
+    add("LY2", "LY", "y2x")
+    for t in range(NT):
+        lin("mv%d" % t, "R1", float(256 * (t + 1) + 10 * 4096), "R0", "s")
+        sc("MT%d" % t, "inb", "mv%d" % t)
+    ts(T.iox[:], T.iob[:], col("R0"), col("R1"), AL.mult, AL.add, ["iob", "R0", "R1"], ["iox"], 0.5)
+    lin("N0", "R0", -1.0, 1.0)
+    ts(col("TN"), col("TH"), 0.5, col("N0"), AL.add, AL.mult, ["TH", "N0"], ["TN"])
+    lin("T1", "R0", -1023.5, "TN")
+    lin("T2a", "R0", 15000.0, 1024.0)
+    lin("T2", "TN", 1.0, "T2a")
+    lin("Twa", "LFc", 1.0, -1024.0)
+    lin("Twb", "R0", -100000.0, "Twa")
+    lin("Tw", "TN", 1.0, "Twb")
+    lin("cy", "R", -2048.0, -512.0, "s")
+    lin("cy1a", "R1", 4096.0, "cy", "s")
+    lin("cy1", "R0", -100000.0, "cy1a", "s")
+    lin("cy2", "R0", 1536.0 - 32768.0 + 512.0, "cy", "s")
+    for h in "12":
+        lin("n" + h, "cy" + h, -1.0, 0.0, "s")
+        lin("a" + h, "cy" + h, 1.0, -1664.0, "s")
+    lin("B0", "R0", LINK - E, float(E), "s")
+    for t in range(NT - 1):
+        lin("AB%d" % t, "R1", float(M + P * (t + 1) - E), "B0", "s")
+    ts(T.ioo[:], T.ioo[:], col("R"), None, AL.add, None, ["ioo", "R"], ["ioo"])
+    aff("s", T.dum[:, 0:16], T.ioo[:, 0:16], 1.0, float(AD), ["ioo"], ["dum0"])
+    aff("s", T.dum[:, 16:32], T.ioo[:, 0:16], 1.0, float(AD + 256), ["ioo"], ["dum1"])
+    ts(T.dj[:], T.dj[:], col("R"), None, AL.add, None, ["dj", "R"], ["dj"])
+    aff("s", T.thr[:], T.dj[:], -1.0, -0.5, ["dj"], ["thr"])
+
+    def consts_x():
+        ts(T.t64[:], T.t64[:], col("R"), None, AL.is_equal, None, ["t64", "R"], ["t64"])
+        aff("s", T.dh[:], T.t64[:], float(2 ** 21 + 65536), -65536.0, ["t64"], ["dh"])
+        ms(T.rs[:], 0.0, ["rs"])
+        ms(T.rs[:, 0::16], float(2 ** 22), ["rs"])
+        lin("R64", "R", 64.0, 0.0, "s")
+        ts(T.kc[:], T.i64[:], col("R64"), None, AL.add, None, ["i64", "R64"], ["kc"])
+        lin("MX", "R0", float(E), 0.0, "s")
+        sc("Wm", "inb", "W")
+        ts(T.pi[:, 3:4], T.pi[:, 2:3], 3, None, AL.bitwise_and, None, ["pi2"], ["pi3"])
+        ts(T.pi[:, 4:5], T.pi[:, 2:3], 2, None, AL.logical_shift_right, None, ["pi2"], ["pi4"])
+        cp(col("m4"), T.pi[:, 3:4], ["pi3"], ["m4"])
+        cp(col("d4"), T.pi[:, 4:5], ["pi4"], ["d4"])
+        lin("pr", "m4", 16.0, "d4")
+        ts(T.prm[:, 0:4], T.prf[:, 0:4], col("pr"), None, AL.add, None, ["prf", "pr"], ["prm"])
 
     def SEL(r, m):
         return T.bigh[:, r, 15 - m:143 - m]
@@ -213,115 +296,14 @@ def rank_program(g, core, T, topo):
     def RED(k, i):
         return T.big[:, k, 15 - i:143 - i]
 
-    names = {"I": -1}
+    def mm(bank, nm, rhs, rd, start=False, stop=False):
+        mms(bank, [(PS[bank][:, 0:256], mat(nm), rhs)], [nm] + rd, start, stop)
 
-    def mat(name):
-        names[name] = len(names)
-        return T.mb[:, names[name], :]
-
-    def MB(name):
-        return T.eq[:] if name == "I" else T.mb[:, names[name], :]
-
-    y1w, y2w = priority_weights()
-    cor1, cor2 = y1w.sum(1), y2w.sum(1)
-    LINKC = float(2048.0 + cor1[0] + cor2[0] + CEN)
-    done = {"K": ["eq", "Kf"], "K2": [], "K3": ["j7"]}
-
-    def key(s, name):
-        done[s].append(s + name)
-        return [s + name]
-
-    def scaled(q, s, todo):
-        for nm, base, bn, wgt, rd in todo:
-            aff(q, mat(nm), base, wgt, 0.0, [bn] + rd, key(s, nm))
-
-    def first_k():
-        ts(T.c0[:], T.pin[:, 1792:M], float(-CEN), None, AL.add, None, ["pinT"], ["c0"])
-        mms(6, [(PS[6][:, 0:16], SEL(0, m), T.c0[:, m::16]) for m in range(16)], ["bigh0", "c0"])
-        ts(T.sc[:], T.pin[:, 1792:M], cN1, None, AL.mult, None, ["pinT", "cN1"], ["sc"])
-        tt(T.t3[:], T.eq[:], T.gt[:], AL.subtract, ["eq", "gt"], ["t3"])
-        tt(A[:, 1792:M], T.sc[:], T.cs32[:], AL.add, ["sc", "cs32"], ["A1"])
-        ts(T.ku[:, 0:16], PS[6][:, 0:16], float(CEN), None, AL.add, None, ["#6"], ["k1u"])
-        ts(T.mh[:, 0, :], T.b0[:], 1.0, None, AL.mult, None, ["b0"], key("K", "h0"))
-        ts(T.ioo[:], T.ioo[:], cR, None, AL.add, None, ["ioo", "cG"], ["ioo"])
-        cp(cT2, T.thw[:, 0:1], ["th"], ["cT2"])
-        aff("v", cTH, cR0, -10000.0, 0.5, ["cR0"], ["cTH"])
-        cp(T.iob[:], T.iop[:], ["iop"], key("K2", "iob"))
-        tt(cTH, cTH, cT2, AL.add, ["cTH", "cT2"], ["cTH"])
-        ts(T.t1[:], T.u1[:], 16.5 - NS, None, AL.is_gt, None, ["u1"], ["t1"])
-        aff("v", cY, cR0, BETA, 0.0, ["cR0"], ["cY"])
-        tt(mat("nblk2"), T.t1[:], T.inb[:], AL.subtract, ["t1", "inb"], key("K2", "nb2"))
-        cp(A[:, 0:896], T.pin[:, 0:896], ["pin0"], ["A0"])
-        cp(A[:, 896:1792], T.pin[:, 896:1792], ["pin1", "A0", "A1", "A2"], ["A"])
-
-    def consts_s():
-        aff("s", cX, cR0, B, -B, ["cR0"], ["cX"])
-        for k in (0, 1):
-            aff("s", T.big[:, k, :], T.bb[:], (2.0, -1.0)[k], 0.0, ["bb"], key("K", "b%d" % k))
-        scaled("s", "K", [("nI", T.eq[:], "eq", -1.0, []), ("nblk", T.inb[:], "inb", -1.0, [])]
-               + [(nm, T.b0[:], "b0", wgt, []) for nm, wgt in (("b0e", -B), ("b0p", B), ("b0h", -256.0), ("b0c", 59392.0))])
-        aff("s", cZ2, cR0, float(y2w[0, 0] + BETA), -BETA, ["cR0"], ["cZ2"])
-        aff("s", cY2, cR0, -15.0, 1.0, ["cR0"], ["cY2"])
-        aff("s", cN15, cR0, -15.0, 0.0, ["cR0"], ["cN15"])
-        scaled("s", "K2", [("I256", T.eq[:], "eq", 256.0, []), ("In1", T.eq[:], "eq", BETA * 2 / B, []), ("I1", T.eq[:], "eq", cR1, ["cR1"]),
-                           ("LG", T.inb[:], "inb", cZ2, ["cZ2"]), ("LH", T.inb[:], "inb", cY2, ["cY2"]),
-                           ("CNb", T.b0[:], "b0", -15.0, []), ("CNa", T.z0[:], "z0", cN15, ["cN15"])])
-
-    def consts_s2():
-        scaled("s", "K", [("LF", T.t3[:], "t3", cX, ["cX"])])
-        aff("s", T.dum[:, 0:16], T.ioo[:, 0:16], 1.0, float(AD), ["ioo"], key("K", "d0"))
-        aff("s", T.dum[:, 16:32], T.ioo[:, 0:16], 1.0, float(AD + 256), ["ioo"] + done["K"], ["K"])
-
-    def consts_b():
-        aff("v", T.t1[:], T.eq[:], 2048.0, 0.0, ["eq"], ["t1"])
-        aff("v", T.t2[:], T.gt[:], -BETA, 0.0, ["gt"], ["t2"])
-        ts(T.t4[:], T.u1[:], -1.0, 0.0, AL.add, AL.max, ["u1"], ["t4"])
-        tt(T.t1[:], T.t1[:], T.t2[:], AL.add, ["t1", "t2"], ["t1"])
-        aff("v", T.t4[:], T.t4[:], cY, 0.0, ["t4", "cY"], ["t4"])
-        aff("v", cM, cR0, float(y2w[0, 0] - 2048.0 - BETA), -BETA, ["cR0"], ["cM"])
-        aff("v", T.t2[:], T.b0[:], 2 * BETA, 0.0, ["b0"], ["t2"])
-        tt(mat("LY1"), T.t1[:], T.t4[:], AL.add, ["t1", "t4"], key("K2", "ly1"))
-        aff("v", T.t1[:], T.z0[:], cM, 0.0, ["z0", "cM"], ["t1"])
-        aff("v", cZ3, cR0, -1.0, 1.0, ["cR0"], ["cZ3"])
-        tt(T.t1[:], T.t1[:], T.t2[:], AL.add, ["t1", "t2"], ["t1"])
-        aff("v", cC1, cR, -BETA, float(BETA - cor1[1]), ["cG"], ["cC1"])
-        aff("v", cC2, cR, -BETA, float(BETA - cor2[1]), ["cG"], ["cC2"])
-        tt(mat("LY2"), T.t1[:], MB("LY1"), AL.add, ["t1", "K2ly1"], key("K2", "ly2"))
-        ts(col[:, 24:26], col[:, 24:26], cZ3, None, AL.mult, None, ["cC1", "cC2", "cZ3"], ["cC"])
-        aff("v", cB0, cR0, LINKC - E, float(E), ["cR0"], ["cB0"])
-        scaled("v", "K2", [("C1b", T.inb[:], "inb", cC1, ["cC"]), ("C1a", T.z0[:], "z0", cC1, ["cC"]),
-                           ("C2b", T.inb[:], "inb", cC2, ["cC"]), ("C2a", T.z0[:], "z0", cC2, ["cC"])])
-        cp(T.mh[:, 1, :], T.inb[:], ["inb"], key("K2", "h1"))
-        cp(T.mh[:, 2, :], T.z0[:], ["z0"], key("K2", "h2"))
-        aff("v", cKD, cR, -8192.0, LINKC + 15 * 8192.0, ["cG"], key("K2", "kd"))
-        for t in range(NT):
-            aff("v", cAB[t], cR1, float(M + P * (t + 1) - E) if t < NT - 1 else 0.0, cB0, ["cR1", "cB0"], key("K2", "ab%d" % t))
-        ts(T.t256[:], T.t256[:], cR, None, AL.is_equal, None, ["t256", "cG"], ["t256"])
-        ts(T.dj[:], T.dj[:], cR, None, AL.add, None, ["dj", "cG"], ["dj"])
-        aff("v", T.dg[:], T.t256[:], float(2 ** 20 + 8192), -8192.0, ["t256"], key("K2", "dg"))
-        aff("v", T.thr[:, 4:8], T.dj[:], -B, -B / 2, ["dj", "cTH"] + done["K2"], ["K2"])
-
-    def consts_c():
-        aff("v", T.dh[:], T.t256[:, 0:64], float(2 ** 21 + 65536), -65536.0, ["t256"], key("K3", "dh"))
-        ms(T.rs[:], 0.0, ["rs"])
-        aff("v", cM, cR, 64.0, 0.0, ["cG"], ["cM"])
-        cp(cW, T.thw[:, 4:5], ["hw"], ["cW"])
-        ms(T.rs[:, 0::16], float(2 ** 22), ["rs"])
-        ts(T.kc[:], T.sq[:], cM, None, AL.add, None, ["sq", "cM"], key("K3", "kc"))
-        aff("v", cMX, cR0, float(E), 0.0, ["cR0"], key("K3", "mx"))
-        cp(T.mh[:, 3, :], T.eq[:], ["eq"], key("K3", "h3"))
-        scaled("v", "K3", [("W", T.inb[:], "inb", cW, ["cW"])])
-        for k in (2, 3):
-            aff("v", T.big[:, k, :], T.bb[:], (2048.0, -1024.0)[k - 2], 0.0, ["bb"], key("K3", "b%d" % k))
-        ts(T.pi[:, 3:4], T.pi[:, 2:3], 3, None, AL.bitwise_and, None, ["pi2"], ["pi3"])
-        ts(T.pi[:, 4:5], T.pi[:, 2:3], 2, None, AL.logical_shift_right, None, ["pi2"], ["pi4"])
-        aff("v", T.dmj[:, 0:4], T.dj[:], 1.0, float(FD - M - P), ["dj"], key("K3", "dm"))
-        cp(col[:, 13:15], T.pi[:, 3:5], ["pi3", "pi4"], ["c13"])
-        ts(col[:, 15:16], col[:, 13:14], 16.0, col[:, 14:15], AL.mult, AL.add, ["c13"], ["c15"])
-        ts(T.prm[:, 0:4], T.prf[:, 0:4], col[:, 15:16], None, AL.add, None, ["prf", "c15", "rs"] + done["K3"], ["K3"])
-
-    FALL = ["F", "F0", "F1", "F2"]
     AB, MX = (T.a0, T.a1), (T.m0, T.m1)
+    bK, bY1, bV1, bY2, bV2, bGO, bLO, bLA = 7, 7, 4, 5, 6, 0, 2, 1
+    H = [slice(0, 256), slice(256, 512)]
+    c16, ge, s = [T.c16[:, h] for h in H], [T.ge[:, h] for h in H], [T.s[:, h] for h in H]
+    sw = T.s[:, 512:768]
 
     def blocks(h, lo, hi):
         return ["a%d_%d" % (h, k) for k in range(lo // 32, hi // 32)]
@@ -329,321 +311,226 @@ def rank_program(g, core, T, topo):
     def arow(h, i, lo, hi):
         return AB[h][:, 16 * lo + i:16 * hi:16]
 
-    def gather_a(q, h, lo, hi):
-        out, src = AB[h][:, 16 * lo:16 * hi], Fw.indirect(T.cu[:, 256 * h + lo:256 * h + hi])
-        if q == "s":
-            act(out, src, AF.Copy, FALL + ["cu%d" % h], blocks(h, lo, hi))
-        else:
-            cp(out, src, FALL + ["cu%d" % h], blocks(h, lo, hi))
-
-    def col1(t):
-        cp(T.cu[:, 0:256], Ar.indirect(T.ku[:, 0:16]), ["A", "k1u"], ["cu0"])
-        ts(T.c16[:, 0:256], T.cu[:, 0:256], float(-CEN), None, AL.add, None, ["cu0"], ["h1"])
-        mms(6, [(PS[6][:, 0:16], SEL(0, m), T.c16[:, m:256:16]) for m in range(16)], ["bigh0", "h1"])
-        if t > 0:
-            mms(1, [(PS[1][:, 0:16], SEL(1, m), T.c16[:, m:256:16]) for m in range(16)], ["bigh1", "h1"])
-
-    def col1_s(t):
-        act(T.c32[:, 0:256], Ar.indirect(T.ku[:, 0:16]), AF.Copy, ["A", "k1u"], ["c1"])
-        act(T.hi[:], T.c32[:, 0:256], AF.Identity, ["c1"], ["hi"], scale=1.0 / 256, bias=0.5 / 256 - 0.5 + 192 - t)
-        act(T.ee[:, 0:256], T.c32[:, 0:256], AF.Relu, ["c1"], ["e1"], bias=float(1 - E))
-
-    def next_k(t):
-        ts(T.ku[:, 16:32], PS[6][:, 0:16], float(CEN), None, AL.add, None, ["#6"], ["k2u"])
-        cp(T.kk[:, 0:32], T.ku[:, 0:32], ["k1u", "k2u"], ["kk"])
-        ts(T.pm[:], T.kk[:, 0:32], 255, None, AL.bitwise_and, None, ["kk"], ["pm"])
-        cp(T.pu[:], T.pm[:, 16:32], ["pm"], ["pu"])
-
-    def row1_k(t):
-        ts(T.ku[:, 32:48], PS[1][:, 0:16], float(CEN), None, AL.add, None, ["#1"], ["r1u"])
-
-    def col2_s(t):
-        act(T.c32[:, 256:512], Ar.indirect(T.ku[:, 16:32]), AF.Copy, ["A", "k2u"], ["c2"])
-        act(T.ee[:, 256:512], T.c32[:, 256:512], AF.Relu, ["c2"], ["e2"], bias=float(1 - E))
-        act(T.cs32[:], T.c32[:, 256:512], AF.Identity, ["c2"], ["cs32"], bias=float(-CEN))
-
-    def col2_v(t):
+    def prefetch(t):
         n0 = M + P * t
-        tt(T.e12[:], A[:, n0 - P:n0].indirect(T.pu[:]), T.c32[:, 0:256], AL.is_equal, ["A", "pu", "c1"], ["e12"])
-
-    def col2(t):
-        o = PS[5][:, 0:256]
-        mms(5, [(o, MB("b0c"), T.one[:]), (o, T.mh[:, 0, :], T.c16[:, 0:256]), (o, MB("b0h"), T.hi[:]), (o, MB("b0p"), T.ee[:, 0:256]),
-                (o, MB("LF"), T.ee[:, 256:512]), (o, MB("b0e"), T.e12[:])], ["K", "h1", "hi", "e1", "e2", "e12"])
-        tt(T.c16[:, 256:512], o, T.cs32[:], AL.min, ["#5", "cs32"], ["h2"])
-        ts(T.cu[:, 256:512], T.c16[:, 256:512], float(CEN), None, AL.add, None, ["h2"], ["cu1"])
-
-    def mark_w(t):
-        act(T.w[:], PS[5][:, 0:256], AF.Relu, ["#5"], ["w"], scale=-1.0, bias=float(E - CEN))
-
-    def write_offsets(t):
+        win, wn, top = (T.pin[:, 0:M + 8], ["pin0", "pinT", "pinE"], float(M)) if t == 0 else (A[:, 0:E + 8], ["A"], float(E))
+        FR = ["F", "F0", "F1", "F2"]
+        ts(T.cu[:, H[0]], win.indirect(T.ku[:, 0:16]), 16.0, None, AL.add, None, wn + ["k1u"], ["cu0"], ind=GC)
+        ts(c16[0], T.cu[:, H[0]], float(-CEN - 16), None, AL.add, None, ["cu0"], ["h1"], 0.5)
+        mms(bK, [(PS[bK][:, 0:16], SEL(0, m), T.c16[:, m:256:16]) for m in range(16)], ["SEL", "h1"])
+        ts(T.ku[:, 16:32], PS[bK][:, 0:16], float(CEN), top, AL.add, AL.min, ["#%d" % bK], ["k2u"])
+        ts(T.cu[:, H[1]], win.indirect(T.ku[:, 16:32]), 16.0, None, AL.add, None, wn + ["k2u"], ["cu1"], ind=GC)
+        for q, h, lo, hi in (GAT0 if t == 0 else GAT):
+            out, src = AB[h][:, 16 * lo:16 * hi], Fw.indirect(T.cu[:, 256 * h + lo:256 * h + hi])
+            if q == "s":
+                act(out, src, AF.Copy, FR + ["cu%d" % h], blocks(h, lo, hi), GC)
+            else:
+                cp(out, src, FR + ["cu%d" % h], blocks(h, lo, hi), ind=GC)
+        for h in range(2):
+            ts(ge[h], T.cu[:, H[h]], float(n0 + 16), None, AL.is_ge, None, ["cu%d" % h], ["ge%d" % h], 0.5)
+        cp(T.kk[:], T.ku[:], ["k1u", "k2u"], ["kk"])
+        ts(T.pm[:], T.kk[:], 255, None, AL.bitwise_and, None, ["kk"], ["pm"])
+        cp(T.pu[:], T.pm[:], ["pm"], ["pu"])
+        aff("v", T.hi[:], T.cu[:, H[0]], 1.0 / 256, -15.5 / 256 - 0.5 - 168 - t, ["cu0"], ["hi"], 0.5)
+        tt(T.e12[:], T.lk[:].indirect(T.pu[:, 16:32]), c16[0], AL.is_equal, ["lk", "pu", "h1"], ["e12"], ind=GC)
+        ts(T.cs[:], T.cu[:, H[1]], float(-CEN - 16), None, AL.add, None, ["cu1"], ["cs"], 0.5)
+        mm(bK, "b0", c16[0], ["h1"], True)
+        mm(bK, "b0h", T.hi[:], ["hi"])
+        mm(bK, "b0p", ge[0], ["ge0"])
+        mm(bK, "LF", ge[1], ["ge1"])
+        mm(bK, "b0e", T.e12[:], ["e12"], False, True)
+        tt(c16[1], PS[bK][:, 0:256], T.cs[:], AL.min, ["#%d" % bK, "cs"], ["h2"])
+        ts(T.em[:], c16[1], float(E - CEN), None, AL.is_equal, None, ["h2"], ["em"], 0.5)
         tt(T.own[:], T.pm[:], T.ioo[:], AL.not_equal, ["pm", "ioo"], ["own"])
-        tt(T.ne[:], T.kk[:, 0:16], T.kk[:, 16:32], AL.is_equal, ["kk"], ["ne"])
-        tt(T.own[:, 16:32], T.own[:, 16:32], T.ne[:], AL.max, ["own", "ne"], ["own"])
-        tt(T.own[:], T.own[:], T.dum[:], AL.mult, ["own", "K"], ["own"])
-        tt(T.so[:], T.own[:], T.kk[:, 0:32], AL.max, ["own", "kk"], ["so"])
+        tt(T.own[:], T.own[:], T.dum[:], AL.mult, ["own", "dum0", "dum1"], ["own"])
+        tt(T.so[:], T.own[:], T.kk[:], AL.max, ["own", "kk"], ["so"])
         cp(T.sou[:], T.so[:], ["so"], ["sou"])
+        mm(0, "R1m", ge[0], ["ge0"], True)
+        mm(2, "In", ge[1], ["ge1"], True)
+        mm(2, "Ip", T.em[:], ["em"])
+        mm(bY1, "nI16", c16[0], ["h1"], True)
+        for h in range(2):
+            for lo, hi in (SCH if h else ((0, 128), (128, 256))):
+                mms(h, [(PS[h][:, lo:hi], RED(1, i), arow(h, i, lo, hi)) for i in range(1, 16)],
+                    ["big1"] + blocks(h, lo, hi), h == 1 and lo == 0, False, wr=["#d%d" % lo] * h)
 
-    def sum_a(h, rows, lo, hi, start):
-        mms(h, [(PS[h][:, lo:hi], RED(1, i), arow(h, i, lo, hi)) for i in rows], ["K"] + blocks(h, lo, hi), start=start, stop=False)
+    def early(t):
+        for h, b in enumerate((bV1, bV2)):
+            mm(b, "MT%d" % t, T.iox[:], ["iox"], True)
+            mm(b, "LF", ge[h], ["ge%d" % h])
+        mm(bV2, "b0n", T.e12[:], ["e12"])
+        mm(bY2, "nI16", c16[1], ["h2"], True)
 
-    def xblk(t):
-        return F[:, M + P * t:M + P * t + P]
-
-    def x_psum(t):
-        mms(2, [(PS[2][:, 0:256], MB("I"), xblk(t))], ["K"] + FALL)
-
-    def maxes(h, rows, lo, hi, stop=False):
-        for i in rows:
-            nm = "m%d_%d_%d" % (h, i, lo)
-            o = MX[h][:, 256 * i + lo:256 * i + hi]
-            tt(o, arow(h, i, lo, hi), PS[2][:, lo:hi], AL.max, blocks(h, lo, hi) + ["#2"], [nm])
-            mms(h, [(PS[h][:, lo:hi], RED(0, i), o)], ["K", nm], start=False, stop=stop)
-
-    DB = (3, 5)
-
-    def diff_x(t):
-        for k in range(NS // 2):
-            mms(DB[k], [(PS[DB[k]][:, 256 * r:256 * r + 256], MB("nI"), xblk(t)) for r in range(2)], ["K"] + FALL, stop=False)
-
-    def diff_a(t, lo, hi, stop):
-        for k in range(NS // 2):
-            mms(DB[k], [(PS[DB[k]][:, 256 * r + lo:256 * r + hi], MB("I"), arow(1, 16 - NS + 2 * k + r, lo, hi)) for r in range(2)],
-                ["K"] + blocks(1, lo, hi), start=False, stop=stop)
-
-    def diff_abs(t, k):
-        i = 16 - NS + 2 * k
-        act(T.m1[:, 256 * i:256 * i + 512], PS[DB[k]][:], AF.Abs, ["#%d" % DB[k]], ["md%d" % k], scale=0.5)
-
-    def diff_sum(t, k):
-        i = 16 - NS + 2 * k
-        mms(1, [(PS[1][:, 0:256], RED(0, i + r), T.m1[:, 256 * (i + r):256 * (i + r) + 256]) for r in range(2)], ["K", "md%d" % k],
-            start=False, stop=False)
-
-    def row1_gather(t):
-        act(T.af[:], Fw.indirect(T.ku[:, 32:48]), AF.Copy, FALL + ["r1u"], ["af"])
-
-    def row1_max(t):
-        mms(0, [(PS[0][:, 0:256], RED(1, 1), T.af[:])], ["K", "af"], start=False, stop=False)
-        tt(T.m0[:, 256:512], T.af[:], PS[2][:, 0:256], AL.max, ["af", "#2"], ["m0_1_0"])
-        mms(0, [(PS[0][:, 0:256], RED(0, 1), T.m0[:, 256:512])], ["K", "m0_1_0"], start=False, stop=False)
-
-    def decide1(t):
-        mms(0, [(PS[0][:, 0:256], MB("nblk"), xblk(t))], ["K"] + FALL, start=False)
-        act(T.s[:, 0:256], PS[0][:, 0:256], AF.Sign, ["#0", "K2"], ["s1"], scale=-1.0, bias=cTH)
-        mms(7, [(PS[7][:, 0:256], MB("LH"), T.s[:, 0:256])], ["K2", "s1"])
-        mms(4, [(PS[4][:, 0:256], MB("LY1"), T.s[:, 0:256])], ["K2", "s1"])
-        act(T.n1[:], PS[7][:, 0:256], AF.Relu, ["#7"], ["n1"], scale=-B)
-
-    def write1(t):
-        o = PS[6][:, 0:256]
-        mms(6, [(o, MB("LF"), T.ee[:, 0:256]), (o, MB("I"), T.iob[:]), (o, MB("nI"), T.n1[:])], ["K", "K2", "e1", "n1"])
-        act(T.tw[:, 0:256], o, AF.Relu, ["#6"], ["tw1"], scale=-1.0, bias=float(E - M - P * t - 2 * B))
-
-    def decide1_v(t):
-        tt(T.sel[:, 0:256], PS[4][:, 0:256], T.c16[:, 0:256], AL.min, ["#4", "h1"], ["sel1"])
-        tt(T.pen[:], T.n1[:].indirect(T.pu[:]), T.w[:], AL.is_lt, ["n1", "pu", "w"], ["pen"])
-
-    def scatter(h):
-        tt(Aw.indirect(T.sou[:, 16 * h:16 * h + 16]), T.c32[:, 256 * h:256 * h + 256], T.tw[:, 256 * h:256 * h + 256],
-           AL.subtract, ["sou", "c%d" % (h + 1), "tw%d" % (h + 1)], ["A"])
-
-    def link_a(bank, sfx, hsel, extra):
-        o = PS[bank][:, 0:256]
-        mms(bank, extra + [(o, MB("C1" + sfx), T.s[:, 0:256]), (o, MB("CN" + sfx), T.n1[:]), (o, T.mh[:, hsel, :], T.sel[:, 0:256])],
-            ["K2", "s1", "n1", "sel1"], stop=False)
-
-    def link_b(bank, sfx, hsel):
-        o = PS[bank][:, 0:256]
-        mms(bank, [(o, MB("C2" + sfx), T.s[:, 256:512]), (o, T.mh[:, hsel, :], T.sel[:, 256:512])], ["K2", "s2", "sel2"], start=False)
-
-    def new_rows(t):
+    def distances(t):
         n0 = M + P * t
-        act(A[:, n0:n0 + P], PS[2][:, 0:256], AF.Identity, ["#2", "K2"], ["A"], bias=cAB[t])
+        x, FR = X[:, t, 0:P], ["X", "X0" if t == 0 else "X2"]
+        if t < NT - 1:
+            dma("sy", "fc%d" % t, F[:, 16 + n0:16 + n0 + P], x, FR, ["F"], 65536)
+        else:
+            dma("sy", "st0", T.yx[:], X[:, :, 0:P], ["X", "X0", "X2"], [], 327680)
+        xp = PS[3][:, 0:256]
+        if XB:
+            cp(xp, x, FR, ["#3", "xp"], 0.5)
+        else:
+            mm(3, "I", x, FR, True, True)
+        for h in range(2):
+            act(T.xo[:, H[h]], x.indirect(T.pu[:, 16 * h:16 * h + 16]), AF.Copy, FR + ["pu"], ["xo%d" % h], GC)
 
-    def counts(t):
-        for c in range(4):
-            act(T.jk[:, 256 * c:256 * c + 256], T.cum[:], AF.Sign, ["cum", "K2"], ["acc%d" % c], bias=T.thr[:, 4 + c:5 + c],
-                accum_out=T.acc[:, c:c + 1])
+        def mx(h, i, lo, hi, src, rd):
+            o = MX[h][:, 256 * i + lo:256 * i + hi]
+            tt(o, src, xp[:, lo:hi], AL.max, rd + ["#3", "xp"], ["m%d_%d_%d" % (h, i, lo)], 0.5 if XB else 1.0)
+            return o, ["m%d_%d_%d" % (h, i, lo)]
 
-    ACC = ["acc0", "acc1", "acc2", "acc3"]
+        mm(0, "nblk", x, FR)
+        for i in list(range(1, 10)) + [0] + list(range(10, 16)):
+            if i == 0:
+                mms(0, [(PS[0][:, 0:256], RED(1, 0), T.xo[:, H[0]])], ["big1", "xo0"], False, False)
+            o, nm = mx(0, i, 0, 256, arow(0, i, 0, 256) if i else T.xo[:, H[0]], blocks(0, 0, 256) if i else ["xo0"])
+            mms(0, [(PS[0][:, 0:256], RED(0, i), o)], ["big0"] + nm, False, i == 15)
+        act(s[0], PS[0][:, 0:256], AF.Sign, ["#0", "T1"], ["s1"], scale=-1.0, bias=col("T1"))
+        act(T.so1[:], s[0].indirect(T.pu[:, 16:32]), AF.Copy, ["s1", "pu"], ["so1"], GC)
+        mm(2, "nblk", x, FR)
+        mm(2, "nblk", T.xo[:, H[1]], ["xo1"])
+        o, nm = mx(1, 0, 0, 256, T.xo[:, H[1]], ["xo1"])
+        mm(2, "inb2", o, nm)
+        mm(2, "PEN", T.so1[:], ["so1"], False, True)
+        act(sw, PS[2][:, 0:256], AF.Sign, ["#2", "Tw"], ["sw"], scale=-1.0, bias=col("Tw"))
+        for lo, hi in MC:
+            dn = ["#d%d" % a for a, b in SCH if lo <= a < hi]
+            for nm, rhs, rd in (("nblk", x, FR), ("ZS", s[0], ["s1"]), ("Inb", sw, ["sw"])):
+                mms(1, [(PS[1][:, lo:hi], mat(nm), rhs[:, lo:hi])], [nm] + rd + dn, False, False)
+            for i in range(1, 16):
+                o, nm = mx(1, i, lo, hi, arow(1, i, lo, hi), blocks(1, lo, hi))
+                mms(1, [(PS[1][:, lo:hi], RED(0, i), o)], ["big0"] + nm + dn, False, hi == 256 and i == 15)
+        act(s[1], PS[1][:, 0:256], AF.Sign, ["#1", "T2"], ["s2"], scale=-1.0, bias=col("T2"))
 
-    def link_k(t):
-        scan(T.sc[:], T.dg[:], PS[0][:, 0:256], AL.add, AL.min, ["K2", "#0"], ["sc"])
-        ts(T.ku[:, 0:16], T.sc[:, 15::16], cKD, None, AL.add, None, ["sc", "K2"], ["k1u"])
+    def choose(h):
+        z, bY, bV = str(h + 1), (bY1, bY2)[h], (bV1, bV2)[h]
+        mm(bY, "LY" + z, s[h], ["s" + z], False, True)
+        ts(T.sel[:, H[h]], PS[bY][:, 0:256], col("n" + z), col("a" + z), AL.max, AL.add, ["#%d" % bY, "n" + z, "a" + z], ["sel" + z])
+        mm(bV, "H", s[h], ["s" + z], False, True)
+        tt(T.nc[:, H[h]], PS[bV][:, 0:256], T.cs[:] if h else c16[0], AL.min, ["#%d" % bV, "cs" if h else "h1"], ["nc" + z])
+        ts(Aw.indirect(T.sou[:, 16 * h:16 * h + 16]), T.nc[:, H[h]], 1.0, float(CEN), AL.mult, AL.add, ["sou", "nc" + z], ["A"], ind=SC, n=256)
+
+    def decide(t):
+        last, n0 = t == NT - 1, M + P * t
+        if not last:
+            mm(bGO, "inb", s[1], ["s2"], True, True)
+            act(T.go[:, 0:P], PS[bGO][:, 0:256], AF.Relu, ["#%d" % bGO], ["go"], scale=-1.0, bias=-15.0)
+            scan(T.cum[:], T.go[:], T.go[:], AL.add, AL.max, ["go", "go1"], ["cum"], 0.5)
+        choose(1)
+        if not last:
+            cp(A[:, E:E + 1], col("CE"), ["CE"], ["A"])
+            for h in range(2):
+                mms(bLO, [(PS[bLO][:, 0:16], SEL(1, m), T.sel[:, 256 * h + m:256 * h + 256:16]) for m in range(16)],
+                    ["NRED", "sel%d" % (h + 1)], h == 0, h == 1)
+            ts(T.ku[:, 0:16], PS[bLO][:, 0:16], LINK, None, AL.add, None, ["#%d" % bLO], ["k1u"])
+        mm(bLA, "nz16", T.sel[:, H[0]], ["sel1"], True)
+        if not last:
+            mm(bLA, "p01", T.iox[:], ["iox"])
+        mm(bLA, "nz16", T.sel[:, H[1]], ["sel2"], False, True)
+        ab = "B0" if last else "AB%d" % t
+        act(A[:, n0:n0 + P], PS[bLA][:, 0:256], AF.Identity, ["#%d" % bLA, ab], ["A"], bias=col(ab))
+        if not last:
+            act(T.lk[:], PS[bLA][:, 0:256], AF.Identity, ["#%d" % bLA], ["lk"], bias=LINK - CEN)
 
     def ask(t):
-        n0 = M + P * t
-        ts(T.psu[:, 0:4], T.acc[:, 0:4], -0.5, 128.0, AL.mult, AL.add, ACC, ["psu"])
-        cp(T.xs[:, 64 * t:64 * t + 64], F[:, n0:n0 + P + 16].indirect(T.psu[:, 0:4]), FALL + ["psu"], ["xs%d" % t])
-        send((rank + 1 + t % (N - 1)) % N, T.lx[:, 64 * t:64 * t + 64], T.xs[:, 64 * t:64 * t + 64], "req%d" % t, ["xs%d" % t])
-        arrives((rank - 1 - t % (N - 1)) % N, "req%d" % t, "lx%d" % t)
+        FR, ACC = ["X", "X0", "X1", "X2"], ["acc0", "acc1", "acc2", "acc3"]
+        for c in range(4):
+            act(T.jk[:, c, :], T.cum[:], AF.Sign, ["cum", "thr"], [ACC[c]], bias=T.thr[:, c:c + 1], accum_out=T.acc[:, c:c + 1])
+        ts(T.psu[:, 0:4], T.acc[:, 0:4], -0.5, 160.0, AL.mult, AL.add, ACC, ["psu"])
+        cp(T.xs[:, 64 * t:64 * t + 64], X[:, t, :].indirect(T.psu[:, 0:4]), FR + ["psu"], ["xs%d" % t], ind=GC)
+        d = 1 + t % (N - 1)
+        send((rank + d) % N, (rank - d) % N, T.lx[:, 64 * t:64 * t + 64], T.xs[:, 64 * t:64 * t + 64], "req%d" % t, ["xs%d" % t], "lx%d" % t)
+        ts(T.pre[:], X[:, t + 1, :].indirect(T.psu[:, 0:4]), 0.5, 191.75, AL.mult, AL.add, FR + ["psu"], ["pre"], ind=GC)
 
-    def ask_b(t):
-        n1 = M + P * (t + 1)
-        ts(T.psf[:, 4:8], T.acc[:, 0:4], -0.5, -127.0, AL.mult, AL.add, ACC, ["psg"])
-        ts(T.psf[:, 0:4], T.acc[:, 0:4], -0.5, 128.0, AL.mult, AL.add, ACC, ["psf"])
-        tt(T.pst[:, 0:4], T.psf[:, 4:8], T.dmj[:, 0:4], AL.mult, ["psg", "K3"], ["pst"])
-        ts(T.pre[:], F[:, n1:n1 + P + 16].indirect(T.psu[:, 0:4]), 0.5, 191.75, AL.mult, AL.add, FALL + ["psu"], ["pre"])
-        tt(T.pst[:, 0:4], T.pst[:, 0:4], T.psf[:, 0:4], AL.max, ["pst", "psf"], ["pst"])
-        cp(T.apu[:, 0:4], T.pst[:, 0:4], ["pst"], ["apu"])
-
-    SBK = (4, 3)
-
-    def serve_a(t):
-        lx, nm = T.lx[:, 64 * t:64 * t + 64], "lx%d" % t
-        mms(7, [(PS[7][:, 0:64], MB("W"), lx)], ["K3", nm])
+    def serve(t):
+        lx, nm, FR = T.lx[:, 64 * t:64 * t + 64], "lx%d" % t, ["F", "F0", "F1", "F2"]
+        o = PS[6][:, 0:64]
+        mms(6, [(o, mat("Wm"), lx)], ["Wm", nm])
         for hf in range(2):
-            mms(SBK[hf], [(PS[SBK[hf]][:, i::16], MB("I"), T.lx[:, 64 * t + 32 * hf:64 * t + 32 * hf + 32]) for i in range(16)],
-                ["K", nm], each=True)
-        scan(T.sq[:], T.dh[:], PS[7][:, 0:64], AL.add, AL.min, ["K3", "#7"], ["sq"])
+            mms(4 + hf, [(PS[4 + hf][:, i::16], mat("I"), T.lx[:, 64 * t + 32 * hf:64 * t + 32 * hf + 32]) for i in range(16)], ["I", nm], each=True)
+        scan(T.sq[:], T.dh[:], o, AL.add, AL.min, ["dh", "#6"], ["sq"])
         cp(T.q32[:, 0:4], T.sq[:, 15::16], ["sq"], ["q32"])
         ts(T.q33[:, 0:4], T.q32[:, 0:4], 2047, None, AL.bitwise_and, None, ["q32"], ["q33"])
         cp(T.qu[:, 0:4], T.q33[:, 0:4], ["q33"], ["qu"])
-        ts(T.cq[:], A[:, 0:M].indirect(T.qu[:, 0:4]), cMX, None, AL.max, None, ["A", "qu", "K3"], ["cq"])
-
-    def serve_s(t):
-        act(T.sa[:, 512:1024], Fw.indirect(T.cq[:, 32:64]), AF.Copy, FALL + ["cq"], ["sa1"])
-
-    def serve_b(t):
-        cp(T.sa[:, 0:512], Fw.indirect(T.cq[:, 0:32]), FALL + ["cq"], ["sa0"])
-        o = PS[7][:, 0:64]
+        ts(T.cq[:], A[:, 0:M].indirect(T.qu[:, 0:4]), col("MX"), 16.0, AL.max, AL.add, ["A", "qu", "MX"], ["cq"], ind=GC)
+        cp(T.sa[:, 0:512], Fw.indirect(T.cq[:, 0:32]), FR + ["cq"], ["sa0"], ind=GC)
+        if SA == "s":
+            act(T.sa[:, 512:1024], Fw.indirect(T.cq[:, 32:64]), AF.Copy, FR + ["cq"], ["sa1"], GC)
+        else:
+            cp(T.sa[:, 512:1024], Fw.indirect(T.cq[:, 32:64]), FR + ["cq"], ["sa1"], ind=GC)
+        mms(6, [(o, mat("I16"), T.kc[:])], ["I16", "kc"], True, False)
         for hf in range(2):
-            mms(7, ([(o, T.mh[:, 3, :], T.kc[:])] if hf == 0 else [])
-                + [(o, RED(3, m), T.sa[:, 64 * m:64 * m + 64]) for m in range(8 * hf, 8 * hf + 8)],
-                ["K3", "sa%d" % hf], start=hf == 0, stop=False)
+            mms(6, [(o, RED(3, m), T.sa[:, 64 * m:64 * m + 64]) for m in range(8 * hf, 8 * hf + 8)], ["big3", "sa%d" % hf], False, False)
         for hf in range(2):
-            tt(T.sm[:, 512 * hf:512 * hf + 512], T.sa[:, 512 * hf:512 * hf + 512], PS[SBK[hf]][:], AL.max,
-               ["sa%d" % hf, "#%d" % SBK[hf]], ["sm%d" % hf])
-            mms(7, [(o, RED(2, m), T.sm[:, 64 * m:64 * m + 64]) for m in range(8 * hf, 8 * hf + 8)],
-                ["K3", "sm%d" % hf], start=False, stop=hf == 1)
-
-    def serve_c(t):
-        scan(T.sq[:], T.rs[:], PS[7][:, 0:64], AL.add, AL.min, ["K3", "#7"], ["sq"])
+            tt(T.sm[:, 512 * hf:512 * hf + 512], T.sa[:, 512 * hf:512 * hf + 512], PS[4 + hf][:], AL.max, ["sa%d" % hf, "#%d" % (4 + hf)], ["sm%d" % hf])
+            mms(6, [(o, RED(2, m), T.sm[:, 64 * m:64 * m + 64]) for m in range(8 * hf, 8 * hf + 8)], ["big2", "sm%d" % hf], False, hf == 1)
+        scan(T.sq[:], T.rs[:], o, AL.add, AL.min, ["rs", "#6"], ["sq"])
         cp(T.q32[:, 0:4], T.sq[:, 15::16], ["sq"], ["q32"])
         ts(T.q33[:, 0:4], T.q32[:, 0:4], 1023, None, AL.bitwise_and, None, ["q32"], ["q33"])
         cp(T.qu[:, 0:4], T.q33[:, 0:4], ["q33"], ["qu"])
-        ts(T.fh[:, 64 * t:64 * t + 64], T.sa[:, 0:1024].indirect(T.qu[:, 0:4]), 0.5, None, AL.mult, None, ["sa0", "sa1", "qu"], ["fh%d" % t])
-        send((rank - 1 - t % (N - 1)) % N, T.lf[:, 64 * t:64 * t + 64], T.fh[:, 64 * t:64 * t + 64], "rep%d" % t, ["fh%d" % t])
-        arrives((rank + 1 + t % (N - 1)) % N, "rep%d" % t, "lf%d" % t)
+        ts(T.fh[:, 64 * t:64 * t + 64], T.sa[:, 0:1024].indirect(T.qu[:, 0:4]), 0.5, None, AL.mult, None, ["sa0", "sa1", "qu"], ["fh%d" % t], ind=GC)
+        d = 1 + t % (N - 1)
+        send((rank - d) % N, (rank + d) % N, T.lf[:, 64 * t:64 * t + 64], T.fh[:, 64 * t:64 * t + 64], "rep%d" % t, ["fh%d" % t], "lf%d" % t)
 
     def apply(t):
-        n1 = M + P * (t + 1)
-        tt(T.vv[:], T.lf[:, 64 * t:64 * t + 64].indirect(T.prm[:, 0:4]), T.pre[:], AL.add, ["lf%d" % t, "K3", "pre"], ["vv"])
-        tt(F[:, n1:n1 + FD + 64 - M - P].indirect(T.apu[:, 0:4]), T.vv[:], T.neg[:], AL.add, ["vv", "apu", "K3"], FALL)
+        tt(T.vv[:], T.lf[:, 64 * t:64 * t + 64].indirect(T.prm[:, 0:4]), T.pre[:], AL.add, ["lf%d" % t, "prm", "pre"], ["vv"], ind=GC)
+        tt(X[:, t + 1, :].indirect(T.psu[:, 0:4]), T.vv[:], T.neg[:], AL.add, ["vv", "psu", "neg"], ["X"], ind=SC)
 
-    consts_s()
-    first_k()
-    consts_s2()
-    col1(0)
-    col1_s(0)
-    x_psum(0)
-    gather_a("s", 0, 0, 64)
-    next_k(0)
-    col2_s(0)
-    col2_v(0)
-    gather_a("s", 0, 64, 256)
-    col2(0)
-    consts_b()
-    mark_w(0)
-    write_offsets(0)
-    sum_a(0, range(1, 16), 0, 256, True)
-    VR = range(1, 16 - NS)
+    ts(T.c0[:], T.pin[:, 1792:M], float(-CEN), None, AL.add, None, ["pinT"], ["c0"])
+    ts(T.lk[:], T.pin[:, 1792:M], float(-CEN), None, AL.add, None, ["pinT"], ["lk"])
+    mms(bK, [(PS[bK][:, 0:16], SEL(0, m), T.c0[:, m::16]) for m in range(16)], ["SEL", "c0"])
+    ts(T.ku[:, 0:16], PS[bK][:, 0:16], float(CEN), float(M), AL.add, AL.min, ["#%d" % bK], ["k1u"])
+    ts(T.r1n[:], T.iob[:], float(M), col("R1"), AL.add, AL.mult, ["iob", "R1"], ["r1n"])
+    ts(T.sc[:], T.pin[:, 1792:M], col("N1"), None, AL.mult, None, ["pinT", "N1"], ["sc"])
+    tt(T.pin[:, 1792:M], T.sc[:], T.r1n[:], AL.add, ["sc", "r1n"], ["pinT"], 2.0)
+    for k in range(4):
+        cp(A[:, 512 * k:512 * k + 512], T.pin[:, 512 * k:512 * k + 512], ["pin0", "pinT"], ["A_%d" % k])
+    prefetch(0)
+    cp(A[:, E:E + 1], col("CE"), ["CE"], ["A", "A2", "A_0", "A_1", "A_2", "A_3"])
     for t in range(NT):
-        last = t == NT - 1
-        n0 = M + P * t
-        if t > 0:
-            row1_gather(t)
-        gather_a("s", 1, 0, 128)
-        maxes(0, range(1 if t == 0 else 2, 8), 0, 256)
-        diff_x(t)
-        mms(1, [(PS[1][:, 0:256], MB("nblk2"), xblk(t))], ["K2"] + FALL, stop=False)
-        if t > 0:
-            row1_max(t)
-        maxes(0, range(8, 13), 0, 256)
-        sum_a(1, VR, 0, 128, False)
-        diff_a(t, 0, 128, False)
-        maxes(0, range(13, 16), 0, 256)
-        gather_a("s", 1, 128, 192)
-        decide1(t)
-        maxes(1, VR[:4], 0, 128)
-        gather_a("s", 1, 192, 256)
-        diff_a(t, 128, 192, False)
-        sum_a(1, VR, 128, 192, False)
-        maxes(1, VR[4:], 0, 128)
-        decide1_v(t)
-        diff_a(t, 192, 256, True)
-        for k in range(NS // 2):
-            diff_abs(t, k)
-        sum_a(1, VR, 192, 256, False)
-        maxes(1, VR[:3], 128, 256)
-        write1(t)
-        mms(1, [(PS[1][:, 0:256], MB("I256"), T.pen[:])], ["K2", "pen"], start=False, stop=False)
-        maxes(1, VR[3:6], 128, 256)
-        diff_sum(t, 0)
-        maxes(1, VR[6:-2], 128, 256)
-        diff_sum(t, 1)
-        maxes(1, VR[-2:-1], 128, 256)
-        maxes(1, VR[-1:], 128, 256, stop=True)
-        act(T.s[:, 256:512], PS[1][:, 0:256], AF.Sign, ["#1", "K2"], ["s2"], scale=-1.0, bias=cTH)
-        for bank in (7, 4):
-            mms(bank, [(PS[bank][:, 0:256], MB("In1"), T.n1[:])], ["K2", "n1"], stop=False)
-        o3 = PS[3][:, 0:256]
-        scatter(0)
-        mms(7, [(PS[7][:, 0:256], MB("LG"), T.s[:, 256:512])], ["K2", "s2"], start=False)
-        act(T.go[:], PS[7][:, 0:256], AF.Relu, ["#7"], ["go"], scale=2.0)
-        mms(4, [(PS[4][:, 0:256], MB("LY2"), T.s[:, 256:512])], ["K2", "s2"], start=False)
-        mms(3, [(o3, MB("LF"), T.ee[:, 256:512]), (o3, MB("I"), T.iob[:]), (o3, MB("nI"), T.go[:])], ["K", "K2", "e2", "go"])
-        if not last:
-            link_a(0, "b", 1, [])
-            scan(T.cum[:], T.one[:], T.go[:], AL.mult, AL.add, ["K", "go"], ["cum"])
-        tt(T.sel[:, 256:512], PS[4][:, 0:256], T.c16[:, 256:512], AL.min, ["#4", "h2"], ["sel2"])
-        act(T.tw[:, 256:512], o3, AF.Relu, ["#3"], ["tw2"], scale=-1.0, bias=float(E - n0 - 2 * B))
-        if not last:
-            link_b(0, "b", 1)
-        link_a(2, "a", 2, [] if last else [(PS[2][:, 0:256], MB("I1"), T.iob[:])])
-        link_b(2, "a", 2)
-        if last:
-            dma("sy", "st0", T.yx[:], F[:, M:E], FALL, [])
-            scatter(1)
-            new_rows(t)
-            break
-        counts(t)
-        scatter(1)
-        ms(A[:, E:E + 1], float(E), ["A"])
-        new_rows(t)
-        ask(t)
-        link_k(t)
-        col1(t + 1)
+        early(t)
+        distances(t)
+        choose(0)
+        per[0] += 1
         if t == 0:
-            consts_c()
-        col1_s(t + 1)
-        gather_a("s", 0, 0, G1)
-        next_k(t + 1)
-        serve_a(t)
-        serve_s(t)
-        serve_b(t)
-        col2_s(t + 1)
-        gather_a("s", 0, G1, 128)
-        col2_v(t + 1)
-        serve_c(t)
-        gather_a("s", 0, 128, GV)
-        col2(t + 1)
-        mark_w(t + 1)
-        ask_b(t)
-        row1_k(t + 1)
-        if GV < 256:
-            gather_a("v", 0, GV, 256)
-        sum_a(0, range(2, 16), 0, 128, True)
-        write_offsets(t + 1)
-        apply(t)
-        x_psum(t + 1)
-        sum_a(0, range(2, 16), 128, 256, False)
-    dma("sy", "st1", T.yp[:, 0:E // 2], A[:, 0:E // 2], ["A"], [])
-    dma("s", "st2", T.yp[:, E // 2:E], A[:, E // 2:E], ["A"], [])
-    need("sy", ("st0", 16))
-    need("sy", ("st1", 16))
-    need("sy", ("st2", 16))
+            consts_x()
+        decide(t)
+        if t < NT - 1:
+            ask(t)
+            prefetch(t + 1)
+            serve(t)
+            apply(t)
+    dma("sy", "st1", T.yp[:, 0:E // 2], A[:, 0:E // 2], ["A"], [], 851968)
+    dma("s", "st2", T.yp[:, E // 2:E], A[:, E // 2:E], ["A"], [], 851968)
+
+    cnt = {"v": 0, "s": 0, "pe": 0, "gc": 0}
+    seen = {q: {} for q in Q}
+
+    def need(q, sem, val):
+        if seen[q].get(sem, 0) < val:
+            Q[q].wait_ge(T.sem[sem], val)
+            seen[q][sem] = val
+
+    for j in issue_order(nodes):
+        nd = nodes[j]
+        best = {}
+        for i, sync in nd["pre"].items():
+            if sync:
+                sem, val = nodes[i]["ev"]
+                best[sem] = max(best.get(sem, 0), val)
+        for sem in best:
+            need(nd["q"], sem, best[sem])
+        ins = nd["fn"]()
+        if nd["ev"] is None:
+            cnt[nd["q"]] += 1
+            nd["ev"] = (nd["q"], cnt[nd["q"]])
+            ins.then_inc(T.sem[nd["q"]], 1)
+        elif nd["dma"]:
+            ins.then_inc(T.sem[nd["ev"][0]], 16)
+    for k in range(3):
+        need("sy", "st%d" % k, 16)
     g.wait_ge(T.sem.sent, sent[0])
     for q in cnt:
-        need("sy", (q, cnt[q]))
+        need("sy", q, cnt[q])

@@ -5,52 +5,48 @@ E = M + NT * P
 CEN = 1792
 AD = 3336
 LINK = -49920.0
-XB = True
-GAT = [("s", 0, 0, 32), ("s", 0, 32, 96), ("s", 0, 96, 160), ("s", 0, 160, 192), ("v", 0, 192, 224), ("v", 0, 224, 256), ("s", 1, 0, 64),
-       ("s", 1, 64, 128), ("s", 1, 128, 160), ("s", 1, 160, 192), ("s", 1, 192, 224), ("v", 1, 224, 256)]
-GAT0 = [("s", 0, 0, 64), ("s", 0, 64, 128), ("v", 0, 128, 192), ("s", 0, 192, 256), ("s", 1, 0, 64), ("s", 1, 64, 128),
-        ("s", 1, 128, 192), ("v", 1, 192, 256)]
+GAT = ("s32 s64 s64 s32 v16 v16 v16 v16", "v16 v16 s32 s64 s32 s32 s32 s32")
+GAT0 = ("s64 v32 v32 s64 v32 v32", "s32 s32 s32 v32 s32 s32 s32 s32")
 MC = ((0, 128), (128, 256))
-SCH = ((0, 64), (64, 128), (128, 192), (192, 256))
-SA = "s"
-CYC, GC, SC, HOP, REM = 0.00091, 1.5, 3.0, 0.11, 2.0
+NCV = 8
+CYC, GC, SC = 0.00091, 1.5, 3.0
 ORDER = {
-    0: "00070i0n0o0k0p0809010q0j022q0z0a0u0w1a1719180m1t2n100t1l233c110v1d2h390x0r381f1n0b1413272r2s03242u29281y2v151v1x1w1m2d2a2y2b2e2z2f162c2t1z312g0d3a3d0y1h332i3e1q3b1i1j1o0c0e040f050h0g0634352x30323j3o3p1c3f3w1g3k1p3l3q3m413y2o4x3g1b3n3z1u1k3x3v3r444f454q5051534j474g464k3s5557595b2j5d1s4043424b5f5h2l4y3t4z4r565c54584l485a365k5m4o5j5o5q1e493h3i5s5p5g5u5w62696b6d5r4v4i5l4s5e5i4m5t525v6c665n4t6f6h2m2p1r6j126l4a6n4c6p2k6r6t6v0l0s6x6z714d3u76785x6i6a60614h6s20214w5y7a4p4e257c7e7g7i5z7k7m6e6m634n737o7q7s7u7w6w836y72817y842685827f70676u7d7n64772w6k7h7l6g6o657v7p7x7j757t796q687r747b7z4u223780",
-    1: "0e0h090208000a030b06040f0g0q0j0k0i0r0n0s0o0v0w0x0y0l0z0m100c0t0p13110d050u0701181a1914151d12161c171s2d1m2e1l1n1p2g2f1z2h2i202j1o1v2n2k212l2m222p2o2q2r242s1t2t1k1b1e2u2v1f1i2w2x2y23281u1q271w341r1j1x292z30311y393d3f3h3j3l3n1h3a262a322c37334c3p3r3t3w3y4042443b461g484e4l4n4p4r4t4v4x4z51535557595b5d5i5k5m5o5q5s5u5w5y6062646668254i3c3i3g3v3o3e3k3u3s3z3x3q41453m47434m494a2b4w586d506f545l4u4q5a5z4f5n4b5c4d5f565g4g4h634o5v65695x615t4y4j5r5h4s4k5j52675e5p386a6g6e6h6b356c36",
-    2: "0005030c010d06020409070i0j0k0h0e0a0b080l0m0f0n0p0o0q161b1p1z22232425260g0u0v0x280w2021290r270s2c2e0t102a1e2b2d2f1f1g2g182o2p2h172i192j1l2k1t1h0y0z1d2l111a2m1m2n1n2v1o2z1q2q2r1v31333537393b3d3f1u2w2x3i3k3m3o3q3s3u4013124749144b4d4f4h4j1c153y2y1w303h38343z363g3c323l3p3r3n3t3a484c3e4e414k4i3j4g4a3v1i1x3w4l4n1j4p4r4t4v1k4x4z5456585a5c5e45611y3x4s511s4q4y1r5g5i5k5m5o5q5s625u2u42554u524w5z43595j5r5t5d4m445l5b5h4o505n465p575v535f5w5x60632t2s5y",
-    5: "02000305010406070809",
+    0: "0103003g9o0k0j0g020m0l0n040c0805070d2u0s0o0i9v2a279t9q130t110q9x100f0z14122n0u1d2c2i289u152t9w2s171y1f2b1s342l29202j369s2g1r221q1w2e2m2f1m232o1k2p191p9y0r0h9p0p2v2w312x2y2z30161u1i1c1t1l1g211a180x0w1e1o1j2d0v0y1x1h1b321v9z3y3q0e0a0b06463z4m4h455d5f4041335l2637354j3k3n3h424k483a383c3e3b393d4p4r5e4q51433f4l4i44475n5m4b496e626c64726u5y5q606k6i6y6g7c665s6a687e4w7g5u6m6s527m5350554s547s5o577n58736d5z6h6f5p6j615t6367696b7d7f656z6l5v3i789r74707a3j4a2h1n4e762q6q6o5w09757b242r6w4n716n776v796p6r6x5x6t5ra57h4t594c4x3o4o9m8o86848a7o8i808m827w888g8k8e8c7y3u4y3v5a4d9na67i8p8j7p8b854z4u3s87818h8n837x8f8d5b7j3w4v3x7k3t3r898la77za85g5j5i4f4g909c9a92949g8u963l8y9e988q9l8s9i8w56a0a15ha3a2957t93919b8va92k253p7l1z998z7q9h9f8r9d8t8x973m5k5ca49j7r9k7uaa7v",
+    2: "0001020j0h0g0i030b040c2g08060507090d0k0a0e0f0m0l0n0p0q0z0y101u1t1v2b27261w0r2c1a2d282x290s2e0o1c0w0u2f2z1i2a2j2h2i0v0x2k2l2m1x1d0t1e2n1b2o1h1y201k2p2r2q2s1f1j1l152t1g1m2y112u1n1p12132v2w1o35213017161918363a3g3o3k403u3i423w3q3c3m313223334g1z6e4a38243b3j3h433l3x3r413p3d3v3n143e5m5o5y3y3s44605s1q5e5u5k525c5q541r625a4o644u5g665i4s4w3f253z393t456f46375z5n615f5p225d47634v5t4p6g5j5r4x5b4b484c4y4m5w5056584q1s4k49696a5v5h65554h4d6h514e4l534r5l5x4n4z594t576c4f6i6b6d674i4j6j6834",
+    5: "000105030402080906070a",
 }
 f32, bf, f16, i32, u16 = "float32", "bfloat16", "float16", "int32", "uint16"
 
 SB = {
-    "A": ([AD + 512], f32), "F": ([E + 32], bf), "X": ([NT, 320], bf), "lk": ([256], f32), "pin": ([M + 8], i32), "thw": ([8], i32),
+    "A": ([AD + 520], f32), "F": ([E + 32], bf), "X": ([NT, 320], bf), "lk": ([256], f32), "pin": ([M + 8], i32), "thw": ([8], i32),
     "a0": ([4096], bf), "a1": ([4096], bf), "m0": ([4096], bf), "m1": ([4096], bf),
     "xo": ([512], bf), "cs": ([256], f16), "cu": ([512], u16), "c16": ([512], f16),
-    "ge": ([512], f16), "e12": ([256], f16), "em": ([256], f16), "hi": ([256], bf), "s": ([768], bf), "so1": ([256], bf),
-    "go": ([320], bf), "sel": ([512], f16), "nc": ([512], f32), "cum": ([320], bf),
-    "jk": ([4, 320], bf), "acc": ([8], f32), "psu": ([8], u16), "sc": ([256], f32), "kk": ([32], i32), "ku": ([32], u16), "pm": ([32], i32),
+    "ge": ([512], bf), "e12": ([256], bf), "em": ([256], bf), "hi": ([256], bf), "s": ([768], bf), "sT": ([256], bf), "so1": ([256], bf),
+    "go": ([320], bf), "sel": ([512], f16), "nc": ([512], f32), "cum": ([320], bf), "one": ([256], bf),
+    "jk": ([4, 320], bf), "acc": ([8], f32), "psu": ([8], u16), "kk": ([32], i32), "ku": ([32], u16), "pm": ([32], i32),
     "pu": ([32], u16), "own": ([32], f32), "so": ([32], f32), "sou": ([32], u16),
-    "xs": ([256], bf), "lx": ([256], bf), "fh": ([256], bf), "lf": ([256], bf), "pre": ([64], f32), "vv": ([64], bf),
-    "q32": ([8], i32), "q33": ([8], i32), "qu": ([8], u16), "cq": ([64], u16), "sa": ([1024], bf), "sm": ([1024], bf),
-    "sq": ([64], f32), "pi": ([8], i32), "col": ([48], f32), "U": ([144], bf), "t0": ([144], bf), "t1": ([128], bf),
-    "bb": ([144], bf), "big": ([4, 144], bf), "bigh": ([2, 144], f16), "mb": ([36, 128], bf), "mh": ([16, 128], f16),
-    "iob": ([256], bf), "iox": ([256], bf), "r1n": ([256], f32), "dh": ([64], f32), "rs": ([64], f32), "t64": ([64], f32),
+    "xs": ([512], f16), "lx": ([512], f16), "hq": ([256], bf), "qa": ([320], f32), "wl": ([12], i32),
+    "fh": ([256], bf), "lf": ([256], bf), "pre": ([64], f32), "vv": ([64], bf),
+    "q32": ([8], i32), "qv": ([8], u16), "qu": ([8], u16), "cq": ([64], u16), "sa": ([1024], bf), "sm": ([1024], bf),
+    "sq": ([64], f32), "pi": ([8], i32), "col": ([56], f32), "U": ([144], bf), "t0": ([144], bf), "t1": ([128], bf),
+    "bb": ([144], bf), "big": ([4, 144], bf), "selm": ([144], bf), "mb": ([44, 128], bf), "r1i": ([256], i32), "lt": ([128], bf), "ld": ([128], bf),
+    "iob": ([256], bf), "iox": ([256], bf), "dh": ([64], f32), "rs": ([64], f32), "t64": ([64], f32),
     "kc": ([64], f16), "neg": ([64], bf), "ioo": ([32], f32), "dum": ([32], f32), "dj": ([4], f32), "thr": ([4], f32),
     "c0": ([256], f16), "prm": ([8], u16), "prf": ([8], f32), "i64": ([64], f32),
 }
 SCRATCH = {k: ("sbuf", [128] + v[0], v[1]) for k, v in SB.items()}
 for _b in range(8):
-    SCRATCH["p%d" % _b] = ("psum", [128, 1024], bf) if XB and _b == 3 else ("psum", [128, 512], f32)
-SEMAPHORES = (["v", "s", "pe", "gc", "sent"] + ["ld%d" % k for k in range(8)] + ["st%d" % k for k in range(3)]
-              + [nm + str(t) for nm in ("fc", "req", "rep") for t in range(4)])
+    SCRATCH["p%d" % _b] = ("psum", [128, 64, 16], bf) if _b in (3, 5) else ("psum", [128, 512], f32)
+SEMAPHORES = (["v", "s", "pe", "gc", "sent", "wx0", "wx1", "wx2"] + ["ld%d" % k for k in range(8)]
+              + [nm + str(t) for nm in ("st", "fc", "req", "rep") for t in range(4)])
 
 
 def issue_order(nodes):
     seq = []
     for p in range(NT + 1):
         ids = [j for j, nd in enumerate(nodes) if nd["per"] == p]
-        o = ORDER[p if p in ORDER else 2]
-        seq += [ids[int(o[k:k + 2], 36)] for k in range(0, len(o), 2)]
+        o = ORDER[p if p in (0, NT) else 2]
+        seq += [ids[j] for j in [int(o[k:k + 2], 36) for k in range(0, len(o), 2)] if j < len(ids)]
     return seq
 
 
@@ -64,7 +60,7 @@ def rank_program(g, core, T, topo):
     V, S = g.vector, g.scalar
     nodes, lastw, readers, per = [], {}, {}, [0]
 
-    def node(q, fn, rd, wr, cost, lat=HOP, dma=0.0, ev=None, kind=0):
+    def node(q, fn, rd, wr, cost, dma=0.0, ev=None, kind=0):
         pre = {}
         for r in list(rd) + list(wr):
             for i in ([lastw[r]] if r in lastw else []) + (readers.get(r, []) if r in wr else []):
@@ -84,20 +80,20 @@ def rank_program(g, core, T, topo):
         return n
 
     def op(q, fn, rd, wr, n, ind=0.0):
-        node(q, fn, [r for r in rd if r[0] != "#"], list(wr) + [r for r in rd if r[0] == "#"],
+        node(q, fn, [r.replace("@", "#") for r in rd if r[0] != "#"], list(wr) + [r for r in rd if r[0] == "#"],
              0.06 + n * ind * CYC if ind else max(n, 64) * CYC, kind=1 if ind == GC else 2 if ind else 0)
 
-    def mms(bank, items, rd, start=True, stop=True, each=False, wr=()):
+    def mms(bank, items, rd, start=True, stop=True):
         def fn():
             for k, (o, l, r) in enumerate(items):
-                ins = g.tensor.matmul(o, l, r, each or (start and k == 0), each or (stop and k == len(items) - 1))
+                ins = g.tensor.matmul(o, l, r, start and k == 0, stop and k == len(items) - 1)
             return ins
         b = ["#%d" % bank]
         mid = not (start or stop)
-        node("pe", fn, list(rd) + (b if mid else []), ([] if mid else b) + list(wr), sum(max(64, width(r)) for _, _, r in items) * CYC / 2)
+        node("pe", fn, list(rd) + (b if mid else []), [] if mid else b, sum(max(64, width(r)) for _, _, r in items) * CYC / 2)
 
     def dma(q, sem, out, in_, rd, wr, nbytes):
-        node(q, lambda: Q[q].dma_start(out, in_), rd, wr + ["#q" + q], 0.05, 0.0, nbytes / 4e5 + 0.1, (sem, 16))
+        node(q, lambda: Q[q].dma_start(out, in_), rd, wr + ["#q" + q], 0.05, nbytes / 4e5 + 0.1, (sem, 16))
 
     sent = [0]
 
@@ -105,7 +101,7 @@ def rank_program(g, core, T, topo):
         dst = T.cores[dst_rank]
         rid, pid = topo.addr(dst)[:2]
         sent[0] += len(topo.engines(core, dst))
-        node("gc", lambda: g.remote_dma(out, in_, T.sem[sem], T.sem.sent, pid, rid, topo.mask(core, dst)), rd, [name], 0.3, REM, 0.0,
+        node("gc", lambda: g.remote_dma(out, in_, T.sem[sem], T.sem.sent, pid, rid, topo.mask(core, dst)), rd, [name], 0.3, 0.0,
              (sem, len(topo.engines(T.cores[src_rank], core))), 3)
 
     def ts(out, in0, s1, s2, o0, o1, rd, wr, per=1.0, ind=0.0, n=None):
@@ -134,7 +130,7 @@ def rank_program(g, core, T, topo):
         if flag:
             op("gc", lambda: g.iota(out, pat, base, cm, allow_small_or_imprecise_dtypes=True), [], wr, 150 + 2 * width(out))
         else:
-            op("gc", lambda: g.iota(out, pat, base, cm), [], wr, 150)
+            op("gc", lambda: g.iota(out, pat, base, cm), [], wr, 150 + 2 * width(out))
 
     def aff(q, out, a, scale, bias, rd, wr, per=1.0):
         if q == "v":
@@ -144,16 +140,12 @@ def rank_program(g, core, T, topo):
 
     PS = [T["p%d" % b] for b in range(8)]
     A, F, X = T.A, T.F, T.X
-    Aw, Fw = A[:, 0:AD + 512], F[:, 0:E + 32]
+    Aw, Fw = A[:, 0:AD + 520], F[:, 0:E + 32]
     U = T.U[:, 0:128]
 
+    ms(T.one[:], 1.0, ["one"], 128)
     dma("sy", "ld0", T.pin[:, 1792:M], T.ptr[:, 1792:M], [], ["pinT"], 131072)
-    dma("sy", "ld5", T.thw[:, 0:1], T.th[:], [], ["th"], 30000)
     dma("sy", "ld1", T.pin[:, 0:1792], T.ptr[:, 0:1792], [], ["pin0"], 917504)
-    dma("sy", "ld3", F[:, 16:16 + M], T.fr[:], [], ["F0"], 524288)
-    dma("sy", "ld4", X[:, 0, 0:P], T.nw[:, 0:P], [], ["X0"], 65536)
-    dma("sy", "ld7", X[:, 1:NT, 0:P], T.nw[:, P:NT * P], [], ["X2"], 262144)
-    dma("sy", "ld6", T.thw[:, 4:5], T.hw[:], [], ["hw"], 30000)
 
     cols, mats = {}, {}
 
@@ -161,10 +153,10 @@ def rank_program(g, core, T, topo):
         cols.setdefault(nm, len(cols))
         return T.col[:, cols[nm]:cols[nm] + 1]
 
-    def mat(nm, h=False):
+    def mat(nm):
         if nm not in mats:
-            mats[nm] = (T.mh if h else T.mb)[:, sum(1 for v in mats.values() if v[1] == h), :], h
-        return mats[nm][0]
+            mats[nm] = T.mb[:, len(mats), :]
+        return mats[nm]
 
     def cmp(nm, src, val, o, mul=None):
         if mul is None:
@@ -175,11 +167,11 @@ def rank_program(g, core, T, topo):
     def lin(nm, src, mul, add, q="v"):
         aff(q, col(nm), col(src), col(mul) if mul in cols else mul, col(add) if add in cols else add, [src] + [z for z in (mul, add) if z in cols], [nm])
 
-    def sc(nm, base, w, q="s", h=False):
-        aff("v" if h else q, mat(nm, h), mat(base), col(w) if w in cols else w, 0.0, [base] + ([w] if w in cols else []), [nm], 0.5)
+    def sc(nm, base, w):
+        aff("s", mat(nm), mat(base), col(w) if w in cols else w, 0.0, [base] + ([w] if w in cols else []), [nm])
 
-    def add(nm, a, b, o=AL.add, h=False):
-        tt(mat(nm, h), mat(a), mat(b), o, [a, b], [nm], 2.0)
+    def add(nm, a, b, o=AL.add):
+        tt(mat(nm), mat(a), mat(b), o, [a, b], [nm])
 
     iota(T.pi[:, 0:1], [[0, 1]], 1, ["pi0"], False)
     iota(T.t0[:], [[1, 144]], 0, ["t0"])
@@ -192,7 +184,7 @@ def rank_program(g, core, T, topo):
     iota(T.i64[:], [[1, 64]], 0, ["i64"])
     iota(T.prf[:, 0:4], [[4, 4]], 0, ["prf"])
     iota(T.neg[:], [[0, 64]], 0, ["neg"], base=-192)
-    ms(F[:, 16 + M:E + 32], 99.0, ["F2"], 650)
+    iota(F[:, 16 + M:E + 32], [[0, E + 16 - M]], 0, ["F2"], base=99)
     ms(T.go[:, P:320], 1.0, ["go1"])
     ms(F[:, 0:16], 99.0, ["F1"])
     ms(X[:, :, P:320], 0.0, ["X1"], 160)
@@ -201,18 +193,14 @@ def rank_program(g, core, T, topo):
     ts(T.pi[:, 2:3], T.pi[:, 0:1], 15, None, AL.bitwise_and, None, ["pi0"], ["pi2"])
     cp(col("G"), T.pi[:, 1:2], ["pi1"], ["G"])
     cp(col("R"), T.pi[:, 2:3], ["pi2"], ["R"])
-    cp(col("TH"), T.thw[:, 0:1], ["th"], ["TH"])
-    cp(col("W"), T.thw[:, 4:5], ["hw"], ["W"])
     cmp("R0", "R", 0.0, AL.is_equal)
     cmp("R1", "R", 1.0, AL.is_equal)
-    cmp("N1", "R", 1.0, AL.not_equal)
     cmp("LFc", "R", 1.5, AL.is_gt, -8192.0)
     lin("CE", "R1", float(-1 - E), float(E))
     cp(T.pin[:, M:M + 1], col("CE"), ["CE"], ["pinE"])
     ts(T.U[:], T.t0[:], col("G"), None, AL.subtract, None, ["t0", "G"], ["U"], 0.5)
     ts(T.bb[:], T.U[:], 15.0, None, AL.is_equal, None, ["U"], ["bb"], 0.5)
-    ts(T.bigh[:, 0, :], T.bb[:], col("R0"), None, AL.mult, None, ["bb", "R0"], ["SEL"], 0.5)
-    ts(T.bigh[:, 1, :], T.bb[:], -1.0, None, AL.mult, None, ["bb"], ["NRED"], 0.5)
+    ts(T.selm[:], T.bb[:], col("R0"), None, AL.mult, None, ["bb", "R0"], ["SEL"], 0.5)
     for k, w in enumerate((2.0, -1.0, 2048.0, -1024.0)):
         aff("s", T.big[:, k, :], T.bb[:], w, 0.0, ["bb"], ["big%d" % k])
     ts(mat("inb"), T.t1[:], col("G"), None, AL.is_equal, None, ["t1", "G"], ["inb"], 0.5)
@@ -224,23 +212,19 @@ def rank_program(g, core, T, topo):
     add("gt", "gU", "inb", AL.mult)
     add("PEN", "g2", "inb", AL.mult)
     add("t3", "I", "gt", AL.subtract)
-    sc("LF", "t3", "LFc", h=True)
-    sc("b0", "inb", "R0", h=True)
-    sc("b0p", "b0", 4096.0, h=True)
-    sc("b0e", "b0", -32768.0, h=True)
-    sc("b0n", "b0", -4096.0, h=True)
+    sc("LF", "t3", "LFc")
+    sc("b0", "inb", "R0")
+    sc("b0p", "b0", 4096.0)
+    sc("b0e", "b0", -32768.0)
+    sc("b0n", "b0", -4096.0)
     lin("n256", "R0", -256.0, 0.0, "s")
     sc("b0h", "inb", "n256")
-    lin("cB", "R1", -1.0, 0.0)
-    ts(col("cA"), col("TH"), 1024.0, col("cB"), AL.add, AL.mult, ["TH", "cB"], ["cA"])
-    sc("R1m", "z0", "cA", h=True)
-    sc("In", "I", -1024.0, h=True)
-    sc("Ip", "I", 1024.0, h=True)
-    sc("nI16", "I", -1.0, h=True)
-    sc("nz16", "z0", -1.0, h=True)
-    sc("I16", "I", 1.0, h=True)
-    for nm, base, w in (("nblk", "inb", -1.0), ("inb2", "inb", 2.0), ("H", "inb", 2048.0), ("ZS", "z0", -1024.0), ("Inb", "I", -1024.0),
-                        ("LY", "t3", 2048.0), ("y1x", "p01", 4096.0), ("nI", "I", -1.0)):
+    lin("cA", "R1", -1024.0, 0.0, "s")
+    sc("R1m", "z0", "cA")
+    sc("Ip", "I", 1024.0)
+    sc("nz", "z0", -1.0)
+    for nm, base, w in (("nblk", "inb", -1.0), ("inb2", "inb", 2.0), ("H", "inb", 2048.0), ("ZS", "z0", -1024.0), ("In2", "I", -2048.0),
+                        ("Inb", "I", -1024.0), ("LY", "t3", 2048.0), ("y1x", "p01", 4096.0), ("nI", "I", -1.0)):
         sc(nm, base, w)
     lin("y2c", "R0", -2048.0, -2048.0, "s")
     sc("y2x", "z0", "y2c")
@@ -250,18 +234,26 @@ def rank_program(g, core, T, topo):
         lin("mv%d" % t, "R1", float(256 * (t + 1) + 10 * 4096), "R0", "s")
         sc("MT%d" % t, "inb", "mv%d" % t)
     ts(T.iox[:], T.iob[:], col("R0"), col("R1"), AL.mult, AL.add, ["iob", "R0", "R1"], ["iox"], 0.5)
-    lin("N0", "R0", -1.0, 1.0)
-    ts(col("TN"), col("TH"), 0.5, col("N0"), AL.add, AL.mult, ["TH", "N0"], ["TN"])
-    lin("T1", "R0", -1023.5, "TN")
-    lin("T2a", "R0", 15000.0, 1024.0)
-    lin("T2", "TN", 1.0, "T2a")
-    lin("Twa", "LFc", 1.0, -1024.0)
-    lin("Twb", "R0", -100000.0, "Twa")
-    lin("Tw", "TN", 1.0, "Twb")
+
+    def consts_t():
+        cp(col("TH"), T.thw[:, 0:1], ["th"], ["TH"])
+        lin("N0", "R0", 1.0, -1.0, "s")
+        lin("TN", "TH", "N0", 0.0)
+        lin("nR1", "R1", -1.0, 0.0, "s")
+        lin("TA", "TH", "nR1", 0.0)
+        for b, w in enumerate((1024.0, -15104.0, 32768.0)):
+            lin("T%d" % b, "R0", w, "TN", "s")
+            sc("TD%d" % b if b else "TDa", "I", "T%d" % b)
+        sc("TZ", "z0", "TA")
+        add("TD0", "TDa", "TZ")
+
     lin("cy", "R", -2048.0, -512.0, "s")
     lin("cy1a", "R1", 4096.0, "cy", "s")
     lin("cy1", "R0", -100000.0, "cy1a", "s")
-    lin("cy2", "R0", 1536.0 - 32768.0 + 512.0, "cy", "s")
+    lin("cyb", "R", -4096.0, 1536.0, "s")
+    lin("cy2", "R0", -65536.0, "cyb", "s")
+    lin("hs", "R0", -32768.0, 2048.0, "s")
+    sc("Hs", "inb", "hs")
     for h in "12":
         lin("n" + h, "cy" + h, -1.0, 0.0, "s")
         lin("a" + h, "cy" + h, 1.0, -1664.0, "s")
@@ -276,13 +268,13 @@ def rank_program(g, core, T, topo):
 
     def consts_x():
         ts(T.t64[:], T.t64[:], col("R"), None, AL.is_equal, None, ["t64", "R"], ["t64"])
-        aff("s", T.dh[:], T.t64[:], float(2 ** 21 + 65536), -65536.0, ["t64"], ["dh"])
+        aff("s", T.dh[:], T.t64[:], float(2 ** 20 + 4096), -4096.0, ["t64"], ["dh"])
         ms(T.rs[:], 0.0, ["rs"])
         ms(T.rs[:, 0::16], float(2 ** 22), ["rs"])
         lin("R64", "R", 64.0, 0.0, "s")
         ts(T.kc[:], T.i64[:], col("R64"), None, AL.add, None, ["i64", "R64"], ["kc"])
         lin("MX", "R0", float(E), 0.0, "s")
-        sc("Wm", "inb", "W")
+        lin("QO", "R", -4096.0, 61440.0, "s")
         ts(T.pi[:, 3:4], T.pi[:, 2:3], 3, None, AL.bitwise_and, None, ["pi2"], ["pi3"])
         ts(T.pi[:, 4:5], T.pi[:, 2:3], 2, None, AL.logical_shift_right, None, ["pi2"], ["pi4"])
         cp(col("m4"), T.pi[:, 3:4], ["pi3"], ["m4"])
@@ -290,23 +282,30 @@ def rank_program(g, core, T, topo):
         lin("pr", "m4", 16.0, "d4")
         ts(T.prm[:, 0:4], T.prf[:, 0:4], col("pr"), None, AL.add, None, ["prf", "pr"], ["prm"])
 
-    def SEL(r, m):
-        return T.bigh[:, r, 15 - m:143 - m]
+    def SEL(m):
+        return T.selm[:, 15 - m:143 - m]
 
     def RED(k, i):
         return T.big[:, k, 15 - i:143 - i]
 
-    def mm(bank, nm, rhs, rd, start=False, stop=False):
-        mms(bank, [(PS[bank][:, 0:256], mat(nm), rhs)], [nm] + rd, start, stop)
+    def mm(bank, nm, rhs, rd, start=False, stop=False, at=0):
+        mms(bank, [(PS[bank][:, at:at + 256], mat(nm), rhs)], [nm] + rd, start, stop)
+
+    def mt(bank, nm, tile, rd, start=False, stop=False, i=None, hs=(0, 1)):
+        mms(bank, [(PS[bank][:, 128 * u:128 * u + 128] if i is None else PS[bank][:, 128 * u + i:128 * u + 128:16], tile(u),
+                    mat(nm) if i is None else mat(nm)[:, 0::16]) for u in hs], [nm] + rd, start, stop)
+
+    def hv(a):
+        return lambda u: a[:, 128 * u:128 * u + 128]
 
     AB, MX = (T.a0, T.a1), (T.m0, T.m1)
-    bK, bY1, bV1, bY2, bV2, bGO, bLO, bLA = 7, 7, 4, 5, 6, 0, 2, 1
+    bK, bY, bGO, bLO, bLA = 7, (4, 7), 0, 2, 1
     H = [slice(0, 256), slice(256, 512)]
     c16, ge, s = [T.c16[:, h] for h in H], [T.ge[:, h] for h in H], [T.s[:, h] for h in H]
     sw = T.s[:, 512:768]
 
     def blocks(h, lo, hi):
-        return ["a%d_%d" % (h, k) for k in range(lo // 32, hi // 32)]
+        return ["a%d_%d" % (h, k) for k in range(lo // 16, hi // 16)]
 
     def arow(h, i, lo, hi):
         return AB[h][:, 16 * lo + i:16 * hi:16]
@@ -317,15 +316,19 @@ def rank_program(g, core, T, topo):
         FR = ["F", "F0", "F1", "F2"]
         ts(T.cu[:, H[0]], win.indirect(T.ku[:, 0:16]), 16.0, None, AL.add, None, wn + ["k1u"], ["cu0"], ind=GC)
         ts(c16[0], T.cu[:, H[0]], float(-CEN - 16), None, AL.add, None, ["cu0"], ["h1"], 0.5)
-        mms(bK, [(PS[bK][:, 0:16], SEL(0, m), T.c16[:, m:256:16]) for m in range(16)], ["SEL", "h1"])
+        mms(bK, [(PS[bK][:, 0:16], SEL(m), T.c16[:, m:256:16]) for m in range(16)], ["SEL", "h1"])
         ts(T.ku[:, 16:32], PS[bK][:, 0:16], float(CEN), top, AL.add, AL.min, ["#%d" % bK], ["k2u"])
         ts(T.cu[:, H[1]], win.indirect(T.ku[:, 16:32]), 16.0, None, AL.add, None, wn + ["k2u"], ["cu1"], ind=GC)
-        for q, h, lo, hi in (GAT0 if t == 0 else GAT):
-            out, src = AB[h][:, 16 * lo:16 * hi], Fw.indirect(T.cu[:, 256 * h + lo:256 * h + hi])
-            if q == "s":
-                act(out, src, AF.Copy, FR + ["cu%d" % h], blocks(h, lo, hi), GC)
-            else:
-                cp(out, src, FR + ["cu%d" % h], blocks(h, lo, hi), ind=GC)
+        for h in range(2):
+            lo = 0
+            for w in (GAT if t else GAT0)[h].split():
+                hi = lo + int(w[1:])
+                out, src = AB[h][:, 16 * lo:16 * hi], Fw.indirect(T.cu[:, 256 * h + lo:256 * h + hi])
+                if w[0] == "s":
+                    act(out, src, AF.Copy, FR + ["cu%d" % h], blocks(h, lo, hi), GC)
+                else:
+                    cp(out, src, FR + ["cu%d" % h], blocks(h, lo, hi), ind=GC)
+                lo = hi
         for h in range(2):
             ts(ge[h], T.cu[:, H[h]], float(n0 + 16), None, AL.is_ge, None, ["cu%d" % h], ["ge%d" % h], 0.5)
         cp(T.kk[:], T.ku[:], ["k1u", "k2u"], ["kk"])
@@ -344,22 +347,26 @@ def rank_program(g, core, T, topo):
         tt(T.own[:], T.pm[:], T.ioo[:], AL.not_equal, ["pm", "ioo"], ["own"])
         tt(T.own[:], T.own[:], T.dum[:], AL.mult, ["own", "dum0", "dum1"], ["own"])
         tt(T.so[:], T.own[:], T.kk[:], AL.max, ["own", "kk"], ["so"])
-        cp(T.sou[:], T.so[:], ["so"], ["sou"])
-        mm(0, "R1m", ge[0], ["ge0"], True)
-        mm(2, "In", ge[1], ["ge1"], True)
+        ts(T.sou[:], T.so[:], 1.00016, None, AL.mult, None, ["so"], ["sou"])
+        mt(0, "TD0", hv(T.one), ["one"], True)
+        for b in (1, 2):
+            mm(b, "TD%d" % b, T.one[:], ["one"], True)
+        mm(2, "PEN", T.one[:], ["one"])
+        mt(0, "R1m", hv(ge[0]), ["ge0"])
+        mm(2, "Inb", ge[1], ["ge1"])
         mm(2, "Ip", T.em[:], ["em"])
-        mm(bY1, "nI16", c16[0], ["h1"], True)
-        for h in range(2):
-            for lo, hi in (SCH if h else ((0, 128), (128, 256))):
-                mms(h, [(PS[h][:, lo:hi], RED(1, i), arow(h, i, lo, hi)) for i in range(1, 16)],
-                    ["big1"] + blocks(h, lo, hi), h == 1 and lo == 0, False, wr=["#d%d" % lo] * h)
+        for u in range(2):
+            mms(0, [(PS[0][:, 128 * u + i:128 * u + 128:16], arow(0, i, 128 * u, 128 * u + 128), mat("nblk")[:, 0::16]) for i in range(1, 16)],
+                ["nblk"] + blocks(0, 128 * u, 128 * u + 128), False, False)
+        for lo in range(0, 256, 64):
+            mms(1, [(PS[1][:, lo:lo + 64], RED(1, i), arow(1, i, lo, lo + 64)) for i in range(1, 16)], ["big1"] + blocks(1, lo, lo + 64), False, False)
 
     def early(t):
-        for h, b in enumerate((bV1, bV2)):
-            mm(b, "MT%d" % t, T.iox[:], ["iox"], True)
-            mm(b, "LF", ge[h], ["ge%d" % h])
-        mm(bV2, "b0n", T.e12[:], ["e12"])
-        mm(bY2, "nI16", c16[1], ["h2"], True)
+        for h, b in enumerate(bY):
+            mm(b, "nI", c16[h], ["h%d" % (h + 1)], True)
+            mm(b, "MT%d" % t, T.iox[:], ["iox"], at=256)
+            mm(b, "LF", ge[h], ["ge%d" % h], at=256)
+        mm(bY[1], "b0n", T.e12[:], ["e12"], at=256)
 
     def distances(t):
         n0 = M + P * t
@@ -368,69 +375,76 @@ def rank_program(g, core, T, topo):
             dma("sy", "fc%d" % t, F[:, 16 + n0:16 + n0 + P], x, FR, ["F"], 65536)
         else:
             dma("sy", "st0", T.yx[:], X[:, :, 0:P], ["X", "X0", "X2"], [], 327680)
-        xp = PS[3][:, 0:256]
-        if XB:
-            cp(xp, x, FR, ["#3", "xp"], 0.5)
-        else:
-            mm(3, "I", x, FR, True, True)
+        cp(PS[3][:, 0:16, :], x, FR, ["#3", "xp"], 0.5)
         for h in range(2):
             act(T.xo[:, H[h]], x.indirect(T.pu[:, 16 * h:16 * h + 16]), AF.Copy, FR + ["pu"], ["xo%d" % h], GC)
 
         def mx(h, i, lo, hi, src, rd):
             o = MX[h][:, 256 * i + lo:256 * i + hi]
-            tt(o, src, xp[:, lo:hi], AL.max, rd + ["#3", "xp"], ["m%d_%d_%d" % (h, i, lo)], 0.5 if XB else 1.0)
-            return o, ["m%d_%d_%d" % (h, i, lo)]
+            tt(o, src, PS[3][:, lo // 16:hi // 16, :], AL.max, rd + ["@3", "xp"], ["m%d_%d_%d" % (h, i, lo)], 0.5)
+            return MX[h][:, 256 * i:256 * i + 256], ["m%d_%d_%d" % (h, i, lo)]
 
-        mm(0, "nblk", x, FR)
-        for i in list(range(1, 10)) + [0] + list(range(10, 16)):
-            if i == 0:
-                mms(0, [(PS[0][:, 0:256], RED(1, 0), T.xo[:, H[0]])], ["big1", "xo0"], False, False)
-            o, nm = mx(0, i, 0, 256, arow(0, i, 0, 256) if i else T.xo[:, H[0]], blocks(0, 0, 256) if i else ["xo0"])
-            mms(0, [(PS[0][:, 0:256], RED(0, i), o)], ["big0"] + nm, False, i == 15)
-        act(s[0], PS[0][:, 0:256], AF.Sign, ["#0", "T1"], ["s1"], scale=-1.0, bias=col("T1"))
+        mt(0, "nblk", hv(x), FR)
+        mt(0, "nblk", hv(T.xo), ["xo0"], i=0)
+        for lo, hi in (MC if t == 0 else ((0, 256),)):
+            for i in list(range(1, 10)) + [0] + list(range(10, 16)):
+                o, nm = mx(0, i, lo, hi, arow(0, i, lo, hi) if i else T.xo[:, lo:hi], blocks(0, lo, hi) if i else ["xo0"])
+                mt(0, "inb2", hv(o), nm, False, i == 15 and hi == 256, i, range(lo // 128, hi // 128))
+        act(T.sT[:], PS[0][:, 0:256], AF.Sign, ["#0"], ["t1"], scale=-1.0, bias=0.5)
+        node("pe", lambda: [g.tensor.transpose(PS[5][:, 8 * u:8 * u + 8, :], T.sT[:, 128 * u:128 * u + 128], mat("I"))
+                            for u in range(2)][-1], ["I", "t1"], ["#5"], 128 * CYC)
+        cp(s[0], PS[5][:, 0:16, :], ["#5"], ["s1"], 0.5)
         act(T.so1[:], s[0].indirect(T.pu[:, 16:32]), AF.Copy, ["s1", "pu"], ["so1"], GC)
         mm(2, "nblk", x, FR)
         mm(2, "nblk", T.xo[:, H[1]], ["xo1"])
         o, nm = mx(1, 0, 0, 256, T.xo[:, H[1]], ["xo1"])
         mm(2, "inb2", o, nm)
         mm(2, "PEN", T.so1[:], ["so1"], False, True)
-        act(sw, PS[2][:, 0:256], AF.Sign, ["#2", "Tw"], ["sw"], scale=-1.0, bias=col("Tw"))
+        act(sw, PS[2][:, 0:256], AF.Sign, ["#2"], ["sw"], scale=-1.0, bias=-1023.5)
+        mm(1, "nblk", x, FR)
+        mm(1, "ZS", s[0], ["s1"])
+        mm(bY[1], "LY2", sw, ["sw"])
+        mm(bY[1], "Hs", sw, ["sw"], at=256)
         for lo, hi in MC:
-            dn = ["#d%d" % a for a, b in SCH if lo <= a < hi]
-            for nm, rhs, rd in (("nblk", x, FR), ("ZS", s[0], ["s1"]), ("Inb", sw, ["sw"])):
-                mms(1, [(PS[1][:, lo:hi], mat(nm), rhs[:, lo:hi])], [nm] + rd + dn, False, False)
             for i in range(1, 16):
                 o, nm = mx(1, i, lo, hi, arow(1, i, lo, hi), blocks(1, lo, hi))
-                mms(1, [(PS[1][:, lo:hi], RED(0, i), o)], ["big0"] + nm + dn, False, hi == 256 and i == 15)
-        act(s[1], PS[1][:, 0:256], AF.Sign, ["#1", "T2"], ["s2"], scale=-1.0, bias=col("T2"))
+                mms(1, [(PS[1][:, lo:hi], RED(0, i), o[:, lo:hi])], ["big0"] + nm, False, hi == 256 and i == 15)
+        act(s[1], PS[1][:, 0:256], AF.Sign, ["#1"], ["s2"], scale=-1.0, bias=0.5)
+
+    def hash_x(t):
+        x, FR, wm = X[:, t, 0:P], ["X", "X0" if t == 0 else "X2"], "Wm%d" % (t % (N - 1))
+        mm(6, wm, x, FR, True, True)
+        act(T.hq[:], PS[6][:, 0:256], AF.Identity, ["#6"], ["hq"], scale=1.0 / 2048, bias=191.5 + 1.0 / 4096)
+        mm(6, wm, x, FR, True)
+        mm(6, "In2", T.hq[:], ["hq"], False, True)
+        act(T.qa[:, 0:P], PS[6][:, 0:256], AF.Identity, ["#6"], ["qa"], bias=2048.0 * 192)
 
     def choose(h):
-        z, bY, bV = str(h + 1), (bY1, bY2)[h], (bV1, bV2)[h]
-        mm(bY, "LY" + z, s[h], ["s" + z], False, True)
-        ts(T.sel[:, H[h]], PS[bY][:, 0:256], col("n" + z), col("a" + z), AL.max, AL.add, ["#%d" % bY, "n" + z, "a" + z], ["sel" + z])
-        mm(bV, "H", s[h], ["s" + z], False, True)
-        tt(T.nc[:, H[h]], PS[bV][:, 0:256], T.cs[:] if h else c16[0], AL.min, ["#%d" % bV, "cs" if h else "h1"], ["nc" + z])
+        z, b = str(h + 1), bY[h]
+        mm(b, "LY" + z, s[h], ["s" + z])
+        mm(b, "H", s[h], ["s" + z], False, True, 256)
+        ts(T.sel[:, H[h]], PS[b][:, 0:256], col("n" + z), col("a" + z), AL.max, AL.add, ["@%d" % b, "n" + z, "a" + z], ["sel" + z])
+        tt(T.nc[:, H[h]], PS[b][:, 256:512], T.cs[:] if h else c16[0], AL.min, ["@%d" % b, "cs" if h else "h1"], ["nc" + z])
         ts(Aw.indirect(T.sou[:, 16 * h:16 * h + 16]), T.nc[:, H[h]], 1.0, float(CEN), AL.mult, AL.add, ["sou", "nc" + z], ["A"], ind=SC, n=256)
 
     def decide(t):
         last, n0 = t == NT - 1, M + P * t
         if not last:
-            mm(bGO, "inb", s[1], ["s2"], True, True)
-            act(T.go[:, 0:P], PS[bGO][:, 0:256], AF.Relu, ["#%d" % bGO], ["go"], scale=-1.0, bias=-15.0)
+            mm(bGO, "inb", s[1], ["s2"], False, True)
+            act(T.go[:, 0:P], PS[bGO][:, 0:256], AF.Relu, ["#%d" % bGO], ["go"], scale=-1.0, bias=-31.0)
             scan(T.cum[:], T.go[:], T.go[:], AL.add, AL.max, ["go", "go1"], ["cum"], 0.5)
         choose(1)
         if not last:
-            cp(A[:, E:E + 1], col("CE"), ["CE"], ["A"])
             for h in range(2):
-                mms(bLO, [(PS[bLO][:, 0:16], SEL(1, m), T.sel[:, 256 * h + m:256 * h + 256:16]) for m in range(16)],
-                    ["NRED", "sel%d" % (h + 1)], h == 0, h == 1)
+                mms(bLO, [(PS[bLO][:, 0:16], RED(1, m), T.sel[:, 256 * h + m:256 * h + 256:16]) for m in range(16)],
+                    ["big1", "sel%d" % (h + 1)], h == 0, h == 1)
             ts(T.ku[:, 0:16], PS[bLO][:, 0:16], LINK, None, AL.add, None, ["#%d" % bLO], ["k1u"])
-        mm(bLA, "nz16", T.sel[:, H[0]], ["sel1"], True)
+        mm(bLA, "nz", T.sel[:, H[0]], ["sel1"], True)
         if not last:
             mm(bLA, "p01", T.iox[:], ["iox"])
-        mm(bLA, "nz16", T.sel[:, H[1]], ["sel2"], False, True)
+        mm(bLA, "nz", T.sel[:, H[1]], ["sel2"], False, True)
         ab = "B0" if last else "AB%d" % t
-        act(A[:, n0:n0 + P], PS[bLA][:, 0:256], AF.Identity, ["#%d" % bLA, ab], ["A"], bias=col(ab))
+        act(A[:, n0:n0 + P], PS[bLA][:, 0:256], AF.Identity, ["#%d" % bLA, ab] + ["A"] * last, ["An" if last else "A"], bias=col(ab))
         if not last:
             act(T.lk[:], PS[bLA][:, 0:256], AF.Identity, ["#%d" % bLA], ["lk"], bias=LINK - CEN)
 
@@ -439,38 +453,39 @@ def rank_program(g, core, T, topo):
         for c in range(4):
             act(T.jk[:, c, :], T.cum[:], AF.Sign, ["cum", "thr"], [ACC[c]], bias=T.thr[:, c:c + 1], accum_out=T.acc[:, c:c + 1])
         ts(T.psu[:, 0:4], T.acc[:, 0:4], -0.5, 160.0, AL.mult, AL.add, ACC, ["psu"])
-        cp(T.xs[:, 64 * t:64 * t + 64], X[:, t, :].indirect(T.psu[:, 0:4]), FR + ["psu"], ["xs%d" % t], ind=GC)
+        cp(T.xs[:, 128 * t:128 * t + 64], X[:, t, :].indirect(T.psu[:, 0:4]), FR + ["psu"], ["xs%d" % t], ind=GC)
+        cp(T.xs[:, 128 * t + 64:128 * t + 128], T.qa[:].indirect(T.psu[:, 0:4]), ["qa", "qa1", "psu"], ["xq%d" % t], ind=GC)
         d = 1 + t % (N - 1)
-        send((rank + d) % N, (rank - d) % N, T.lx[:, 64 * t:64 * t + 64], T.xs[:, 64 * t:64 * t + 64], "req%d" % t, ["xs%d" % t], "lx%d" % t)
+        send((rank + d) % N, (rank - d) % N, T.lx[:, 128 * t:128 * t + 128], T.xs[:, 128 * t:128 * t + 128], "req%d" % t,
+             ["xs%d" % t, "xq%d" % t], "lx%d" % t)
         ts(T.pre[:], X[:, t + 1, :].indirect(T.psu[:, 0:4]), 0.5, 191.75, AL.mult, AL.add, FR + ["psu"], ["pre"], ind=GC)
 
     def serve(t):
-        lx, nm, FR = T.lx[:, 64 * t:64 * t + 64], "lx%d" % t, ["F", "F0", "F1", "F2"]
+        lx, nm, FR = T.lx[:, 128 * t:128 * t + 64], "lx%d" % t, ["F", "F0", "F1", "F2"]
         o = PS[6][:, 0:64]
-        mms(6, [(o, mat("Wm"), lx)], ["Wm", nm])
-        for hf in range(2):
-            mms(4 + hf, [(PS[4 + hf][:, i::16], mat("I"), T.lx[:, 64 * t + 32 * hf:64 * t + 32 * hf + 32]) for i in range(16)], ["I", nm], each=True)
-        scan(T.sq[:], T.dh[:], o, AL.add, AL.min, ["dh", "#6"], ["sq"])
-        cp(T.q32[:, 0:4], T.sq[:, 15::16], ["sq"], ["q32"])
-        ts(T.q33[:, 0:4], T.q32[:, 0:4], 2047, None, AL.bitwise_and, None, ["q32"], ["q33"])
-        cp(T.qu[:, 0:4], T.q33[:, 0:4], ["q33"], ["qu"])
+        for u in range(2):
+            cp(T.ld[:, u::2], lx, [nm], ["ld%d" % u], 0.5)
+        node("pe", lambda: g.tensor.transpose(PS[3][:, 0:8, :], T.ld[:], mat("I")), ["I", "ld0", "ld1"], ["#3"], 64 * CYC)
+        cp(T.lt[:], PS[3][:, 0:8, :], ["#3"], ["lt"], 0.5)
+        node("pe", lambda: [g.tensor.transpose(PS[3][:, :, i:i + 2], T.lt[:], mat("I")) for i in range(0, 16, 2)][-1], ["I", "lt"], ["#3"], 512 * CYC)
+        scan(T.sq[:], T.dh[:], T.lx[:, 128 * t + 64:128 * t + 128], AL.add, AL.min, ["dh", nm], ["sq"])
+        ts(T.qu[:, 0:4], T.sq[:, 15::16], col("QO"), None, AL.add, None, ["sq", "QO"], ["qu"])
         ts(T.cq[:], A[:, 0:M].indirect(T.qu[:, 0:4]), col("MX"), 16.0, AL.max, AL.add, ["A", "qu", "MX"], ["cq"], ind=GC)
         cp(T.sa[:, 0:512], Fw.indirect(T.cq[:, 0:32]), FR + ["cq"], ["sa0"], ind=GC)
-        if SA == "s":
-            act(T.sa[:, 512:1024], Fw.indirect(T.cq[:, 32:64]), AF.Copy, FR + ["cq"], ["sa1"], GC)
-        else:
-            cp(T.sa[:, 512:1024], Fw.indirect(T.cq[:, 32:64]), FR + ["cq"], ["sa1"], ind=GC)
-        mms(6, [(o, mat("I16"), T.kc[:])], ["I16", "kc"], True, False)
+        act(T.sa[:, 512:1024], Fw.indirect(T.cq[:, 32:64]), AF.Copy, FR + ["cq"], ["sa1"], GC)
+        mms(6, [(o, mat("I"), T.kc[:])], ["I", "kc"], True, False)
         for hf in range(2):
             mms(6, [(o, RED(3, m), T.sa[:, 64 * m:64 * m + 64]) for m in range(8 * hf, 8 * hf + 8)], ["big3", "sa%d" % hf], False, False)
         for hf in range(2):
-            tt(T.sm[:, 512 * hf:512 * hf + 512], T.sa[:, 512 * hf:512 * hf + 512], PS[4 + hf][:], AL.max, ["sa%d" % hf, "#%d" % (4 + hf)], ["sm%d" % hf])
+            tt(T.sm[:, 512 * hf:512 * hf + 512], T.sa[:, 512 * hf:512 * hf + 512], PS[3][:, 32 * hf:32 * hf + 32, :], AL.max,
+               ["sa%d" % hf, "@3"], ["sm%d" % hf], 0.5)
             mms(6, [(o, RED(2, m), T.sm[:, 64 * m:64 * m + 64]) for m in range(8 * hf, 8 * hf + 8)], ["big2", "sm%d" % hf], False, hf == 1)
         scan(T.sq[:], T.rs[:], o, AL.add, AL.min, ["rs", "#6"], ["sq"])
-        cp(T.q32[:, 0:4], T.sq[:, 15::16], ["sq"], ["q32"])
-        ts(T.q33[:, 0:4], T.q32[:, 0:4], 1023, None, AL.bitwise_and, None, ["q32"], ["q33"])
-        cp(T.qu[:, 0:4], T.q33[:, 0:4], ["q33"], ["qu"])
-        ts(T.fh[:, 64 * t:64 * t + 64], T.sa[:, 0:1024].indirect(T.qu[:, 0:4]), 0.5, None, AL.mult, None, ["sa0", "sa1", "qu"], ["fh%d" % t], ind=GC)
+        aff("v", T.q32[:, 0:4], T.sq[:, 15::16], 1.0 / 1024, 1.0 / 2048 - 0.5, ["sq"], ["q32"])
+        for c in range(4):
+            aff("v", T.qv[:, c:c + 1], T.q32[:, c:c + 1], -1024.0, T.sq[:, 16 * c + 15:16 * c + 16], ["q32", "sq"], ["qv%d" % c])
+        ts(T.fh[:, 64 * t:64 * t + 64], T.sa[:, 0:1024].indirect(T.qv[:, 0:4]), 0.5, None, AL.mult, None,
+           ["sa0", "sa1", "qv0", "qv1", "qv2", "qv3"], ["fh%d" % t], ind=GC)
         d = 1 + t % (N - 1)
         send((rank - d) % N, (rank + d) % N, T.lf[:, 64 * t:64 * t + 64], T.fh[:, 64 * t:64 * t + 64], "rep%d" % t, ["fh%d" % t], "lf%d" % t)
 
@@ -480,30 +495,44 @@ def rank_program(g, core, T, topo):
 
     ts(T.c0[:], T.pin[:, 1792:M], float(-CEN), None, AL.add, None, ["pinT"], ["c0"])
     ts(T.lk[:], T.pin[:, 1792:M], float(-CEN), None, AL.add, None, ["pinT"], ["lk"])
-    mms(bK, [(PS[bK][:, 0:16], SEL(0, m), T.c0[:, m::16]) for m in range(16)], ["SEL", "c0"])
+    iota(T.r1i[:], [[1, 256]], 0, ["r1i"], False, M)
+    dma("sy", "ld2", T.pin[1::16, 1792:M], T.r1i[1::16, :], ["r1i"], ["pinT"], 20000)
+    dma("sy", "ld3", F[:, 16:16 + M], T.fr[:], [], ["F0"], 524288)
+    dma("sy", "ld4", X[:, 0, 0:P], T.nw[:, 0:P], [], ["X0"], 65536)
+    dma("sy", "ld5", T.thw[:, 0:1], T.th[:], [], ["th"], 30000)
+    dma("sy", "ld7", X[:, 1:NT, 0:P], T.nw[:, P:NT * P], [], ["X2"], 262144)
+    dma("sy", "ld6", T.thw[:, 4:5], T.hw[:], [], ["hw"], 30000)
+    mms(bK, [(PS[bK][:, 0:16], SEL(m), T.c0[:, m::16]) for m in range(16)], ["SEL", "c0"])
     ts(T.ku[:, 0:16], PS[bK][:, 0:16], float(CEN), float(M), AL.add, AL.min, ["#%d" % bK], ["k1u"])
-    ts(T.r1n[:], T.iob[:], float(M), col("R1"), AL.add, AL.mult, ["iob", "R1"], ["r1n"])
-    ts(T.sc[:], T.pin[:, 1792:M], col("N1"), None, AL.mult, None, ["pinT", "N1"], ["sc"])
-    tt(T.pin[:, 1792:M], T.sc[:], T.r1n[:], AL.add, ["sc", "r1n"], ["pinT"], 2.0)
-    for k in range(4):
-        cp(A[:, 512 * k:512 * k + 512], T.pin[:, 512 * k:512 * k + 512], ["pin0", "pinT"], ["A_%d" % k])
+    consts_t()
+    ms(T.qa[:, P:320], 0.0, ["qa1"])
+    for d in range(N - 1):
+        send((rank - 1 - d) % N, (rank + 1 + d) % N, T.wl[:, 4 * d:4 * d + 1], T.thw[:, 4:5], "wx%d" % d, ["hw"], "wl%d" % d)
+        cp(col("W%d" % d), T.wl[:, 4 * d:4 * d + 1], ["wl%d" % d], ["W%d" % d])
+        sc("Wm%d" % d, "inb", "W%d" % d)
+    for k in range(NCV):
+        cp(A[:, 256 * k:256 * k + 256], T.pin[:, 256 * k:256 * k + 256], ["pin0", "pinT"], ["A_%d" % k])
     prefetch(0)
-    cp(A[:, E:E + 1], col("CE"), ["CE"], ["A", "A2", "A_0", "A_1", "A_2", "A_3"])
     for t in range(NT):
         early(t)
         distances(t)
-        choose(0)
-        per[0] += 1
         if t == 0:
+            cp(A[:, E:E + 1], col("CE"), ["CE"], ["A", "A2"] + ["A_%d" % k for k in range(8)])
             consts_x()
+        choose(0)
+        if t < NT - 1:
+            hash_x(t)
+            mm(bGO, "inb", sw, ["sw"], True)
+        per[0] += 1
         decide(t)
         if t < NT - 1:
             ask(t)
             prefetch(t + 1)
             serve(t)
             apply(t)
-    dma("sy", "st1", T.yp[:, 0:E // 2], A[:, 0:E // 2], ["A"], [], 851968)
-    dma("s", "st2", T.yp[:, E // 2:E], A[:, E // 2:E], ["A"], [], 851968)
+    dma("sy", "st1", T.yp[:, 0:1536], A[:, 0:1536], ["A"], [], 786432)
+    dma("s", "st2", T.yp[:, 1536:E - P], A[:, 1536:E - P], ["A"], [], 786432)
+    dma("s", "st3", T.yp[:, E - P:E], A[:, E - P:E], ["An"], [], 131072)
 
     cnt = {"v": 0, "s": 0, "pe": 0, "gc": 0}
     seen = {q: {} for q in Q}
@@ -529,7 +558,7 @@ def rank_program(g, core, T, topo):
             ins.then_inc(T.sem[nd["q"]], 1)
         elif nd["dma"]:
             ins.then_inc(T.sem[nd["ev"][0]], 16)
-    for k in range(3):
+    for k in range(4):
         need("sy", "st%d" % k, 16)
     g.wait_ge(T.sem.sent, sent[0])
     for q in cnt:

from concourse.mybir import dt, AluOpType, AxisListType, ActivationFunctionType

M, P, NT, C = 2048, 256, 5, 64
E = M + NT * P
CEN = 1792
AD = 3336
LINK = -49920.0
GAT = ("s32 s64 s64 s32 v16 v16 v16 v16", "v16 v16 s32 s64 s32 s32 s32 s32")
GAT0 = ("s64 v32 v32 s64 v32 v32", "s32 s32 s32 v32 s32 s32 s32 s32")
MC = ((0, 128), (128, 256))
NCV = 8
CYC, GC, SC = 0.00091, 1.5, 3.0
ORDER = {
    0: "0103003g9o0k0j0g020m0l0n040c0805070d2u0s0o0i9v2a279t9q130t110q9x100f0z14122n0u1d2c2i289u152t9w2s171y1f2b1s342l29202j369s2g1r221q1w2e2m2f1m232o1k2p191p9y0r0h9p0p2v2w312x2y2z30161u1i1c1t1l1g211a180x0w1e1o1j2d0v0y1x1h1b321v9z3y3q0e0a0b06463z4m4h455d5f4041335l2637354j3k3n3h424k483a383c3e3b393d4p4r5e4q51433f4l4i44475n5m4b496e626c64726u5y5q606k6i6y6g7c665s6a687e4w7g5u6m6s527m5350554s547s5o577n58736d5z6h6f5p6j615t6367696b7d7f656z6l5v3i789r74707a3j4a2h1n4e762q6q6o5w09757b242r6w4n716n776v796p6r6x5x6t5ra57h4t594c4x3o4o9m8o86848a7o8i808m827w888g8k8e8c7y3u4y3v5a4d9na67i8p8j7p8b854z4u3s87818h8n837x8f8d5b7j3w4v3x7k3t3r898la77za85g5j5i4f4g909c9a92949g8u963l8y9e988q9l8s9i8w56a0a15ha3a2957t93919b8va92k253p7l1z998z7q9h9f8r9d8t8x973m5k5ca49j7r9k7uaa7v",
    2: "0001020j0h0g0i030b040c2g08060507090d0k0a0e0f0m0l0n0p0q0z0y101u1t1v2b27261w0r2c1a2d282x290s2e0o1c0w0u2f2z1i2a2j2h2i0v0x2k2l2m1x1d0t1e2n1b2o1h1y201k2p2r2q2s1f1j1l152t1g1m2y112u1n1p12132v2w1o35213017161918363a3g3o3k403u3i423w3q3c3m313223334g1z6e4a38243b3j3h433l3x3r413p3d3v3n143e5m5o5y3y3s44605s1q5e5u5k525c5q541r625a4o644u5g665i4s4w3f253z393t456f46375z5n615f5p225d47634v5t4p6g5j5r4x5b4b484c4y4m5w5056584q1s4k49696a5v5h65554h4d6h514e4l534r5l5x4n4z594t576c4f6i6b6d674i4j6j6834",
    5: "000105030402080906070a",
}
f32, bf, f16, i32, u16 = "float32", "bfloat16", "float16", "int32", "uint16"

SB = {
    "A": ([AD + 520], f32), "F": ([E + 32], bf), "X": ([NT, 320], bf), "lk": ([256], f32), "pin": ([M + 8], i32), "thw": ([8], i32),
    "a0": ([4096], bf), "a1": ([4096], bf), "m0": ([4096], bf), "m1": ([4096], bf),
    "xo": ([512], bf), "cs": ([256], f16), "cu": ([512], u16), "c16": ([512], f16),
    "ge": ([512], bf), "e12": ([256], bf), "em": ([256], bf), "hi": ([256], bf), "s": ([768], bf), "sT": ([256], bf), "so1": ([256], bf),
    "go": ([320], bf), "sel": ([512], f16), "nc": ([512], f32), "cum": ([320], bf), "one": ([256], bf),
    "jk": ([4, 320], bf), "acc": ([8], f32), "psu": ([8], u16), "kk": ([32], i32), "ku": ([32], u16), "pm": ([32], i32),
    "pu": ([32], u16), "own": ([32], f32), "so": ([32], f32), "sou": ([32], u16),
    "xs": ([512], f16), "lx": ([512], f16), "hq": ([256], bf), "qa": ([320], f32), "wl": ([12], i32),
    "fh": ([256], bf), "lf": ([256], bf), "pre": ([64], f32), "vv": ([64], bf),
    "q32": ([8], i32), "qv": ([8], u16), "qu": ([8], u16), "cq": ([64], u16), "sa": ([1024], bf), "sm": ([1024], bf),
    "sq": ([64], f32), "pi": ([8], i32), "col": ([56], f32), "U": ([144], bf), "t0": ([144], bf), "t1": ([128], bf),
    "bb": ([144], bf), "big": ([4, 144], bf), "selm": ([144], bf), "mb": ([44, 128], bf), "r1i": ([256], i32), "lt": ([128], bf), "ld": ([128], bf),
    "iob": ([256], bf), "iox": ([256], bf), "dh": ([64], f32), "rs": ([64], f32), "t64": ([64], f32),
    "kc": ([64], f16), "neg": ([64], bf), "ioo": ([32], f32), "dum": ([32], f32), "dj": ([4], f32), "thr": ([4], f32),
    "c0": ([256], f16), "prm": ([8], u16), "prf": ([8], f32), "i64": ([64], f32),
}
SCRATCH = {k: ("sbuf", [128] + v[0], v[1]) for k, v in SB.items()}
for _b in range(8):
    SCRATCH["p%d" % _b] = ("psum", [128, 64, 16], bf) if _b in (3, 5) else ("psum", [128, 512], f32)
SEMAPHORES = (["v", "s", "pe", "gc", "sent", "wx0", "wx1", "wx2"] + ["ld%d" % k for k in range(8)]
              + [nm + str(t) for nm in ("st", "fc", "req", "rep") for t in range(4)])


def issue_order(nodes):
    seq = []
    for p in range(NT + 1):
        ids = [j for j, nd in enumerate(nodes) if nd["per"] == p]
        o = ORDER[p if p in (0, NT) else 2]
        seq += [ids[j] for j in [int(o[k:k + 2], 36) for k in range(0, len(o), 2)] if j < len(ids)]
    return seq


def rank_program(g, core, T, topo):
    rank = T.rank_of(core)
    if rank is None:
        return
    N = len(T.cores)
    AL, AF = AluOpType, ActivationFunctionType
    Q = {"v": g.vector, "s": g.scalar, "pe": g.tensor, "gc": g, "sy": g.sync}
    V, S = g.vector, g.scalar
    nodes, lastw, readers, per = [], {}, {}, [0]

    def node(q, fn, rd, wr, cost, dma=0.0, ev=None, kind=0):
        pre = {}
        for r in list(rd) + list(wr):
            for i in ([lastw[r]] if r in lastw else []) + (readers.get(r, []) if r in wr else []):
                pre[i] = pre.get(i, False) or not (r[0] == "#" and nodes[i]["q"] == q)
        j = len(nodes)
        nodes.append({"q": q, "fn": fn, "pre": pre, "cost": cost, "dma": dma, "ev": ev, "kind": kind, "per": per[0], "lab": list(wr) + list(rd)})
        for r in rd:
            readers.setdefault(r, []).append(j)
        for r in wr:
            lastw[r] = j
            readers[r] = []

    def width(x):
        n = 1
        for d in x.shape[1:]:
            n *= d
        return n

    def op(q, fn, rd, wr, n, ind=0.0):
        node(q, fn, [r.replace("@", "#") for r in rd if r[0] != "#"], list(wr) + [r for r in rd if r[0] == "#"],
             0.06 + n * ind * CYC if ind else max(n, 64) * CYC, kind=1 if ind == GC else 2 if ind else 0)

    def mms(bank, items, rd, start=True, stop=True):
        def fn():
            for k, (o, l, r) in enumerate(items):
                ins = g.tensor.matmul(o, l, r, start and k == 0, stop and k == len(items) - 1)
            return ins
        b = ["#%d" % bank]
        mid = not (start or stop)
        node("pe", fn, list(rd) + (b if mid else []), [] if mid else b, sum(max(64, width(r)) for _, _, r in items) * CYC / 2)

    def dma(q, sem, out, in_, rd, wr, nbytes):
        node(q, lambda: Q[q].dma_start(out, in_), rd, wr + ["#q" + q], 0.05, nbytes / 4e5 + 0.1, (sem, 16))

    sent = [0]

    def send(dst_rank, src_rank, out, in_, sem, rd, name):
        dst = T.cores[dst_rank]
        rid, pid = topo.addr(dst)[:2]
        sent[0] += len(topo.engines(core, dst))
        node("gc", lambda: g.remote_dma(out, in_, T.sem[sem], T.sem.sent, pid, rid, topo.mask(core, dst)), rd, [name], 0.3, 0.0,
             (sem, len(topo.engines(T.cores[src_rank], core))), 3)

    def ts(out, in0, s1, s2, o0, o1, rd, wr, per=1.0, ind=0.0, n=None):
        n = n or width(out)
        if o1 is None:
            op("v", lambda: V.tensor_scalar(out, in0, s1, None, o0), rd, wr, n * per, ind)
        else:
            op("v", lambda: V.tensor_scalar(out, in0, s1, s2, o0, o1), rd, wr, n * per, ind)

    def tt(out, a, b, o, rd, wr, per=1.0, ind=0.0):
        op("v", lambda: V.tensor_tensor(out, a, b, o), rd, wr, width(b) * per, ind)

    def cp(out, a, rd, wr, per=1.0, ind=0.0):
        op("v", lambda: V.tensor_copy(out, a), rd, wr, width(out) * per, ind)

    def ms(out, val, wr, n=64):
        op("v", lambda: V.memset(out, val), [], wr, n)

    def scan(out, d0, d1, o0, o1, rd, wr, per=1.0):
        op("v", lambda: V.tensor_tensor_scan(out, d0, d1, 0.0, o0, o1), rd, wr, width(out) * per)

    def act(out, a, f, rd, wr, ind=0.0, **kw):
        op("s", lambda: S.activation(out, a, f, **kw), rd, wr, width(out), ind)

    def iota(out, pat, cm, wr, flag=True, base=0):
        if flag:
            op("gc", lambda: g.iota(out, pat, base, cm, allow_small_or_imprecise_dtypes=True), [], wr, 150 + 2 * width(out))
        else:
            op("gc", lambda: g.iota(out, pat, base, cm), [], wr, 150 + 2 * width(out))

    def aff(q, out, a, scale, bias, rd, wr, per=1.0):
        if q == "v":
            ts(out, a, scale, bias, AL.mult, AL.add, rd, wr, per)
        else:
            act(out, a, AF.Identity, rd, wr, scale=scale, bias=bias)

    PS = [T["p%d" % b] for b in range(8)]
    A, F, X = T.A, T.F, T.X
    Aw, Fw = A[:, 0:AD + 520], F[:, 0:E + 32]
    U = T.U[:, 0:128]

    ms(T.one[:], 1.0, ["one"], 128)
    dma("sy", "ld0", T.pin[:, 1792:M], T.ptr[:, 1792:M], [], ["pinT"], 131072)
    dma("sy", "ld1", T.pin[:, 0:1792], T.ptr[:, 0:1792], [], ["pin0"], 917504)

    cols, mats = {}, {}

    def col(nm):
        cols.setdefault(nm, len(cols))
        return T.col[:, cols[nm]:cols[nm] + 1]

    def mat(nm):
        if nm not in mats:
            mats[nm] = T.mb[:, len(mats), :]
        return mats[nm]

    def cmp(nm, src, val, o, mul=None):
        if mul is None:
            ts(col(nm), col(src), val, None, o, None, [src], [nm])
        else:
            ts(col(nm), col(src), val, mul, o, AL.mult, [src], [nm])

    def lin(nm, src, mul, add, q="v"):
        aff(q, col(nm), col(src), col(mul) if mul in cols else mul, col(add) if add in cols else add, [src] + [z for z in (mul, add) if z in cols], [nm])

    def sc(nm, base, w):
        aff("s", mat(nm), mat(base), col(w) if w in cols else w, 0.0, [base] + ([w] if w in cols else []), [nm])

    def add(nm, a, b, o=AL.add):
        tt(mat(nm), mat(a), mat(b), o, [a, b], [nm])

    iota(T.pi[:, 0:1], [[0, 1]], 1, ["pi0"], False)
    iota(T.t0[:], [[1, 144]], 0, ["t0"])
    iota(T.t1[:], [[16, 8], [0, 16]], 0, ["t1"])
    iota(T.iob[:], [[1, 256]], 0, ["iob"])
    iota(T.ioo[:], [[0, 2], [16, 16]], 0, ["ioo"])
    iota(T.dj[:], [[16, 4]], 0, ["dj"])
    iota(A[:, M:E + 8], [[0, E + 8 - M]], 0, ["A2"], base=E)
    iota(T.t64[:], [[0, 4], [1, 16]], 0, ["t64"])
    iota(T.i64[:], [[1, 64]], 0, ["i64"])
    iota(T.prf[:, 0:4], [[4, 4]], 0, ["prf"])
    iota(T.neg[:], [[0, 64]], 0, ["neg"], base=-192)
    iota(F[:, 16 + M:E + 32], [[0, E + 16 - M]], 0, ["F2"], base=99)
    ms(T.go[:, P:320], 1.0, ["go1"])
    ms(F[:, 0:16], 99.0, ["F1"])
    ms(X[:, :, P:320], 0.0, ["X1"], 160)
    ms(T.pin[:, M:M + 8], E, ["pinE"])
    ts(T.pi[:, 1:2], T.pi[:, 0:1], 112, None, AL.bitwise_and, None, ["pi0"], ["pi1"])
    ts(T.pi[:, 2:3], T.pi[:, 0:1], 15, None, AL.bitwise_and, None, ["pi0"], ["pi2"])
    cp(col("G"), T.pi[:, 1:2], ["pi1"], ["G"])
    cp(col("R"), T.pi[:, 2:3], ["pi2"], ["R"])
    cmp("R0", "R", 0.0, AL.is_equal)
    cmp("R1", "R", 1.0, AL.is_equal)
    cmp("LFc", "R", 1.5, AL.is_gt, -8192.0)
    lin("CE", "R1", float(-1 - E), float(E))
    cp(T.pin[:, M:M + 1], col("CE"), ["CE"], ["pinE"])
    ts(T.U[:], T.t0[:], col("G"), None, AL.subtract, None, ["t0", "G"], ["U"], 0.5)
    ts(T.bb[:], T.U[:], 15.0, None, AL.is_equal, None, ["U"], ["bb"], 0.5)
    ts(T.selm[:], T.bb[:], col("R0"), None, AL.mult, None, ["bb", "R0"], ["SEL"], 0.5)
    for k, w in enumerate((2.0, -1.0, 2048.0, -1024.0)):
        aff("s", T.big[:, k, :], T.bb[:], w, 0.0, ["bb"], ["big%d" % k])
    ts(mat("inb"), T.t1[:], col("G"), None, AL.is_equal, None, ["t1", "G"], ["inb"], 0.5)
    ts(mat("I"), U, col("R"), None, AL.is_equal, None, ["U", "R"], ["I"], 0.5)
    ts(mat("z0"), U, 0.0, None, AL.is_equal, None, ["U"], ["z0"], 0.5)
    ts(mat("gU"), U, col("R"), None, AL.is_gt, None, ["U", "R"], ["gU"], 0.5)
    ts(mat("p01"), U, 1.0, col("R0"), AL.is_equal, AL.mult, ["U", "R0"], ["p01"], 0.5)
    ts(mat("g2"), U, 1.5, 512.0, AL.is_gt, AL.mult, ["U"], ["g2"], 0.5)
    add("gt", "gU", "inb", AL.mult)
    add("PEN", "g2", "inb", AL.mult)
    add("t3", "I", "gt", AL.subtract)
    sc("LF", "t3", "LFc")
    sc("b0", "inb", "R0")
    sc("b0p", "b0", 4096.0)
    sc("b0e", "b0", -32768.0)
    sc("b0n", "b0", -4096.0)
    lin("n256", "R0", -256.0, 0.0, "s")
    sc("b0h", "inb", "n256")
    lin("cA", "R1", -1024.0, 0.0, "s")
    sc("R1m", "z0", "cA")
    sc("Ip", "I", 1024.0)
    sc("nz", "z0", -1.0)
    for nm, base, w in (("nblk", "inb", -1.0), ("inb2", "inb", 2.0), ("H", "inb", 2048.0), ("ZS", "z0", -1024.0), ("In2", "I", -2048.0),
                        ("Inb", "I", -1024.0), ("LY", "t3", 2048.0), ("y1x", "p01", 4096.0), ("nI", "I", -1.0)):
        sc(nm, base, w)
    lin("y2c", "R0", -2048.0, -2048.0, "s")
    sc("y2x", "z0", "y2c")
    add("LY1", "LY", "y1x")
    add("LY2", "LY", "y2x")
    for t in range(NT):
        lin("mv%d" % t, "R1", float(256 * (t + 1) + 10 * 4096), "R0", "s")
        sc("MT%d" % t, "inb", "mv%d" % t)
    ts(T.iox[:], T.iob[:], col("R0"), col("R1"), AL.mult, AL.add, ["iob", "R0", "R1"], ["iox"], 0.5)

    def consts_t():
        cp(col("TH"), T.thw[:, 0:1], ["th"], ["TH"])
        lin("N0", "R0", 1.0, -1.0, "s")
        lin("TN", "TH", "N0", 0.0)
        lin("nR1", "R1", -1.0, 0.0, "s")
        lin("TA", "TH", "nR1", 0.0)
        for b, w in enumerate((1024.0, -15104.0, 32768.0)):
            lin("T%d" % b, "R0", w, "TN", "s")
            sc("TD%d" % b if b else "TDa", "I", "T%d" % b)
        sc("TZ", "z0", "TA")
        add("TD0", "TDa", "TZ")

    lin("cy", "R", -2048.0, -512.0, "s")
    lin("cy1a", "R1", 4096.0, "cy", "s")
    lin("cy1", "R0", -100000.0, "cy1a", "s")
    lin("cyb", "R", -4096.0, 1536.0, "s")
    lin("cy2", "R0", -65536.0, "cyb", "s")
    lin("hs", "R0", -32768.0, 2048.0, "s")
    sc("Hs", "inb", "hs")
    for h in "12":
        lin("n" + h, "cy" + h, -1.0, 0.0, "s")
        lin("a" + h, "cy" + h, 1.0, -1664.0, "s")
    lin("B0", "R0", LINK - E, float(E), "s")
    for t in range(NT - 1):
        lin("AB%d" % t, "R1", float(M + P * (t + 1) - E), "B0", "s")
    ts(T.ioo[:], T.ioo[:], col("R"), None, AL.add, None, ["ioo", "R"], ["ioo"])
    aff("s", T.dum[:, 0:16], T.ioo[:, 0:16], 1.0, float(AD), ["ioo"], ["dum0"])
    aff("s", T.dum[:, 16:32], T.ioo[:, 0:16], 1.0, float(AD + 256), ["ioo"], ["dum1"])
    ts(T.dj[:], T.dj[:], col("R"), None, AL.add, None, ["dj", "R"], ["dj"])
    aff("s", T.thr[:], T.dj[:], -1.0, -0.5, ["dj"], ["thr"])

    def consts_x():
        ts(T.t64[:], T.t64[:], col("R"), None, AL.is_equal, None, ["t64", "R"], ["t64"])
        aff("s", T.dh[:], T.t64[:], float(2 ** 20 + 4096), -4096.0, ["t64"], ["dh"])
        ms(T.rs[:], 0.0, ["rs"])
        ms(T.rs[:, 0::16], float(2 ** 22), ["rs"])
        lin("R64", "R", 64.0, 0.0, "s")
        ts(T.kc[:], T.i64[:], col("R64"), None, AL.add, None, ["i64", "R64"], ["kc"])
        lin("MX", "R0", float(E), 0.0, "s")
        lin("QO", "R", -4096.0, 61440.0, "s")
        ts(T.pi[:, 3:4], T.pi[:, 2:3], 3, None, AL.bitwise_and, None, ["pi2"], ["pi3"])
        ts(T.pi[:, 4:5], T.pi[:, 2:3], 2, None, AL.logical_shift_right, None, ["pi2"], ["pi4"])
        cp(col("m4"), T.pi[:, 3:4], ["pi3"], ["m4"])
        cp(col("d4"), T.pi[:, 4:5], ["pi4"], ["d4"])
        lin("pr", "m4", 16.0, "d4")
        ts(T.prm[:, 0:4], T.prf[:, 0:4], col("pr"), None, AL.add, None, ["prf", "pr"], ["prm"])

    def SEL(m):
        return T.selm[:, 15 - m:143 - m]

    def RED(k, i):
        return T.big[:, k, 15 - i:143 - i]

    def mm(bank, nm, rhs, rd, start=False, stop=False, at=0):
        mms(bank, [(PS[bank][:, at:at + 256], mat(nm), rhs)], [nm] + rd, start, stop)

    def mt(bank, nm, tile, rd, start=False, stop=False, i=None, hs=(0, 1)):
        mms(bank, [(PS[bank][:, 128 * u:128 * u + 128] if i is None else PS[bank][:, 128 * u + i:128 * u + 128:16], tile(u),
                    mat(nm) if i is None else mat(nm)[:, 0::16]) for u in hs], [nm] + rd, start, stop)

    def hv(a):
        return lambda u: a[:, 128 * u:128 * u + 128]

    AB, MX = (T.a0, T.a1), (T.m0, T.m1)
    bK, bY, bGO, bLO, bLA = 7, (4, 7), 0, 2, 1
    H = [slice(0, 256), slice(256, 512)]
    c16, ge, s = [T.c16[:, h] for h in H], [T.ge[:, h] for h in H], [T.s[:, h] for h in H]
    sw = T.s[:, 512:768]

    def blocks(h, lo, hi):
        return ["a%d_%d" % (h, k) for k in range(lo // 16, hi // 16)]

    def arow(h, i, lo, hi):
        return AB[h][:, 16 * lo + i:16 * hi:16]

    def prefetch(t):
        n0 = M + P * t
        win, wn, top = (T.pin[:, 0:M + 8], ["pin0", "pinT", "pinE"], float(M)) if t == 0 else (A[:, 0:E + 8], ["A"], float(E))
        FR = ["F", "F0", "F1", "F2"]
        ts(T.cu[:, H[0]], win.indirect(T.ku[:, 0:16]), 16.0, None, AL.add, None, wn + ["k1u"], ["cu0"], ind=GC)
        ts(c16[0], T.cu[:, H[0]], float(-CEN - 16), None, AL.add, None, ["cu0"], ["h1"], 0.5)
        mms(bK, [(PS[bK][:, 0:16], SEL(m), T.c16[:, m:256:16]) for m in range(16)], ["SEL", "h1"])
        ts(T.ku[:, 16:32], PS[bK][:, 0:16], float(CEN), top, AL.add, AL.min, ["#%d" % bK], ["k2u"])
        ts(T.cu[:, H[1]], win.indirect(T.ku[:, 16:32]), 16.0, None, AL.add, None, wn + ["k2u"], ["cu1"], ind=GC)
        for h in range(2):
            lo = 0
            for w in (GAT if t else GAT0)[h].split():
                hi = lo + int(w[1:])
                out, src = AB[h][:, 16 * lo:16 * hi], Fw.indirect(T.cu[:, 256 * h + lo:256 * h + hi])
                if w[0] == "s":
                    act(out, src, AF.Copy, FR + ["cu%d" % h], blocks(h, lo, hi), GC)
                else:
                    cp(out, src, FR + ["cu%d" % h], blocks(h, lo, hi), ind=GC)
                lo = hi
        for h in range(2):
            ts(ge[h], T.cu[:, H[h]], float(n0 + 16), None, AL.is_ge, None, ["cu%d" % h], ["ge%d" % h], 0.5)
        cp(T.kk[:], T.ku[:], ["k1u", "k2u"], ["kk"])
        ts(T.pm[:], T.kk[:], 255, None, AL.bitwise_and, None, ["kk"], ["pm"])
        cp(T.pu[:], T.pm[:], ["pm"], ["pu"])
        aff("v", T.hi[:], T.cu[:, H[0]], 1.0 / 256, -15.5 / 256 - 0.5 - 168 - t, ["cu0"], ["hi"], 0.5)
        tt(T.e12[:], T.lk[:].indirect(T.pu[:, 16:32]), c16[0], AL.is_equal, ["lk", "pu", "h1"], ["e12"], ind=GC)
        ts(T.cs[:], T.cu[:, H[1]], float(-CEN - 16), None, AL.add, None, ["cu1"], ["cs"], 0.5)
        mm(bK, "b0", c16[0], ["h1"], True)
        mm(bK, "b0h", T.hi[:], ["hi"])
        mm(bK, "b0p", ge[0], ["ge0"])
        mm(bK, "LF", ge[1], ["ge1"])
        mm(bK, "b0e", T.e12[:], ["e12"], False, True)
        tt(c16[1], PS[bK][:, 0:256], T.cs[:], AL.min, ["#%d" % bK, "cs"], ["h2"])
        ts(T.em[:], c16[1], float(E - CEN), None, AL.is_equal, None, ["h2"], ["em"], 0.5)
        tt(T.own[:], T.pm[:], T.ioo[:], AL.not_equal, ["pm", "ioo"], ["own"])
        tt(T.own[:], T.own[:], T.dum[:], AL.mult, ["own", "dum0", "dum1"], ["own"])
        tt(T.so[:], T.own[:], T.kk[:], AL.max, ["own", "kk"], ["so"])
        ts(T.sou[:], T.so[:], 1.00016, None, AL.mult, None, ["so"], ["sou"])
        mt(0, "TD0", hv(T.one), ["one"], True)
        for b in (1, 2):
            mm(b, "TD%d" % b, T.one[:], ["one"], True)
        mm(2, "PEN", T.one[:], ["one"])
        mt(0, "R1m", hv(ge[0]), ["ge0"])
        mm(2, "Inb", ge[1], ["ge1"])
        mm(2, "Ip", T.em[:], ["em"])
        for u in range(2):
            mms(0, [(PS[0][:, 128 * u + i:128 * u + 128:16], arow(0, i, 128 * u, 128 * u + 128), mat("nblk")[:, 0::16]) for i in range(1, 16)],
                ["nblk"] + blocks(0, 128 * u, 128 * u + 128), False, False)
        for lo in range(0, 256, 64):
            mms(1, [(PS[1][:, lo:lo + 64], RED(1, i), arow(1, i, lo, lo + 64)) for i in range(1, 16)], ["big1"] + blocks(1, lo, lo + 64), False, False)

    def early(t):
        for h, b in enumerate(bY):
            mm(b, "nI", c16[h], ["h%d" % (h + 1)], True)
            mm(b, "MT%d" % t, T.iox[:], ["iox"], at=256)
            mm(b, "LF", ge[h], ["ge%d" % h], at=256)
        mm(bY[1], "b0n", T.e12[:], ["e12"], at=256)

    def distances(t):
        n0 = M + P * t
        x, FR = X[:, t, 0:P], ["X", "X0" if t == 0 else "X2"]
        if t < NT - 1:
            dma("sy", "fc%d" % t, F[:, 16 + n0:16 + n0 + P], x, FR, ["F"], 65536)
        else:
            dma("sy", "st0", T.yx[:], X[:, :, 0:P], ["X", "X0", "X2"], [], 327680)
        cp(PS[3][:, 0:16, :], x, FR, ["#3", "xp"], 0.5)
        for h in range(2):
            act(T.xo[:, H[h]], x.indirect(T.pu[:, 16 * h:16 * h + 16]), AF.Copy, FR + ["pu"], ["xo%d" % h], GC)

        def mx(h, i, lo, hi, src, rd):
            o = MX[h][:, 256 * i + lo:256 * i + hi]
            tt(o, src, PS[3][:, lo // 16:hi // 16, :], AL.max, rd + ["@3", "xp"], ["m%d_%d_%d" % (h, i, lo)], 0.5)
            return MX[h][:, 256 * i:256 * i + 256], ["m%d_%d_%d" % (h, i, lo)]

        mt(0, "nblk", hv(x), FR)
        mt(0, "nblk", hv(T.xo), ["xo0"], i=0)
        for lo, hi in (MC if t == 0 else ((0, 256),)):
            for i in list(range(1, 10)) + [0] + list(range(10, 16)):
                o, nm = mx(0, i, lo, hi, arow(0, i, lo, hi) if i else T.xo[:, lo:hi], blocks(0, lo, hi) if i else ["xo0"])
                mt(0, "inb2", hv(o), nm, False, i == 15 and hi == 256, i, range(lo // 128, hi // 128))
        act(T.sT[:], PS[0][:, 0:256], AF.Sign, ["#0"], ["t1"], scale=-1.0, bias=0.5)
        node("pe", lambda: [g.tensor.transpose(PS[5][:, 8 * u:8 * u + 8, :], T.sT[:, 128 * u:128 * u + 128], mat("I"))
                            for u in range(2)][-1], ["I", "t1"], ["#5"], 128 * CYC)
        cp(s[0], PS[5][:, 0:16, :], ["#5"], ["s1"], 0.5)
        act(T.so1[:], s[0].indirect(T.pu[:, 16:32]), AF.Copy, ["s1", "pu"], ["so1"], GC)
        mm(2, "nblk", x, FR)
        mm(2, "nblk", T.xo[:, H[1]], ["xo1"])
        o, nm = mx(1, 0, 0, 256, T.xo[:, H[1]], ["xo1"])
        mm(2, "inb2", o, nm)
        mm(2, "PEN", T.so1[:], ["so1"], False, True)
        act(sw, PS[2][:, 0:256], AF.Sign, ["#2"], ["sw"], scale=-1.0, bias=-1023.5)
        mm(1, "nblk", x, FR)
        mm(1, "ZS", s[0], ["s1"])
        mm(bY[1], "LY2", sw, ["sw"])
        mm(bY[1], "Hs", sw, ["sw"], at=256)
        for lo, hi in MC:
            for i in range(1, 16):
                o, nm = mx(1, i, lo, hi, arow(1, i, lo, hi), blocks(1, lo, hi))
                mms(1, [(PS[1][:, lo:hi], RED(0, i), o[:, lo:hi])], ["big0"] + nm, False, hi == 256 and i == 15)
        act(s[1], PS[1][:, 0:256], AF.Sign, ["#1"], ["s2"], scale=-1.0, bias=0.5)

    def hash_x(t):
        x, FR, wm = X[:, t, 0:P], ["X", "X0" if t == 0 else "X2"], "Wm%d" % (t % (N - 1))
        mm(6, wm, x, FR, True, True)
        act(T.hq[:], PS[6][:, 0:256], AF.Identity, ["#6"], ["hq"], scale=1.0 / 2048, bias=191.5 + 1.0 / 4096)
        mm(6, wm, x, FR, True)
        mm(6, "In2", T.hq[:], ["hq"], False, True)
        act(T.qa[:, 0:P], PS[6][:, 0:256], AF.Identity, ["#6"], ["qa"], bias=2048.0 * 192)

    def choose(h):
        z, b = str(h + 1), bY[h]
        mm(b, "LY" + z, s[h], ["s" + z])
        mm(b, "H", s[h], ["s" + z], False, True, 256)
        ts(T.sel[:, H[h]], PS[b][:, 0:256], col("n" + z), col("a" + z), AL.max, AL.add, ["@%d" % b, "n" + z, "a" + z], ["sel" + z])
        tt(T.nc[:, H[h]], PS[b][:, 256:512], T.cs[:] if h else c16[0], AL.min, ["@%d" % b, "cs" if h else "h1"], ["nc" + z])
        ts(Aw.indirect(T.sou[:, 16 * h:16 * h + 16]), T.nc[:, H[h]], 1.0, float(CEN), AL.mult, AL.add, ["sou", "nc" + z], ["A"], ind=SC, n=256)

    def decide(t):
        last, n0 = t == NT - 1, M + P * t
        if not last:
            mm(bGO, "inb", s[1], ["s2"], False, True)
            act(T.go[:, 0:P], PS[bGO][:, 0:256], AF.Relu, ["#%d" % bGO], ["go"], scale=-1.0, bias=-31.0)
            scan(T.cum[:], T.go[:], T.go[:], AL.add, AL.max, ["go", "go1"], ["cum"], 0.5)
        choose(1)
        if not last:
            for h in range(2):
                mms(bLO, [(PS[bLO][:, 0:16], RED(1, m), T.sel[:, 256 * h + m:256 * h + 256:16]) for m in range(16)],
                    ["big1", "sel%d" % (h + 1)], h == 0, h == 1)
            ts(T.ku[:, 0:16], PS[bLO][:, 0:16], LINK, None, AL.add, None, ["#%d" % bLO], ["k1u"])
        mm(bLA, "nz", T.sel[:, H[0]], ["sel1"], True)
        if not last:
            mm(bLA, "p01", T.iox[:], ["iox"])
        mm(bLA, "nz", T.sel[:, H[1]], ["sel2"], False, True)
        ab = "B0" if last else "AB%d" % t
        act(A[:, n0:n0 + P], PS[bLA][:, 0:256], AF.Identity, ["#%d" % bLA, ab] + ["A"] * last, ["An" if last else "A"], bias=col(ab))
        if not last:
            act(T.lk[:], PS[bLA][:, 0:256], AF.Identity, ["#%d" % bLA], ["lk"], bias=LINK - CEN)

    def ask(t):
        FR, ACC = ["X", "X0", "X1", "X2"], ["acc0", "acc1", "acc2", "acc3"]
        for c in range(4):
            act(T.jk[:, c, :], T.cum[:], AF.Sign, ["cum", "thr"], [ACC[c]], bias=T.thr[:, c:c + 1], accum_out=T.acc[:, c:c + 1])
        ts(T.psu[:, 0:4], T.acc[:, 0:4], -0.5, 160.0, AL.mult, AL.add, ACC, ["psu"])
        cp(T.xs[:, 128 * t:128 * t + 64], X[:, t, :].indirect(T.psu[:, 0:4]), FR + ["psu"], ["xs%d" % t], ind=GC)
        cp(T.xs[:, 128 * t + 64:128 * t + 128], T.qa[:].indirect(T.psu[:, 0:4]), ["qa", "qa1", "psu"], ["xq%d" % t], ind=GC)
        d = 1 + t % (N - 1)
        send((rank + d) % N, (rank - d) % N, T.lx[:, 128 * t:128 * t + 128], T.xs[:, 128 * t:128 * t + 128], "req%d" % t,
             ["xs%d" % t, "xq%d" % t], "lx%d" % t)
        ts(T.pre[:], X[:, t + 1, :].indirect(T.psu[:, 0:4]), 0.5, 191.75, AL.mult, AL.add, FR + ["psu"], ["pre"], ind=GC)

    def serve(t):
        lx, nm, FR = T.lx[:, 128 * t:128 * t + 64], "lx%d" % t, ["F", "F0", "F1", "F2"]
        o = PS[6][:, 0:64]
        for u in range(2):
            cp(T.ld[:, u::2], lx, [nm], ["ld%d" % u], 0.5)
        node("pe", lambda: g.tensor.transpose(PS[3][:, 0:8, :], T.ld[:], mat("I")), ["I", "ld0", "ld1"], ["#3"], 64 * CYC)
        cp(T.lt[:], PS[3][:, 0:8, :], ["#3"], ["lt"], 0.5)
        node("pe", lambda: [g.tensor.transpose(PS[3][:, :, i:i + 2], T.lt[:], mat("I")) for i in range(0, 16, 2)][-1], ["I", "lt"], ["#3"], 512 * CYC)
        scan(T.sq[:], T.dh[:], T.lx[:, 128 * t + 64:128 * t + 128], AL.add, AL.min, ["dh", nm], ["sq"])
        ts(T.qu[:, 0:4], T.sq[:, 15::16], col("QO"), None, AL.add, None, ["sq", "QO"], ["qu"])
        ts(T.cq[:], A[:, 0:M].indirect(T.qu[:, 0:4]), col("MX"), 16.0, AL.max, AL.add, ["A", "qu", "MX"], ["cq"], ind=GC)
        cp(T.sa[:, 0:512], Fw.indirect(T.cq[:, 0:32]), FR + ["cq"], ["sa0"], ind=GC)
        act(T.sa[:, 512:1024], Fw.indirect(T.cq[:, 32:64]), AF.Copy, FR + ["cq"], ["sa1"], GC)
        mms(6, [(o, mat("I"), T.kc[:])], ["I", "kc"], True, False)
        for hf in range(2):
            mms(6, [(o, RED(3, m), T.sa[:, 64 * m:64 * m + 64]) for m in range(8 * hf, 8 * hf + 8)], ["big3", "sa%d" % hf], False, False)
        for hf in range(2):
            tt(T.sm[:, 512 * hf:512 * hf + 512], T.sa[:, 512 * hf:512 * hf + 512], PS[3][:, 32 * hf:32 * hf + 32, :], AL.max,
               ["sa%d" % hf, "@3"], ["sm%d" % hf], 0.5)
            mms(6, [(o, RED(2, m), T.sm[:, 64 * m:64 * m + 64]) for m in range(8 * hf, 8 * hf + 8)], ["big2", "sm%d" % hf], False, hf == 1)
        scan(T.sq[:], T.rs[:], o, AL.add, AL.min, ["rs", "#6"], ["sq"])
        aff("v", T.q32[:, 0:4], T.sq[:, 15::16], 1.0 / 1024, 1.0 / 2048 - 0.5, ["sq"], ["q32"])
        for c in range(4):
            aff("v", T.qv[:, c:c + 1], T.q32[:, c:c + 1], -1024.0, T.sq[:, 16 * c + 15:16 * c + 16], ["q32", "sq"], ["qv%d" % c])
        ts(T.fh[:, 64 * t:64 * t + 64], T.sa[:, 0:1024].indirect(T.qv[:, 0:4]), 0.5, None, AL.mult, None,
           ["sa0", "sa1", "qv0", "qv1", "qv2", "qv3"], ["fh%d" % t], ind=GC)
        d = 1 + t % (N - 1)
        send((rank - d) % N, (rank + d) % N, T.lf[:, 64 * t:64 * t + 64], T.fh[:, 64 * t:64 * t + 64], "rep%d" % t, ["fh%d" % t], "lf%d" % t)

    def apply(t):
        tt(T.vv[:], T.lf[:, 64 * t:64 * t + 64].indirect(T.prm[:, 0:4]), T.pre[:], AL.add, ["lf%d" % t, "prm", "pre"], ["vv"], ind=GC)
        tt(X[:, t + 1, :].indirect(T.psu[:, 0:4]), T.vv[:], T.neg[:], AL.add, ["vv", "psu", "neg"], ["X"], ind=SC)

    ts(T.c0[:], T.pin[:, 1792:M], float(-CEN), None, AL.add, None, ["pinT"], ["c0"])
    ts(T.lk[:], T.pin[:, 1792:M], float(-CEN), None, AL.add, None, ["pinT"], ["lk"])
    iota(T.r1i[:], [[1, 256]], 0, ["r1i"], False, M)
    dma("sy", "ld2", T.pin[1::16, 1792:M], T.r1i[1::16, :], ["r1i"], ["pinT"], 20000)
    dma("sy", "ld3", F[:, 16:16 + M], T.fr[:], [], ["F0"], 524288)
    dma("sy", "ld4", X[:, 0, 0:P], T.nw[:, 0:P], [], ["X0"], 65536)
    dma("sy", "ld5", T.thw[:, 0:1], T.th[:], [], ["th"], 30000)
    dma("sy", "ld7", X[:, 1:NT, 0:P], T.nw[:, P:NT * P], [], ["X2"], 262144)
    dma("sy", "ld6", T.thw[:, 4:5], T.hw[:], [], ["hw"], 30000)
    mms(bK, [(PS[bK][:, 0:16], SEL(m), T.c0[:, m::16]) for m in range(16)], ["SEL", "c0"])
    ts(T.ku[:, 0:16], PS[bK][:, 0:16], float(CEN), float(M), AL.add, AL.min, ["#%d" % bK], ["k1u"])
    consts_t()
    ms(T.qa[:, P:320], 0.0, ["qa1"])
    for d in range(N - 1):
        send((rank - 1 - d) % N, (rank + 1 + d) % N, T.wl[:, 4 * d:4 * d + 1], T.thw[:, 4:5], "wx%d" % d, ["hw"], "wl%d" % d)
        cp(col("W%d" % d), T.wl[:, 4 * d:4 * d + 1], ["wl%d" % d], ["W%d" % d])
        sc("Wm%d" % d, "inb", "W%d" % d)
    for k in range(NCV):
        cp(A[:, 256 * k:256 * k + 256], T.pin[:, 256 * k:256 * k + 256], ["pin0", "pinT"], ["A_%d" % k])
    prefetch(0)
    for t in range(NT):
        early(t)
        distances(t)
        if t == 0:
            cp(A[:, E:E + 1], col("CE"), ["CE"], ["A", "A2"] + ["A_%d" % k for k in range(8)])
            consts_x()
        choose(0)
        if t < NT - 1:
            hash_x(t)
            mm(bGO, "inb", sw, ["sw"], True)
        per[0] += 1
        decide(t)
        if t < NT - 1:
            ask(t)
            prefetch(t + 1)
            serve(t)
            apply(t)
    dma("sy", "st1", T.yp[:, 0:1536], A[:, 0:1536], ["A"], [], 786432)
    dma("s", "st2", T.yp[:, 1536:E - P], A[:, 1536:E - P], ["A"], [], 786432)
    dma("s", "st3", T.yp[:, E - P:E], A[:, E - P:E], ["An"], [], 131072)

    cnt = {"v": 0, "s": 0, "pe": 0, "gc": 0}
    seen = {q: {} for q in Q}

    def need(q, sem, val):
        if seen[q].get(sem, 0) < val:
            Q[q].wait_ge(T.sem[sem], val)
            seen[q][sem] = val

    for j in issue_order(nodes):
        nd = nodes[j]
        best = {}
        for i, sync in nd["pre"].items():
            if sync:
                sem, val = nodes[i]["ev"]
                best[sem] = max(best.get(sem, 0), val)
        for sem in best:
            need(nd["q"], sem, best[sem])
        ins = nd["fn"]()
        if nd["ev"] is None:
            cnt[nd["q"]] += 1
            nd["ev"] = (nd["q"], cnt[nd["q"]])
            ins.then_inc(T.sem[nd["q"]], 1)
        elif nd["dma"]:
            ins.then_inc(T.sem[nd["ev"][0]], 16)
    for k in range(4):
        need("sy", "st%d" % k, 16)
    g.wait_ge(T.sem.sent, sent[0])
    for q in cnt:
        need("sy", q, cnt[q])
